import numpy as np
import ml_dtypes


def mxq(x, axis, fmt="e4m3"):
    dtype, down = {"e4m3": (ml_dtypes.float8_e4m3fn, 7), "e5m2": (ml_dtypes.float8_e5m2, 14)}[fmt]
    v = np.moveaxis(np.asarray(x, np.float32).astype(ml_dtypes.bfloat16).astype(np.float64), axis, -1)
    blocks = v.reshape(v.shape[:-1] + (-1, 32))
    amax = np.abs(blocks).max(-1, keepdims=True)
    byte = np.maximum(np.where(amax > 0, np.frexp(amax)[1] - 1 + 127, 0) - down, 1)
    scale = np.exp2(byte - 127.0)
    codes = (blocks / scale).astype(np.float32).astype(dtype).astype(np.float64)
    return np.moveaxis((codes * scale).reshape(v.shape), -1, axis)


WIDE = False


def mx_kscale(k):
    if not WIDE:
        return np.ones(k)
    levels = np.array([24, -24, 12, -12, 0])
    if k % 512:
        return np.exp2(np.random.permutation(np.resize(levels, k // 32))).repeat(32)
    a = np.empty((k // 512, 16))
    for p in range(k // 512):
        a[p, :8] = np.random.permutation(np.resize(levels, 8))
        for g in range(8):
            far = levels[np.abs(levels - a[p, g]) >= 10]
            a[p, g + 8] = far[np.random.randint(len(far))]
    return np.exp2(a.ravel()).repeat(32)


def f64(x):
    return np.asarray(x).astype(np.float64)


def striped(idx):
    return np.tile(idx.reshape(-1, 16).T, (8, 1)).astype(np.uint16)


def unstriped(offs):
    return offs[:16].T.reshape(-1).astype(np.int64)


E2M1 = np.array([0.0, 0.5, 1.0, 1.5, 2.0, 3.0, 4.0, 6.0, -0.0, -0.5, -1.0, -1.5, -2.0, -3.0, -4.0, -6.0])


def pack_weight(w, fmt):
    k, n = w.shape
    w = f64(np.asarray(w, np.float32).astype(ml_dtypes.bfloat16)).reshape(k // 32, 32, n)
    amax = np.abs(w).max(1)
    if fmt == "e4m3":
        byte = np.frexp(amax)[1] - 1 + 127 - 7
    else:
        mant, ex = np.frexp(amax / 6.0)
        byte = np.where(mant > 0.5, ex, ex - 1) + 127
    byte = np.clip(np.where(amax > 0, byte, 1), 1, 254)
    scaled = (w * np.exp2(127.0 - byte)[:, None, :]).reshape(k, n).astype(np.float32)
    by_word = np.ascontiguousarray(scaled.reshape(k // 512, 128, 4, n).transpose(0, 1, 3, 2))
    if fmt == "e4m3":
        words = by_word.astype(ml_dtypes.float8_e4m3fn).view(np.uint8)
    else:
        c = by_word.astype(ml_dtypes.float4_e2m1fn).view(np.uint8) & 0xF
        words = (c[..., 0::2] | (c[..., 1::2] << 4)).reshape(k // 512, 128, 2 * n)
    return np.ascontiguousarray(words), np.ascontiguousarray(byte.astype(np.uint8).reshape(k // 512, 16, n))


def unpack_weight(words, scales, fmt):
    g, _, n = scales.shape
    words = np.ascontiguousarray(words).reshape(g, 128, n, -1)
    if fmt == "e4m3":
        vals = words.view(ml_dtypes.float8_e4m3fn).astype(np.float64)
    else:
        nib = np.empty((g, 128, n, 4), np.uint8)
        nib[..., 0::2] = words & 0xF
        nib[..., 1::2] = words >> 4
        vals = E2M1[nib]
    vals = vals * np.repeat(np.exp2(scales.astype(np.float64) - 127.0), 8, axis=1)[..., None]
    return vals.transpose(0, 1, 3, 2).reshape(g * 512, n)


def pack_table4(v):
    words, scales = pack_weight(v, "e2m1")
    g, t = words.shape[0] // 2, v.shape[1]
    return np.ascontiguousarray(words.reshape(g, 2, 128, t, 2).transpose(0, 2, 3, 1, 4).reshape(g, 128, t, 4)), scales


def unpack_table4(words, scales):
    g, _, t, _ = words.shape
    return unpack_weight(words.reshape(g, 128, t, 2, 2).transpose(0, 3, 1, 2, 4).reshape(2 * g, 128, 2 * t), scales, "e2m1")


def gelu(f):
    return 0.5 * f * (1.0 + np.tanh(np.sqrt(2.0 / np.pi) * (f + 0.044715 * f**3)))


K, R, N, T, J = 1024, 512, 512, 2048, 1024


def setup_inputs():
    n = np.random.standard_normal
    s = mx_kscale(K)[:, None]
    u = mx_kscale(R)[:, None]
    p_tab = pack_table4(n((K, T)) * s)
    p_wd = pack_weight(n((R, N)) / np.sqrt(R) / u, "e2m1")
    return {
        "tab_words": p_tab[0],
        "tab_scales": p_tab[1],
        "ws": (n((K, R)) / np.sqrt(2 * K) / s).astype(np.float32),
        "wt": (n((K, R)) / np.sqrt(2 * K) / s).astype(np.float32),
        "sm": (np.random.uniform(0.5, 2.0, R) * u[:, 0]).astype(np.float32),
        "wd_words": p_wd[0],
        "wd_scales": p_wd[1],
        "rT": (n((N, T))).astype(np.float32),
        "wgo": np.tile(np.random.uniform(0.5, 2.0, J), (128, 1)).astype(np.float32),
        "offs": striped(np.random.permutation(T)[:J]),
        "offs2": striped(np.random.permutation(T)[:J]),
    }


def reference(tab_words, tab_scales, ws, wt, sm, wd_words, wd_scales, rT, wgo, offs, offs2):
    idx = unstriped(offs)
    idx2 = unstriped(offs2)
    tab_ = unpack_table4(tab_words, tab_scales)[:, idx]
    tabb_ = unpack_table4(tab_words, tab_scales)[:, idx2]
    ws_ = mxq(f64(ws), 0, "e4m3")
    wt_ = mxq(f64(wt), 0, "e4m3")
    a = ws_.T @ tab_ + wt_.T @ tabb_
    h = f64(sm)[:, None] * gelu(a)
    h_ = mxq(h, 0, "e4m3")
    wd_ = unpack_weight(wd_words, wd_scales, "e2m1")
    y = wd_.T @ h_
    out = np.zeros((N, T))
    out[:, idx2] = f64(wgo)[0] * (y + f64(rT)[:, idx2])
    return out

@@ -1,0 +1,261 @@
+from contextlib import ExitStack
+
+import concourse.mybir as mybir
+from concourse.masks import make_identity
+
+K, R, N, T, J = 1024, 512, 512, 2048, 1024
+FLOPS = 2 * (2 * K * R * J + R * N * J)
+
+F32 = mybir.dt.float32
+BF16 = mybir.dt.bfloat16
+I32 = mybir.dt.int32
+U32 = mybir.dt.uint32
+U16 = mybir.dt.uint16
+U8 = mybir.dt.uint8
+FP8X4 = mybir.dt.float8_e4m3fn_x4
+FP4X4 = mybir.dt.float4_e2m1fn_x4
+ACT = mybir.ActivationFunctionType
+ALU = mybir.AluOpType
+
+P = 128
+H = 512
+HALVES = J // H
+DIRECT = (0,)
+
+
+def tile_list_msg_gelu_resL_kernel(
+    tc, tab_words, tab_scales, ws, wt, sm, wd_words, wd_scales, rT, wgo, offs, offs2, out
+):
+    nc = tc.nc
+    with ExitStack() as ctx:
+        keep = ctx.enter_context(tc.tile_pool(name="keep", bufs=1))
+        big = ctx.enter_context(tc.tile_pool(name="big", bufs=4))
+        two = ctx.enter_context(tc.tile_pool(name="two", bufs=2))
+        four = ctx.enter_context(tc.tile_pool(name="four", bufs=4))
+        psa = ctx.enter_context(tc.psum_pool(name="psa", bufs=4))
+        psb = ctx.enter_context(tc.psum_pool(name="psb", bufs=4))
+
+        lists = [keep.tile([P, J // 16], U16, name="list%d" % l) for l in range(2)]
+        table = keep.tile([P, T], I32, name="table")
+        tscale = keep.tile([P, T], U8, name="tscale")
+        gscale = keep.tile([P, 2 * J], U8, name="gscale", align_bytes=64)
+        sscale = keep.tile([P, 2 * J], U8, name="sscale", align_bytes=64)
+        wdw = keep.tile([P, 2 * N], U8, name="wdw", align_bytes=64)
+        wds = keep.tile([P, N], U8, name="wds", align_bytes=64)
+        smt = keep.tile([P, 4], F32, name="smt")
+        wg = keep.tile([P, J], F32, name="wg")
+        warm = keep.tile([P, 2], F32, name="warm")
+        pages = [keep.tile([P, T], F32, name="page%d" % n) for n in range(4)]
+
+        nc.vector.memset(tscale[:].bitcast(I32), 0)
+        nc.gpsimd.memset(warm[:, 0:1], 0.0)
+        nc.scalar.activation(out=warm[:, 1:2], in_=warm[:, 0:1], func=ACT.Gelu_apprx_tanh)
+
+        nc.sync.dma_start(lists[0][:], offs)
+        for q in range(4):
+            nc.sync.dma_start(out=tscale[32 * q : 32 * q + 8, :].bitcast(I32), in_=tab_scales[:, 4 * q : 4 * q + 4, :].bitcast(I32))
+        nc.sync.dma_start(out=table[:], in_=tab_words[0].rearrange("p t b -> p (t b)").bitcast(I32))
+        nc.sync.dma_start(lists[1][:], offs2)
+
+        passes = [(0, 0), (1, 0), (0, 1), (1, 1)]
+        raws = []
+        for l, d in passes:
+            raw = big.tile([P, 4 * R], F32, name="big")
+            nc.sync.dma_start(out=raw[:], in_=(ws, wt)[l][512 * d : 512 * (d + 1), :].rearrange("(p i) c -> p (i c)", i=4))
+            raws.append(raw)
+
+        for n in range(4):
+            nc.vector.memset(pages[n][:], 0.0)
+        nc.vector.memset(sscale[:].bitcast(I32), 0)
+        nc.vector.memset(wds[:].bitcast(I32), 0)
+
+        nc.sync.dma_start(out=smt[:], in_=sm.rearrange("(p t) -> p t", t=4))
+        nc.sync.dma_start(out=wdw[:].bitcast(I32), in_=wd_words[0].bitcast(I32))
+        for q in range(4):
+            nc.sync.dma_start(out=wds[32 * q : 32 * q + 4, :].bitcast(I32), in_=wd_scales[0, 4 * q : 4 * q + 4, :].bitcast(I32))
+        nc.sync.dma_start(out=wg[:], in_=wgo)
+
+        ident = None
+        if len(DIRECT) < HALVES:
+            ident = keep.tile([P, P], F32, name="ident")
+            make_identity(nc, ident[:])
+
+        def gather_words(h):
+            res = []
+            for l in range(2):
+                both = two.tile([P, H], U32, name="both" if h == 0 else "wb", align_bytes=64)
+                nc.vector.tensor_copy(out=both[:], in_=table[:].bitcast(U32).indirect(lists[l][:, 32 * h : 32 * (h + 1)]))
+                res.append(both)
+            parted = []
+            for l in range(2):
+                pt = keep.tile([P, 4 * H], U8, name="parted%d%d" % (l, h), align_bytes=64)
+                nc.vector.tensor_copy(
+                    out=pt[:].bitcast(U16).rearrange("p (d j) -> p d j", d=2),
+                    in_=res[l][:].bitcast(U16).rearrange("p (j d) -> p d j", d=2),
+                )
+                parted.append(pt)
+            return parted
+
+        for l in range(2):
+            nc.vector.tensor_copy(out=gscale[:, l * J : (l + 1) * J], in_=tscale[:].indirect(lists[l][:]))
+        nc.sync.dma_start(out=sscale[0:112, :].bitcast(I32), in_=gscale[4:116, :].bitcast(I32))
+        parted = [gather_words(0)]
+
+        wq, wsc = [], []
+        for k in range(4):
+            wb = two.tile([P, 4 * R], BF16, name="wb", align_bytes=64)
+            nc.scalar.copy(
+                out=wb[:].rearrange("p (t m i) -> p m i t", t=4, i=4),
+                in_=raws[k][:].rearrange("p (i m t) -> p m i t", i=4, t=4),
+            )
+            codes = keep.tile([P, R], U32, name="wq%d" % k, align_bytes=64)
+            scales = keep.tile([P, R], U8, name="wsc%d" % k, align_bytes=64)
+            nc.vector.quantize_mx(out=codes[:].bitcast(FP8X4), scales=scales[:], in_=wb[:])
+            wq.append(codes)
+            wsc.append(scales)
+        parted.append(gather_words(1))
+
+        def stage_one(h):
+            banks = [psa.tile([P, H], F32, name="abank") for t in range(4)]
+            order = [(k, t) for k in range(4) for t in range(4)] if h == 0 else [(k, t) for t in range(4) for k in range(4)]
+            for k, t in order:
+                l, d = passes[k]
+                nc.tensor.matmul_mx(
+                    out=banks[t][:],
+                    lhsT=wq[k][:, P * t : P * (t + 1)].bitcast(FP8X4),
+                    lhsT_scale=wsc[k][:, P * t : P * (t + 1)],
+                    rhs=parted[h][l][:, 2 * H * d : 2 * H * (d + 1)].bitcast(FP4X4),
+                    rhs_scale=(gscale, sscale)[d][:, l * J + h * H : l * J + (h + 1) * H],
+                    start=(k == 0),
+                    stop=(k == 3),
+                )
+            acts = []
+            for t in range(4):
+                g = four.tile([P, H], F32, name="g")
+                nc.scalar.activation(out=g[:], in_=banks[t][:], func=ACT.Gelu_apprx_tanh)
+                acts.append(g)
+            planes = two.tile([P, 4 * H], BF16, name="planes")
+            for t in range(4):
+                nc.scalar.activation(out=planes[:, H * t : H * (t + 1)], in_=acts[t][:], func=ACT.Copy, scale=smt[:, t : t + 1])
+            woven = keep.tile([P, 4 * H], BF16, name="woven%d" % h, align_bytes=64)
+            nc.scalar.copy(
+                out=woven[:].rearrange("p (c i t) -> p c t i", i=4, t=4),
+                in_=planes[:].rearrange("p (t c i) -> p c t i", t=4, i=4),
+            )
+            return woven
+
+        def quantise_h(woven):
+            hq = two.tile([P, H], U32, name="hq", align_bytes=64)
+            hs = two.tile([P, H], U8, name="hs", align_bytes=64)
+            nc.vector.quantize_mx(out=hq[:].bitcast(FP8X4), scales=hs[:], in_=woven[:])
+            return hq, hs
+
+        states = []
+        for n in range(4):
+            st = big.tile([P, T], F32, name="big")
+            nc.sync.dma_start(out=st[:], in_=rT[P * n : P * (n + 1), :])
+            states.append(st)
+
+        woven0 = stage_one(0)
+
+        picked = []
+        for n in range(4):
+            pk = keep.tile([P, J], F32, name="picked%d" % n)
+            nc.vector.tensor_copy(out=pk[:], in_=states[n][:].indirect(lists[1][:]))
+            picked.append(pk)
+
+        def scatter(h, n, z):
+            nc.vector.tensor_tensor(
+                pages[n][:].indirect(lists[1][:, 32 * h : 32 * (h + 1)]), z[:], wg[:, H * h : H * (h + 1)], ALU.mult
+            )
+            if h == HALVES - 1:
+                nc.sync.dma_start(out=out[P * n : P * (n + 1), :], in_=pages[n][:])
+
+        def direct_sums(h, hq, hs):
+            res = []
+            for n in range(4):
+                y = psb.tile([P, H], F32, name="bbank")
+                nc.tensor.matmul_mx(
+                    out=y[:],
+                    lhsT=wdw[:, 2 * P * n : 2 * P * (n + 1)].bitcast(FP4X4),
+                    lhsT_scale=wds[:, P * n : P * (n + 1)],
+                    rhs=hq[:].bitcast(FP8X4),
+                    rhs_scale=hs[:],
+                    start=True,
+                    stop=True,
+                )
+                res.append(y)
+            return res
+
+        def direct_add(h, n, y):
+            if (h, n) == (0, 2):
+                z = keep.tile([P, H], F32, name="woven1", align_bytes=64)
+            else:
+                z = four.tile([P, H], F32, name="z")
+            nc.vector.tensor_tensor(z[:], y[:], picked[n][:, H * h : H * (h + 1)], ALU.add)
+            return z
+
+        def turn_states(h):
+            res = []
+            for n in range(4):
+                bank = psb.tile([P, H], F32, name="bbank")
+                for b in range(4):
+                    nc.tensor.transpose(bank[:, P * b : P * (b + 1)], picked[n][:, H * h + P * b : H * h + P * (b + 1)], ident[:])
+                st = four.tile([P, H], F32, name="turned")
+                nc.scalar.copy(out=st[:], in_=bank[:])
+                res.append(st)
+            return res
+
+        def turned_sums(hq, hs):
+            res = []
+            for b in range(4):
+                bank = psa.tile([P, N], F32, name="abank")
+                nc.tensor.matmul_mx(
+                    out=bank[:],
+                    lhsT=hq[:, P * b : P * (b + 1)].bitcast(FP8X4),
+                    lhsT_scale=hs[:, P * b : P * (b + 1)],
+                    rhs=wdw[:].bitcast(FP4X4),
+                    rhs_scale=wds[:],
+                    start=True,
+                    stop=True,
+                )
+                yt = four.tile([P, N], F32, name="yt")
+                nc.scalar.copy(out=yt[:], in_=bank[:])
+                res.append(yt)
+            return res
+
+        def turned_add(n, turned, yts):
+            bank = psa.tile([P, H], F32, name="abank")
+            for b in range(4):
+                cols = slice(P * b, P * (b + 1))
+                nc.tensor.matmul(bank[:, cols], lhsT=turned[n][:, cols], rhs=ident[:], start=True, stop=False, is_transpose=True)
+                nc.tensor.matmul(bank[:, cols], lhsT=yts[b][:, P * n : P * (n + 1)], rhs=ident[:], start=False, stop=True, is_transpose=True)
+            z = four.tile([P, H], F32, name="z")
+            nc.scalar.copy(out=z[:], in_=bank[:])
+            return z
+
+        def messages(h, hq, hs):
+            if h in DIRECT:
+                ys = direct_sums(h, hq, hs)
+                return lambda n: direct_add(h, n, ys[n])
+            turned = turn_states(h)
+            yts = turned_sums(hq, hs)
+            return lambda n: turned_add(n, turned, yts)
+
+        hq0, hs0 = quantise_h(woven0)
+        make0 = messages(0, hq0, hs0)
+        z = [make0(0), make0(1)]
+        woven1 = stage_one(1)
+        scatter(0, 0, z[0])
+        scatter(0, 1, z[1])
+        hq1, hs1 = quantise_h(woven1)
+        z.append(make0(2))
+        z.append(make0(3))
+        make1 = messages(1, hq1, hs1)
+        scatter(0, 2, z[2])
+        z.append(make1(0))
+        scatter(0, 3, z[3])
+        for n in range(4):
+            if n < 3:
+                z.append(make1(n + 1))
+            scatter(1, n, z[4 + n])

@@ -18,9 +18,15 @@ ACT = mybir.ActivationFunctionType
 ALU = mybir.AluOpType
 
 P = 128
-H = 512
-HALVES = J // H
-DIRECT = (0,)
+PACK = 4
+K_PASS = P * PACK
+HALF = J // 2
+HALF_COLS = HALF // 16
+TILES = N // P
+BLOCKS = HALF // P
+LIFT = 16
+SOURCE, TARGET = 0, 1
+PASSES = ((SOURCE, 0), (TARGET, 0), (SOURCE, 1), (TARGET, 1))
 
 
 def tile_list_msg_gelu_resL_kernel(
@@ -28,234 +34,255 @@ def tile_list_msg_gelu_resL_kernel(
 ):
     nc = tc.nc
     with ExitStack() as ctx:
-        keep = ctx.enter_context(tc.tile_pool(name="keep", bufs=1))
-        big = ctx.enter_context(tc.tile_pool(name="big", bufs=4))
-        two = ctx.enter_context(tc.tile_pool(name="two", bufs=2))
-        four = ctx.enter_context(tc.tile_pool(name="four", bufs=4))
-        psa = ctx.enter_context(tc.psum_pool(name="psa", bufs=4))
-        psb = ctx.enter_context(tc.psum_pool(name="psb", bufs=4))
+        sbuf = ctx.enter_context(tc.tile_pool(name="sbuf", bufs=1))
+        ring = ctx.enter_context(tc.tile_pool(name="ring", bufs=4))
+        psum_a = ctx.enter_context(tc.psum_pool(name="psum_a", bufs=4))
+        psum_b = ctx.enter_context(tc.psum_pool(name="psum_b", bufs=4))
 
-        lists = [keep.tile([P, J // 16], U16, name="list%d" % l) for l in range(2)]
-        table = keep.tile([P, T], I32, name="table")
-        tscale = keep.tile([P, T], U8, name="tscale")
-        gscale = keep.tile([P, 2 * J], U8, name="gscale", align_bytes=64)
-        sscale = keep.tile([P, 2 * J], U8, name="sscale", align_bytes=64)
-        wdw = keep.tile([P, 2 * N], U8, name="wdw", align_bytes=64)
-        wds = keep.tile([P, N], U8, name="wds", align_bytes=64)
-        smt = keep.tile([P, 4], F32, name="smt")
-        wg = keep.tile([P, J], F32, name="wg")
-        warm = keep.tile([P, 2], F32, name="warm")
-        pages = [keep.tile([P, T], F32, name="page%d" % n) for n in range(4)]
+        def list_half(which, h):
+            return lists[which][:, HALF_COLS * h : HALF_COLS * (h + 1)]
 
-        nc.vector.memset(tscale[:].bitcast(I32), 0)
+        def zero_on_vector(words, zero):
+            cut = words.shape[1] // 2 - 1
+            nc.vector.memset(words[:, :cut], zero)
+            nc.vector.memset(words[:, cut:], zero)
+
+        lists = [sbuf.tile([P, J // 16], U16, name="list%d" % which) for which in (SOURCE, TARGET)]
+        table = sbuf.tile([P, T], I32, name="table")
+        table_scales = sbuf.tile([P, T], U8, name="table_scales", align_bytes=64)
+        nc.gpsimd.memset(table_scales[:].bitcast(I32), 0)
+        nc.sync.dma_start(lists[SOURCE][:], offs)
+        scale_rows = tab_scales.rearrange("d (q s) t -> s q d t", s=4)
+        for s in range(4):
+            nc.sync.dma_start(out=table_scales[s:P:LIFT, :].bitcast(I32), in_=scale_rows[s].bitcast(I32))
+        warm = sbuf.tile([P, 2], F32, name="warm")
         nc.gpsimd.memset(warm[:, 0:1], 0.0)
         nc.scalar.activation(out=warm[:, 1:2], in_=warm[:, 0:1], func=ACT.Gelu_apprx_tanh)
-
-        nc.sync.dma_start(lists[0][:], offs)
-        for q in range(4):
-            nc.sync.dma_start(out=tscale[32 * q : 32 * q + 8, :].bitcast(I32), in_=tab_scales[:, 4 * q : 4 * q + 4, :].bitcast(I32))
         nc.sync.dma_start(out=table[:], in_=tab_words[0].rearrange("p t b -> p (t b)").bitcast(I32))
-        nc.sync.dma_start(lists[1][:], offs2)
+        nc.sync.dma_start(lists[TARGET][:], offs2)
 
-        passes = [(0, 0), (1, 0), (0, 1), (1, 1)]
-        raws = []
-        for l, d in passes:
-            raw = big.tile([P, 4 * R], F32, name="big")
-            nc.sync.dma_start(out=raw[:], in_=(ws, wt)[l][512 * d : 512 * (d + 1), :].rearrange("(p i) c -> p (i c)", i=4))
-            raws.append(raw)
+        raw = []
+        for k, (which, d) in enumerate(PASSES):
+            rows = (ws, wt)[which][K_PASS * d : K_PASS * (d + 1), :].rearrange("(p i) c -> p i c", i=PACK)
+            width = R // 2 if k == 0 else R
+            pieces = []
+            for c0 in range(0, R, width):
+                piece = sbuf.tile([P, PACK, width], F32, name="raw%d_%d" % (k, c0))
+                nc.sync.dma_start(out=piece[:], in_=rows[:, :, c0 : c0 + width])
+                pieces.append(piece)
+            raw.append(pieces)
 
-        for n in range(4):
-            nc.vector.memset(pages[n][:], 0.0)
-        nc.vector.memset(sscale[:].bitcast(I32), 0)
-        nc.vector.memset(wds[:].bitcast(I32), 0)
+        pages = [sbuf.tile([P, T], F32, name="page%d" % n) for n in range(TILES - 1)]
+        lifted = [sbuf.tile([P, 2 * HALF], U8, name="lifted%d" % h, align_bytes=64) for h in range(2)]
+        ident = sbuf.tile([P, P], F32, name="ident")
+        for h in range(2):
+            nc.gpsimd.memset(lifted[h][:].bitcast(I32), 0)
+        make_identity(nc, ident[:])
+        zero_on_vector(pages[0][:], 0.0)
+        zero_on_vector(pages[1][:], 0.0)
+        nc.gpsimd.memset(pages[2][:], 0.0)
 
-        nc.sync.dma_start(out=smt[:], in_=sm.rearrange("(p t) -> p t", t=4))
-        nc.sync.dma_start(out=wdw[:].bitcast(I32), in_=wd_words[0].bitcast(I32))
-        for q in range(4):
-            nc.sync.dma_start(out=wds[32 * q : 32 * q + 4, :].bitcast(I32), in_=wd_scales[0, 4 * q : 4 * q + 4, :].bitcast(I32))
-        nc.sync.dma_start(out=wg[:], in_=wgo)
+        sm_cols = sbuf.tile([P, PACK], F32, name="sm_cols")
+        wd_codes = sbuf.tile([P, 2 * N], U8, name="wd_codes", align_bytes=64)
+        nc.sync.dma_start(out=sm_cols[:], in_=sm.rearrange("(p i) -> p i", i=PACK))
+        nc.sync.dma_start(out=wd_codes[:].bitcast(I32), in_=wd_words[0].bitcast(I32))
 
-        ident = None
-        if len(DIRECT) < HALVES:
-            ident = keep.tile([P, P], F32, name="ident")
-            make_identity(nc, ident[:])
+        def gather_words(which, h, name):
+            both = sbuf.tile([P, HALF], U32, name=name, align_bytes=64)
+            nc.vector.tensor_copy(out=both[:], in_=table[:].bitcast(U32).indirect(list_half(which, h)))
+            return both
 
-        def gather_words(h):
-            res = []
-            for l in range(2):
-                both = two.tile([P, H], U32, name="both" if h == 0 else "wb", align_bytes=64)
-                nc.vector.tensor_copy(out=both[:], in_=table[:].bitcast(U32).indirect(lists[l][:, 32 * h : 32 * (h + 1)]))
-                res.append(both)
-            parted = []
-            for l in range(2):
-                pt = keep.tile([P, 4 * H], U8, name="parted%d%d" % (l, h), align_bytes=64)
-                nc.vector.tensor_copy(
-                    out=pt[:].bitcast(U16).rearrange("p (d j) -> p d j", d=2),
-                    in_=res[l][:].bitcast(U16).rearrange("p (j d) -> p d j", d=2),
-                )
-                parted.append(pt)
+        def part_words(both, name):
+            parted = sbuf.tile([P, 4 * HALF], U8, name=name, align_bytes=64)
+            nc.vector.tensor_copy(
+                out=parted[:].bitcast(U16).rearrange("p (d j) -> p d j", d=2),
+                in_=both[:].bitcast(U16).rearrange("p (j d) -> p d j", d=2),
+            )
             return parted
 
-        for l in range(2):
-            nc.vector.tensor_copy(out=gscale[:, l * J : (l + 1) * J], in_=tscale[:].indirect(lists[l][:]))
-        nc.sync.dma_start(out=sscale[0:112, :].bitcast(I32), in_=gscale[4:116, :].bitcast(I32))
-        parted = [gather_words(0)]
+        def gather_scales(h, name):
+            plane = sbuf.tile([P, 2 * HALF], U8, name=name, align_bytes=64)
+            for which in (SOURCE, TARGET):
+                nc.vector.tensor_copy(
+                    out=plane[:, HALF * which : HALF * (which + 1)], in_=table_scales[:].indirect(list_half(which, h))
+                )
+            nc.sync.dma_start(out=lifted[h][: P - LIFT, :].bitcast(I32), in_=plane[LIFT:, :].bitcast(I32))
+            return plane, lifted[h]
 
-        wq, wsc = [], []
-        for k in range(4):
-            wb = two.tile([P, 4 * R], BF16, name="wb", align_bytes=64)
-            nc.scalar.copy(
-                out=wb[:].rearrange("p (t m i) -> p m i t", t=4, i=4),
-                in_=raws[k][:].rearrange("p (i m t) -> p m i t", i=4, t=4),
+        def quantise_weights(k):
+            rounded = sbuf.tile([P, PACK * R], BF16, name="rounded%d" % k, align_bytes=64)
+            by_m = rounded[:].rearrange("p (t m i) -> p m i t", t=PACK, i=PACK)
+            m0 = 0
+            for piece in raw[k]:
+                m1 = m0 + piece.shape[2] // PACK
+                nc.scalar.copy(out=by_m[:, m0:m1], in_=piece[:].rearrange("p i (m t) -> p m i t", t=PACK))
+                m0 = m1
+            codes = sbuf.tile([P, R], U32, name="w_codes%d" % k, align_bytes=64)
+            plane = sbuf.tile([P, R], U8, name="w_plane%d" % k, align_bytes=64)
+            nc.vector.quantize_mx(out=codes[:].bitcast(FP8X4), scales=plane[:], in_=rounded[:])
+            return codes, plane
+
+        def gather_states(n, cols, name):
+            picked = sbuf.tile([P, 16 * (cols.stop - cols.start)], F32, name=name, align_bytes=64)
+            nc.vector.tensor_copy(out=picked[:], in_=states[n][:].indirect(lists[TARGET][:, cols]))
+            return picked
+
+        both = [gather_words(which, 0, "both%d" % which) for which in (SOURCE, TARGET)]
+        v_words = [[part_words(both[which], "parted%d" % which) for which in (SOURCE, TARGET)], []]
+        v_planes = [gather_scales(0, "gathered_plane")]
+        weights = [quantise_weights(0)]
+        both_source = gather_words(SOURCE, 1, "rounded0")
+        weights.append(quantise_weights(1))
+        v_words[1].append(part_words(both_source, "rounded1"))
+        weights.append(quantise_weights(2))
+        v_planes.append(gather_scales(1, "rounded2"))
+        weights.append(quantise_weights(3))
+
+        both_target = gather_words(TARGET, 1, "rounded3")
+
+        states = []
+        for n, name in enumerate(("raw1_0", "raw2_0", "raw3_0", "table")):
+            state = sbuf.tile([P, T], F32, name=name)
+            nc.sync.dma_start(out=state[:], in_=rT[P * n : P * (n + 1), :])
+            states.append(state)
+        wd_plane = sbuf.tile([P, N], U8, name="table_scales", align_bytes=64)
+        nc.gpsimd.memset(wd_plane[:].bitcast(I32), 0)
+        for q in range(4):
+            nc.sync.dma_start(
+                out=wd_plane[32 * q : 32 * q + 4, :].bitcast(I32), in_=wd_scales[0, 4 * q : 4 * q + 4, :].bitcast(I32)
             )
-            codes = keep.tile([P, R], U32, name="wq%d" % k, align_bytes=64)
-            scales = keep.tile([P, R], U8, name="wsc%d" % k, align_bytes=64)
-            nc.vector.quantize_mx(out=codes[:].bitcast(FP8X4), scales=scales[:], in_=wb[:])
-            wq.append(codes)
-            wsc.append(scales)
-        parted.append(gather_words(1))
 
-        def stage_one(h):
-            banks = [psa.tile([P, H], F32, name="abank") for t in range(4)]
-            order = [(k, t) for k in range(4) for t in range(4)] if h == 0 else [(k, t) for t in range(4) for k in range(4)]
+        def hidden(h):
+            banks = [psum_a.tile([P, HALF], F32, name="bank_a") for t in range(PACK)]
+            if h == 0:
+                order = [(k, t) for k in range(len(PASSES)) for t in range(PACK)]
+            else:
+                order = [(k, t) for t in range(PACK) for k in range(len(PASSES))]
             for k, t in order:
-                l, d = passes[k]
+                which, d = PASSES[k]
+                codes, plane = weights[k]
                 nc.tensor.matmul_mx(
                     out=banks[t][:],
-                    lhsT=wq[k][:, P * t : P * (t + 1)].bitcast(FP8X4),
-                    lhsT_scale=wsc[k][:, P * t : P * (t + 1)],
-                    rhs=parted[h][l][:, 2 * H * d : 2 * H * (d + 1)].bitcast(FP4X4),
-                    rhs_scale=(gscale, sscale)[d][:, l * J + h * H : l * J + (h + 1) * H],
+                    lhsT=codes[:, P * t : P * (t + 1)].bitcast(FP8X4),
+                    lhsT_scale=plane[:, P * t : P * (t + 1)],
+                    rhs=v_words[h][which][:, 2 * HALF * d : 2 * HALF * (d + 1)].bitcast(FP4X4),
+                    rhs_scale=v_planes[h][d][:, HALF * which : HALF * (which + 1)],
                     start=(k == 0),
-                    stop=(k == 3),
+                    stop=(k == len(PASSES) - 1),
                 )
             acts = []
-            for t in range(4):
-                g = four.tile([P, H], F32, name="g")
-                nc.scalar.activation(out=g[:], in_=banks[t][:], func=ACT.Gelu_apprx_tanh)
-                acts.append(g)
-            planes = two.tile([P, 4 * H], BF16, name="planes")
-            for t in range(4):
-                nc.scalar.activation(out=planes[:, H * t : H * (t + 1)], in_=acts[t][:], func=ACT.Copy, scale=smt[:, t : t + 1])
-            woven = keep.tile([P, 4 * H], BF16, name="woven%d" % h, align_bytes=64)
+            for t in range(PACK):
+                act = ring.tile([P, HALF], F32, name="act")
+                nc.scalar.activation(out=act[:], in_=banks[t][:], func=ACT.Gelu_apprx_tanh)
+                acts.append(act)
+            scaled = sbuf.tile([P, PACK * HALF], BF16, name="scaled%d" % h)
+            for t in range(PACK):
+                nc.scalar.activation(
+                    out=scaled[:, HALF * t : HALF * (t + 1)], in_=acts[t][:], func=ACT.Copy, scale=sm_cols[:, t : t + 1]
+                )
+            woven = sbuf.tile([P, PACK * HALF], BF16, name="woven%d" % h, align_bytes=64)
             nc.scalar.copy(
-                out=woven[:].rearrange("p (c i t) -> p c t i", i=4, t=4),
-                in_=planes[:].rearrange("p (t c i) -> p c t i", t=4, i=4),
+                out=woven[:].rearrange("p (c e t) -> p c t e", e=4, t=PACK),
+                in_=scaled[:].rearrange("p (t c e) -> p c t e", t=PACK, e=4),
             )
             return woven
 
-        def quantise_h(woven):
-            hq = two.tile([P, H], U32, name="hq", align_bytes=64)
-            hs = two.tile([P, H], U8, name="hs", align_bytes=64)
-            nc.vector.quantize_mx(out=hq[:].bitcast(FP8X4), scales=hs[:], in_=woven[:])
-            return hq, hs
-
-        states = []
-        for n in range(4):
-            st = big.tile([P, T], F32, name="big")
-            nc.sync.dma_start(out=st[:], in_=rT[P * n : P * (n + 1), :])
-            states.append(st)
-
-        woven0 = stage_one(0)
+        def quantise_hidden(h, woven):
+            codes = sbuf.tile([P, HALF], U32, name="h_codes%d" % h, align_bytes=64)
+            plane = sbuf.tile([P, HALF], U8, name="h_plane%d" % h, align_bytes=64)
+            nc.vector.quantize_mx(out=codes[:].bitcast(FP8X4), scales=plane[:], in_=woven[:])
+            return codes, plane
 
         picked = []
-        for n in range(4):
-            pk = keep.tile([P, J], F32, name="picked%d" % n)
-            nc.vector.tensor_copy(out=pk[:], in_=states[n][:].indirect(lists[1][:]))
-            picked.append(pk)
+        for n in range(TILES - 1):
+            whole = gather_states(n, slice(0, 2 * HALF_COLS), "picked%d" % n)
+            picked.append((whole[:, :HALF], whole[:, HALF:]))
+            if n == 0:
+                v_words[1].append(part_words(both_target, "parted_target"))
+        woven_first = hidden(0)
+        edge_w = sbuf.tile([P, J], F32, name="gathered_plane", align_bytes=64)
+        nc.sync.dma_start(out=edge_w[:], in_=wgo)
+        last_first = gather_states(TILES - 1, slice(0, HALF_COLS), "picked_last")
+        h_first = quantise_hidden(0, woven_first)
+        last_second = gather_states(TILES - 1, slice(HALF_COLS, 2 * HALF_COLS), "woven0")
+        picked.append((last_first[:], last_second[:]))
 
-        def scatter(h, n, z):
+        last_page = sbuf.tile([P, T], F32, name="table")
+        nc.gpsimd.memset(last_page[:], 0.0)
+        pages.append(last_page)
+
+        def scatter(h, n, sums):
             nc.vector.tensor_tensor(
-                pages[n][:].indirect(lists[1][:, 32 * h : 32 * (h + 1)]), z[:], wg[:, H * h : H * (h + 1)], ALU.mult
+                pages[n][:].indirect(list_half(TARGET, h)), sums, edge_w[:, HALF * h : HALF * (h + 1)], ALU.mult
             )
-            if h == HALVES - 1:
-                nc.sync.dma_start(out=out[P * n : P * (n + 1), :], in_=pages[n][:])
 
-        def direct_sums(h, hq, hs):
-            res = []
-            for n in range(4):
-                y = psb.tile([P, H], F32, name="bbank")
-                nc.tensor.matmul_mx(
-                    out=y[:],
-                    lhsT=wdw[:, 2 * P * n : 2 * P * (n + 1)].bitcast(FP4X4),
-                    lhsT_scale=wds[:, P * n : P * (n + 1)],
-                    rhs=hq[:].bitcast(FP8X4),
-                    rhs_scale=hs[:],
-                    start=True,
-                    stop=True,
-                )
-                res.append(y)
-            return res
+        y_first = []
+        for n in range(TILES):
+            bank = psum_b.tile([P, HALF], F32, name="bank_b")
+            nc.tensor.matmul_mx(
+                out=bank[:],
+                lhsT=wd_codes[:, 2 * P * n : 2 * P * (n + 1)].bitcast(FP4X4),
+                lhsT_scale=wd_plane[:, P * n : P * (n + 1)],
+                rhs=h_first[0][:].bitcast(FP8X4),
+                rhs_scale=h_first[1][:],
+                start=True,
+                stop=True,
+            )
+            y_first.append(bank)
 
-        def direct_add(h, n, y):
-            if (h, n) == (0, 2):
-                z = keep.tile([P, H], F32, name="woven1", align_bytes=64)
-            else:
-                z = four.tile([P, H], F32, name="z")
-            nc.vector.tensor_tensor(z[:], y[:], picked[n][:, H * h : H * (h + 1)], ALU.add)
-            return z
+        def add_and_scatter_pair(n0, name):
+            pair = sbuf.tile([P, 2, HALF], F32, name=name, align_bytes=64)
+            for u in range(2):
+                nc.vector.tensor_tensor(pair[:, u, :], y_first[n0 + u][:], picked[n0 + u][0], ALU.add)
+            for u in range(2):
+                scatter(0, n0 + u, pair[:, u, :])
 
-        def turn_states(h):
-            res = []
-            for n in range(4):
-                bank = psb.tile([P, H], F32, name="bbank")
-                for b in range(4):
-                    nc.tensor.transpose(bank[:, P * b : P * (b + 1)], picked[n][:, H * h + P * b : H * h + P * (b + 1)], ident[:])
-                st = four.tile([P, H], F32, name="turned")
-                nc.scalar.copy(out=st[:], in_=bank[:])
-                res.append(st)
-            return res
+        woven_second = hidden(1)
+        add_and_scatter_pair(0, "pair")
+        h_second = quantise_hidden(1, woven_second)
 
-        def turned_sums(hq, hs):
-            res = []
-            for b in range(4):
-                bank = psa.tile([P, N], F32, name="abank")
-                nc.tensor.matmul_mx(
-                    out=bank[:],
-                    lhsT=hq[:, P * b : P * (b + 1)].bitcast(FP8X4),
-                    lhsT_scale=hs[:, P * b : P * (b + 1)],
-                    rhs=wdw[:].bitcast(FP4X4),
-                    rhs_scale=wds[:],
-                    start=True,
-                    stop=True,
-                )
-                yt = four.tile([P, N], F32, name="yt")
-                nc.scalar.copy(out=yt[:], in_=bank[:])
-                res.append(yt)
-            return res
 
-        def turned_add(n, turned, yts):
-            bank = psa.tile([P, H], F32, name="abank")
-            for b in range(4):
+        def turn_states(n):
+            bank = psum_b.tile([P, HALF], F32, name="bank_b")
+            for b in range(BLOCKS):
+                nc.tensor.transpose(bank[:, P * b : P * (b + 1)], picked[n][1][:, P * b : P * (b + 1)], ident[:])
+            turned = ring.tile([P, HALF], F32, name="turned")
+            nc.scalar.copy(out=turned[:], in_=bank[:])
+            return turned
+
+        def turned_product(b):
+            bank = psum_a.tile([P, N], F32, name="bank_a")
+            nc.tensor.matmul_mx(
+                out=bank[:],
+                lhsT=h_second[0][:, P * b : P * (b + 1)].bitcast(FP8X4),
+                lhsT_scale=h_second[1][:, P * b : P * (b + 1)],
+                rhs=wd_codes[:].bitcast(FP4X4),
+                rhs_scale=wd_plane[:],
+                start=True,
+                stop=True,
+            )
+            y_turned = ring.tile([P, N], F32, name="y_turned")
+            nc.scalar.copy(out=y_turned[:], in_=bank[:])
+            return y_turned
+
+        def turn_back(n, turned, y_turned):
+            bank = psum_a.tile([P, HALF], F32, name="bank_a")
+            for b in range(BLOCKS):
                 cols = slice(P * b, P * (b + 1))
-                nc.tensor.matmul(bank[:, cols], lhsT=turned[n][:, cols], rhs=ident[:], start=True, stop=False, is_transpose=True)
-                nc.tensor.matmul(bank[:, cols], lhsT=yts[b][:, P * n : P * (n + 1)], rhs=ident[:], start=False, stop=True, is_transpose=True)
-            z = four.tile([P, H], F32, name="z")
-            nc.scalar.copy(out=z[:], in_=bank[:])
-            return z
+                for first, source in ((True, turned[:, cols]), (False, y_turned[b][:, P * n : P * (n + 1)])):
+                    nc.tensor.matmul(
+                        bank[:, cols], lhsT=source, rhs=ident[:], start=first, stop=not first, is_transpose=True
+                    )
+            sums = ring.tile([P, HALF], F32, name="sums")
+            nc.scalar.copy(out=sums[:], in_=bank[:])
+            return sums
 
-        def messages(h, hq, hs):
-            if h in DIRECT:
-                ys = direct_sums(h, hq, hs)
-                return lambda n: direct_add(h, n, ys[n])
-            turned = turn_states(h)
-            yts = turned_sums(hq, hs)
-            return lambda n: turned_add(n, turned, yts)
-
-        hq0, hs0 = quantise_h(woven0)
-        make0 = messages(0, hq0, hs0)
-        z = [make0(0), make0(1)]
-        woven1 = stage_one(1)
-        scatter(0, 0, z[0])
-        scatter(0, 1, z[1])
-        hq1, hs1 = quantise_h(woven1)
-        z.append(make0(2))
-        z.append(make0(3))
-        make1 = messages(1, hq1, hs1)
-        scatter(0, 2, z[2])
-        z.append(make1(0))
-        scatter(0, 3, z[3])
-        for n in range(4):
-            if n < 3:
-                z.append(make1(n + 1))
-            scatter(1, n, z[4 + n])
+        turned = [turn_states(n) for n in range(2)]
+        y_turned = [turned_product(b) for b in range(BLOCKS)]
+        sums = [turn_back(0, turned[0], y_turned)]
+        add_and_scatter_pair(2, "woven1")
+        turned.extend(turn_states(n) for n in range(2, TILES))
+        sums.extend(turn_back(n, turned[n], y_turned) for n in range(1, TILES))
+        for n in range(TILES):
+            scatter(1, n, sums[n][:])
+            nc.sync.dma_start(out=out[P * n : P * (n + 1), :], in_=pages[n][:])

@@ -25,6 +25,8 @@ HALF_COLS = HALF // 16
 TILES = N // P
 BLOCKS = HALF // P
 LIFT = 16
+DIRECT = 2
+STATE_AT = 4 * (T - HALF)
 SOURCE, TARGET = 0, 1
 PASSES = ((SOURCE, 0), (TARGET, 0), (SOURCE, 1), (TARGET, 1))
 
@@ -35,9 +37,12 @@ def tile_list_msg_gelu_resL_kernel(
     nc = tc.nc
     with ExitStack() as ctx:
         sbuf = ctx.enter_context(tc.tile_pool(name="sbuf", bufs=1))
+        laid = ctx.enter_context(tc.tile_pool(name="laid", bufs=1))
         ring = ctx.enter_context(tc.tile_pool(name="ring", bufs=4))
-        psum_a = ctx.enter_context(tc.psum_pool(name="psum_a", bufs=4))
-        psum_b = ctx.enter_context(tc.psum_pool(name="psum_b", bufs=4))
+        psum = ctx.enter_context(tc.psum_pool(name="psum", bufs=1))
+
+        def bank_tile(index):
+            return psum.tile([P, HALF], F32, name="bank%d" % index)
 
         def list_half(which, h):
             return lists[which][:, HALF_COLS * h : HALF_COLS * (h + 1)]
@@ -48,66 +53,62 @@ def tile_list_msg_gelu_resL_kernel(
             nc.vector.memset(words[:, cut:], zero)
 
         lists = [sbuf.tile([P, J // 16], U16, name="list%d" % which) for which in (SOURCE, TARGET)]
-        table = sbuf.tile([P, T], I32, name="table")
+        table = laid.tile([P, T], I32, name="table", offset=STATE_AT)
         table_scales = sbuf.tile([P, T], U8, name="table_scales", align_bytes=64)
         nc.gpsimd.memset(table_scales[:].bitcast(I32), 0)
         nc.sync.dma_start(lists[SOURCE][:], offs)
         scale_rows = tab_scales.rearrange("d (q s) t -> s q d t", s=4)
         for s in range(4):
             nc.sync.dma_start(out=table_scales[s:P:LIFT, :].bitcast(I32), in_=scale_rows[s].bitcast(I32))
-        warm = sbuf.tile([P, 2], F32, name="warm")
-        nc.gpsimd.memset(warm[:, 0:1], 0.0)
-        nc.scalar.activation(out=warm[:, 1:2], in_=warm[:, 0:1], func=ACT.Gelu_apprx_tanh)
-        nc.sync.dma_start(out=table[:], in_=tab_words[0].rearrange("p t b -> p (t b)").bitcast(I32))
+
         nc.sync.dma_start(lists[TARGET][:], offs2)
 
-        raw = []
-        for k, (which, d) in enumerate(PASSES):
+        def load_weights(k, width, names):
+            which, d = PASSES[k]
             rows = (ws, wt)[which][K_PASS * d : K_PASS * (d + 1), :].rearrange("(p i) c -> p i c", i=PACK)
-            width = R // 2 if k == 0 else R
             pieces = []
-            for c0 in range(0, R, width):
-                piece = sbuf.tile([P, PACK, width], F32, name="raw%d_%d" % (k, c0))
+            for c0, name in zip(range(0, R, width), names):
+                piece = sbuf.tile([P, PACK, width], F32, name=name, align_bytes=64)
                 nc.sync.dma_start(out=piece[:], in_=rows[:, :, c0 : c0 + width])
                 pieces.append(piece)
-            raw.append(pieces)
+            return pieces
 
-        pages = [sbuf.tile([P, T], F32, name="page%d" % n) for n in range(TILES - 1)]
-        lifted = [sbuf.tile([P, 2 * HALF], U8, name="lifted%d" % h, align_bytes=64) for h in range(2)]
+        raw = [load_weights(0, R // 2, ("raw0a", "raw0b"))]
+        nc.sync.dma_start(out=table[:], in_=tab_words[0].rearrange("p t b -> p (t b)").bitcast(I32))
+        raw.append(load_weights(1, R // 2, ("raw1a", "raw1b")))
+        raw.append(load_weights(2, R, ("raw2",)))
+
+        pages = [sbuf.tile([P, T], F32, name="page0")]
+        lifted = sbuf.tile([P, 2 * J], U8, name="lifted", align_bytes=64)
         ident = sbuf.tile([P, P], F32, name="ident")
-        for h in range(2):
-            nc.gpsimd.memset(lifted[h][:].bitcast(I32), 0)
+        wd_plane = sbuf.tile([P, N], U8, name="wd_plane", align_bytes=64)
+        nc.gpsimd.memset(wd_plane[:].bitcast(I32), 0)
         make_identity(nc, ident[:])
-        zero_on_vector(pages[0][:], 0.0)
-        zero_on_vector(pages[1][:], 0.0)
-        nc.gpsimd.memset(pages[2][:], 0.0)
-
         sm_cols = sbuf.tile([P, PACK], F32, name="sm_cols")
-        wd_codes = sbuf.tile([P, 2 * N], U8, name="wd_codes", align_bytes=64)
-        nc.sync.dma_start(out=sm_cols[:], in_=sm.rearrange("(p i) -> p i", i=PACK))
-        nc.sync.dma_start(out=wd_codes[:].bitcast(I32), in_=wd_words[0].bitcast(I32))
+        nc.gpsimd.dma_start(out=sm_cols[:], in_=sm.rearrange("(p i) -> p i", i=PACK))
+        for q in range(4):
+            nc.gpsimd.dma_start(
+                out=wd_plane[32 * q : 32 * q + 4, :].bitcast(I32), in_=wd_scales[0, 4 * q : 4 * q + 4, :].bitcast(I32)
+            )
+        zero_on_vector(lifted[:].bitcast(I32), 0)
+        nc.vector.memset(pages[0][:], 0.0)
 
-        def gather_words(which, h, name):
-            both = sbuf.tile([P, HALF], U32, name=name, align_bytes=64)
-            nc.vector.tensor_copy(out=both[:], in_=table[:].bitcast(U32).indirect(list_half(which, h)))
+        def gather_words(which, cols, name):
+            both = sbuf.tile([P, 16 * (cols.stop - cols.start)], U32, name=name, align_bytes=64)
+            nc.vector.tensor_copy(out=both[:], in_=table[:].bitcast(U32).indirect(lists[which][:, cols]))
             return both
 
         def part_words(both, name):
-            parted = sbuf.tile([P, 4 * HALF], U8, name=name, align_bytes=64)
-            nc.vector.tensor_copy(
-                out=parted[:].bitcast(U16).rearrange("p (d j) -> p d j", d=2),
-                in_=both[:].bitcast(U16).rearrange("p (j d) -> p d j", d=2),
-            )
-            return parted
-
-        def gather_scales(h, name):
-            plane = sbuf.tile([P, 2 * HALF], U8, name=name, align_bytes=64)
+            parted = sbuf.tile([P, 8 * HALF], U8, name=name, align_bytes=64)
+            result = []
             for which in (SOURCE, TARGET):
+                own = parted[:, 4 * HALF * which : 4 * HALF * (which + 1)]
                 nc.vector.tensor_copy(
-                    out=plane[:, HALF * which : HALF * (which + 1)], in_=table_scales[:].indirect(list_half(which, h))
+                    out=own.bitcast(U16).rearrange("p (d j) -> p d j", d=2),
+                    in_=both[which][:].bitcast(U16).rearrange("p (j d) -> p d j", d=2),
                 )
-            nc.sync.dma_start(out=lifted[h][: P - LIFT, :].bitcast(I32), in_=plane[LIFT:, :].bitcast(I32))
-            return plane, lifted[h]
+                result.append(own)
+            return result
 
         def quantise_weights(k):
             rounded = sbuf.tile([P, PACK * R], BF16, name="rounded%d" % k, align_bytes=64)
@@ -127,33 +128,37 @@ def tile_list_msg_gelu_resL_kernel(
             nc.vector.tensor_copy(out=picked[:], in_=states[n][:].indirect(lists[TARGET][:, cols]))
             return picked
 
-        both = [gather_words(which, 0, "both%d" % which) for which in (SOURCE, TARGET)]
-        v_words = [[part_words(both[which], "parted%d" % which) for which in (SOURCE, TARGET)], []]
-        v_planes = [gather_scales(0, "gathered_plane")]
-        weights = [quantise_weights(0)]
-        both_source = gather_words(SOURCE, 1, "rounded0")
-        weights.append(quantise_weights(1))
-        v_words[1].append(part_words(both_source, "rounded1"))
-        weights.append(quantise_weights(2))
-        v_planes.append(gather_scales(1, "rounded2"))
-        weights.append(quantise_weights(3))
-
-        both_target = gather_words(TARGET, 1, "rounded3")
-
-        states = []
-        for n, name in enumerate(("raw1_0", "raw2_0", "raw3_0", "table")):
-            state = sbuf.tile([P, T], F32, name=name)
-            nc.sync.dma_start(out=state[:], in_=rT[P * n : P * (n + 1), :])
-            states.append(state)
-        wd_plane = sbuf.tile([P, N], U8, name="table_scales", align_bytes=64)
-        nc.gpsimd.memset(wd_plane[:].bitcast(I32), 0)
-        for q in range(4):
-            nc.sync.dma_start(
-                out=wd_plane[32 * q : 32 * q + 4, :].bitcast(I32), in_=wd_scales[0, 4 * q : 4 * q + 4, :].bitcast(I32)
+        gathered = sbuf.tile([P, 2 * J], U8, name="gathered_plane", align_bytes=64)
+        for which in (SOURCE, TARGET):
+            nc.vector.tensor_copy(
+                out=gathered[:, J * which : J * (which + 1)], in_=table_scales[:].indirect(lists[which][:])
             )
+        nc.sync.dma_start(out=lifted[: P - LIFT, :].bitcast(I32), in_=gathered[LIFT:, :].bitcast(I32))
+        v_planes = (gathered, lifted)
+        raw.append(load_weights(3, R // 2, ("table_scales", "raw3b")))
+
+        first_cols, second_cols = slice(0, HALF_COLS), slice(HALF_COLS, 2 * HALF_COLS)
+        weights = [quantise_weights(0)]
+        both = [gather_words(which, first_cols, "both%d" % which) for which in (SOURCE, TARGET)]
+        v_words = [part_words(both, "parted")]
+        weights.append(quantise_weights(1))
+        both = [gather_words(SOURCE, second_cols, "rounded1")]
+        weights.append(quantise_weights(2))
+        both.append(gather_words(TARGET, second_cols, "rounded2"))
+        weights.append(quantise_weights(3))
+        v_words.append(part_words(both, "rounded3"))
+
+        wd_codes = sbuf.tile([P, 2 * N], U8, name="wd_codes", align_bytes=64)
+        nc.sync.dma_start(out=wd_codes[:].bitcast(I32), in_=wd_words[0].bitcast(I32))
+        states = []
+        for n, name in enumerate(("raw1a", "raw1b", "raw2")):
+            states.append(sbuf.tile([P, T], F32, name=name, align_bytes=64))
+        states.append(laid.tile([P, T], F32, name="last_states", offset=STATE_AT))
+        for n, state in enumerate(states):
+            nc.sync.dma_start(out=state[:], in_=rT[P * n : P * (n + 1), :])
 
         def hidden(h):
-            banks = [psum_a.tile([P, HALF], F32, name="bank_a") for t in range(PACK)]
+            banks = [bank_tile(t) for t in range(PACK)]
             if h == 0:
                 order = [(k, t) for k in range(len(PASSES)) for t in range(PACK)]
             else:
@@ -166,7 +171,7 @@ def tile_list_msg_gelu_resL_kernel(
                     lhsT=codes[:, P * t : P * (t + 1)].bitcast(FP8X4),
                     lhsT_scale=plane[:, P * t : P * (t + 1)],
                     rhs=v_words[h][which][:, 2 * HALF * d : 2 * HALF * (d + 1)].bitcast(FP4X4),
-                    rhs_scale=v_planes[h][d][:, HALF * which : HALF * (which + 1)],
+                    rhs_scale=v_planes[d][:, J * which + HALF * h : J * which + HALF * (h + 1)],
                     start=(k == 0),
                     stop=(k == len(PASSES) - 1),
                 )
@@ -187,38 +192,44 @@ def tile_list_msg_gelu_resL_kernel(
             )
             return woven
 
-        def quantise_hidden(h, woven):
-            codes = sbuf.tile([P, HALF], U32, name="h_codes%d" % h, align_bytes=64)
-            plane = sbuf.tile([P, HALF], U8, name="h_plane%d" % h, align_bytes=64)
+        def quantise_hidden(codes_name, plane_name, woven):
+            codes = sbuf.tile([P, HALF], U32, name=codes_name, align_bytes=64)
+            plane = sbuf.tile([P, HALF], U8, name=plane_name, align_bytes=64)
             nc.vector.quantize_mx(out=codes[:].bitcast(FP8X4), scales=plane[:], in_=woven[:])
             return codes, plane
 
+        whole_cols = slice(0, 2 * HALF_COLS)
         picked = []
         for n in range(TILES - 1):
-            whole = gather_states(n, slice(0, 2 * HALF_COLS), "picked%d" % n)
+            whole = gather_states(n, whole_cols, "picked%d" % n)
             picked.append((whole[:, :HALF], whole[:, HALF:]))
-            if n == 0:
-                v_words[1].append(part_words(both_target, "parted_target"))
         woven_first = hidden(0)
-        edge_w = sbuf.tile([P, J], F32, name="gathered_plane", align_bytes=64)
-        nc.sync.dma_start(out=edge_w[:], in_=wgo)
-        last_first = gather_states(TILES - 1, slice(0, HALF_COLS), "picked_last")
-        h_first = quantise_hidden(0, woven_first)
-        last_second = gather_states(TILES - 1, slice(HALF_COLS, 2 * HALF_COLS), "woven0")
-        picked.append((last_first[:], last_second[:]))
+        edge_w = []
+        for h, name in enumerate(("parted", "rounded3")):
+            piece = sbuf.tile([P, HALF], F32, name=name, align_bytes=64)
+            nc.sync.dma_start(out=piece[:], in_=wgo[:, HALF * h : HALF * (h + 1)])
+            edge_w.append(piece)
+        h_first = quantise_hidden("raw2", "h_plane0", woven_first)
+        last = gather_states(TILES - 1, whole_cols, "woven0")
+        picked.append((last[:, :HALF], last[:, HALF:]))
 
-        last_page = sbuf.tile([P, T], F32, name="table")
-        nc.gpsimd.memset(last_page[:], 0.0)
-        pages.append(last_page)
+        def late_page(name):
+            page = sbuf.tile([P, T], F32, name=name, align_bytes=64)
+            nc.gpsimd.memset(page[:], 0.0)
+            pages.append(page)
+
+        page = laid.tile([P, T], F32, name="page1", offset=STATE_AT + 4 * HALF)
+        nc.gpsimd.memset(page[:], 0.0)
+        pages.append(page)
 
         def scatter(h, n, sums):
             nc.vector.tensor_tensor(
-                pages[n][:].indirect(list_half(TARGET, h)), sums, edge_w[:, HALF * h : HALF * (h + 1)], ALU.mult
+                pages[n][:].indirect(list_half(TARGET, h)), sums, edge_w[h][:], ALU.mult
             )
 
         y_first = []
-        for n in range(TILES):
-            bank = psum_b.tile([P, HALF], F32, name="bank_b")
+        for n in range(DIRECT):
+            bank = bank_tile(4 + n)
             nc.tensor.matmul_mx(
                 out=bank[:],
                 lhsT=wd_codes[:, 2 * P * n : 2 * P * (n + 1)].bitcast(FP4X4),
@@ -230,46 +241,51 @@ def tile_list_msg_gelu_resL_kernel(
             )
             y_first.append(bank)
 
-        def add_and_scatter_pair(n0, name):
-            pair = sbuf.tile([P, 2, HALF], F32, name=name, align_bytes=64)
-            for u in range(2):
-                nc.vector.tensor_tensor(pair[:, u, :], y_first[n0 + u][:], picked[n0 + u][0], ALU.add)
-            for u in range(2):
-                scatter(0, n0 + u, pair[:, u, :])
+        direct = [
+            laid.tile([P, HALF], F32, name="direct0", offset=STATE_AT),
+            sbuf.tile([P, HALF], F32, name="direct1", align_bytes=64),
+        ]
+        for n in range(DIRECT):
+            nc.vector.tensor_tensor(direct[n][:], y_first[n][:], picked[n][0], ALU.add)
+        for n in range(DIRECT):
+            scatter(0, n, direct[n][:])
+        page = laid.tile([P, T], F32, name="page2", offset=0)
+        nc.gpsimd.memset(page[:], 0.0)
+        pages.append(page)
 
         woven_second = hidden(1)
-        add_and_scatter_pair(0, "pair")
-        h_second = quantise_hidden(1, woven_second)
+        h_second = quantise_hidden("direct1", "h_plane1", woven_second)
+        late_page("woven1")
 
-
-        def turn_states(n):
-            bank = psum_b.tile([P, HALF], F32, name="bank_b")
+        def turned_product(hq, n):
+            bank = bank_tile(n % 2)
             for b in range(BLOCKS):
-                nc.tensor.transpose(bank[:, P * b : P * (b + 1)], picked[n][1][:, P * b : P * (b + 1)], ident[:])
+                nc.tensor.matmul_mx(
+                    out=bank[:, P * b : P * (b + 1)],
+                    lhsT=hq[0][:, P * b : P * (b + 1)].bitcast(FP8X4),
+                    lhsT_scale=hq[1][:, P * b : P * (b + 1)],
+                    rhs=wd_codes[:, 2 * P * n : 2 * P * (n + 1)].bitcast(FP4X4),
+                    rhs_scale=wd_plane[:, P * n : P * (n + 1)],
+                    start=True,
+                    stop=True,
+                )
+            y_turned = ring.tile([P, HALF], F32, name="y_turned")
+            nc.scalar.copy(out=y_turned[:], in_=bank[:])
+            return y_turned
+
+        def turn_states(h, n):
+            bank = bank_tile(4 - 2 * h + n % 2)
+            for b in range(BLOCKS):
+                nc.tensor.transpose(bank[:, P * b : P * (b + 1)], picked[n][h][:, P * b : P * (b + 1)], ident[:])
             turned = ring.tile([P, HALF], F32, name="turned")
             nc.scalar.copy(out=turned[:], in_=bank[:])
             return turned
 
-        def turned_product(b):
-            bank = psum_a.tile([P, N], F32, name="bank_a")
-            nc.tensor.matmul_mx(
-                out=bank[:],
-                lhsT=h_second[0][:, P * b : P * (b + 1)].bitcast(FP8X4),
-                lhsT_scale=h_second[1][:, P * b : P * (b + 1)],
-                rhs=wd_codes[:].bitcast(FP4X4),
-                rhs_scale=wd_plane[:],
-                start=True,
-                stop=True,
-            )
-            y_turned = ring.tile([P, N], F32, name="y_turned")
-            nc.scalar.copy(out=y_turned[:], in_=bank[:])
-            return y_turned
-
-        def turn_back(n, turned, y_turned):
-            bank = psum_a.tile([P, HALF], F32, name="bank_a")
+        def turn_back(h, n, turned, y_turned):
+            bank = bank_tile(4 * h + n)
             for b in range(BLOCKS):
                 cols = slice(P * b, P * (b + 1))
-                for first, source in ((True, turned[:, cols]), (False, y_turned[b][:, P * n : P * (n + 1)])):
+                for first, source in ((True, turned[:, cols]), (False, y_turned[:, cols])):
                     nc.tensor.matmul(
                         bank[:, cols], lhsT=source, rhs=ident[:], start=first, stop=not first, is_transpose=True
                     )
@@ -277,12 +293,12 @@ def tile_list_msg_gelu_resL_kernel(
             nc.scalar.copy(out=sums[:], in_=bank[:])
             return sums
 
-        turned = [turn_states(n) for n in range(2)]
-        y_turned = [turned_product(b) for b in range(BLOCKS)]
-        sums = [turn_back(0, turned[0], y_turned)]
-        add_and_scatter_pair(2, "woven1")
-        turned.extend(turn_states(n) for n in range(2, TILES))
-        sums.extend(turn_back(n, turned[n], y_turned) for n in range(1, TILES))
+        for n in range(DIRECT, TILES):
+            sums = turn_back(0, n, turn_states(0, n), turned_product(h_first, n))
+            scatter(0, n, sums[:])
+
+        turned = [turn_states(1, n) for n in range(TILES)]
         for n in range(TILES):
-            scatter(1, n, sums[n][:])
+            sums = turn_back(1, n, turned[n], turned_product(h_second, n))
+            scatter(1, n, sums[:])
             nc.sync.dma_start(out=out[P * n : P * (n + 1), :], in_=pages[n][:])

@@ -26,7 +26,6 @@ TILES = N // P
 BLOCKS = HALF // P
 LIFT = 16
 DIRECT = 2
-STATE_AT = 4 * (T - HALF)
 SOURCE, TARGET = 0, 1
 PASSES = ((SOURCE, 0), (TARGET, 0), (SOURCE, 1), (TARGET, 1))
 
@@ -37,7 +36,6 @@ def tile_list_msg_gelu_resL_kernel(
     nc = tc.nc
     with ExitStack() as ctx:
         sbuf = ctx.enter_context(tc.tile_pool(name="sbuf", bufs=1))
-        laid = ctx.enter_context(tc.tile_pool(name="laid", bufs=1))
         ring = ctx.enter_context(tc.tile_pool(name="ring", bufs=4))
         psum = ctx.enter_context(tc.psum_pool(name="psum", bufs=1))
 
@@ -53,7 +51,7 @@ def tile_list_msg_gelu_resL_kernel(
             nc.vector.memset(words[:, cut:], zero)
 
         lists = [sbuf.tile([P, J // 16], U16, name="list%d" % which) for which in (SOURCE, TARGET)]
-        table = laid.tile([P, T], I32, name="table", offset=STATE_AT)
+        table = sbuf.tile([P, T], I32, name="table", align_bytes=64)
         table_scales = sbuf.tile([P, T], U8, name="table_scales", align_bytes=64)
         nc.gpsimd.memset(table_scales[:].bitcast(I32), 0)
         nc.sync.dma_start(lists[SOURCE][:], offs)
@@ -75,7 +73,7 @@ def tile_list_msg_gelu_resL_kernel(
 
         raw = [load_weights(0, R // 2, ("raw0a", "raw0b"))]
         nc.sync.dma_start(out=table[:], in_=tab_words[0].rearrange("p t b -> p (t b)").bitcast(I32))
-        raw.append(load_weights(1, R // 2, ("raw1a", "raw1b")))
+        raw.append(load_weights(1, R, ("raw1",)))
         raw.append(load_weights(2, R, ("raw2",)))
 
         pages = [sbuf.tile([P, T], F32, name="page0")]
@@ -135,27 +133,26 @@ def tile_list_msg_gelu_resL_kernel(
             )
         nc.sync.dma_start(out=lifted[: P - LIFT, :].bitcast(I32), in_=gathered[LIFT:, :].bitcast(I32))
         v_planes = (gathered, lifted)
-        raw.append(load_weights(3, R // 2, ("table_scales", "raw3b")))
+        raw.append(load_weights(3, R, ("table_scales",)))
 
         first_cols, second_cols = slice(0, HALF_COLS), slice(HALF_COLS, 2 * HALF_COLS)
         weights = [quantise_weights(0)]
         both = [gather_words(which, first_cols, "both%d" % which) for which in (SOURCE, TARGET)]
         v_words = [part_words(both, "parted")]
         weights.append(quantise_weights(1))
-        both = [gather_words(SOURCE, second_cols, "rounded1")]
+        both = [gather_words(SOURCE, second_cols, "raw1")]
         weights.append(quantise_weights(2))
-        both.append(gather_words(TARGET, second_cols, "rounded2"))
+        both.append(gather_words(TARGET, second_cols, "raw2"))
         weights.append(quantise_weights(3))
-        v_words.append(part_words(both, "rounded3"))
+        v_words.append(part_words(both, "table_scales"))
 
         wd_codes = sbuf.tile([P, 2 * N], U8, name="wd_codes", align_bytes=64)
         nc.sync.dma_start(out=wd_codes[:].bitcast(I32), in_=wd_words[0].bitcast(I32))
         states = []
-        for n, name in enumerate(("raw1a", "raw1b", "raw2")):
-            states.append(sbuf.tile([P, T], F32, name=name, align_bytes=64))
-        states.append(laid.tile([P, T], F32, name="last_states", offset=STATE_AT))
-        for n, state in enumerate(states):
+        for n, name in enumerate(("rounded0", "rounded1", "rounded2", "table")):
+            state = sbuf.tile([P, T], F32, name=name, align_bytes=64)
             nc.sync.dma_start(out=state[:], in_=rT[P * n : P * (n + 1), :])
+            states.append(state)
 
         def hidden(h):
             banks = [bank_tile(t) for t in range(PACK)]
@@ -180,7 +177,7 @@ def tile_list_msg_gelu_resL_kernel(
                 act = ring.tile([P, HALF], F32, name="act")
                 nc.scalar.activation(out=act[:], in_=banks[t][:], func=ACT.Gelu_apprx_tanh)
                 acts.append(act)
-            scaled = sbuf.tile([P, PACK * HALF], BF16, name="scaled%d" % h)
+            scaled = sbuf.tile([P, PACK * HALF], BF16, name="scaled%d" % h, align_bytes=64)
             for t in range(PACK):
                 nc.scalar.activation(
                     out=scaled[:, HALF * t : HALF * (t + 1)], in_=acts[t][:], func=ACT.Copy, scale=sm_cols[:, t : t + 1]
@@ -205,12 +202,12 @@ def tile_list_msg_gelu_resL_kernel(
             picked.append((whole[:, :HALF], whole[:, HALF:]))
         woven_first = hidden(0)
         edge_w = []
-        for h, name in enumerate(("parted", "rounded3")):
+        for h, name in enumerate(("parted", "table_scales")):
             piece = sbuf.tile([P, HALF], F32, name=name, align_bytes=64)
             nc.sync.dma_start(out=piece[:], in_=wgo[:, HALF * h : HALF * (h + 1)])
             edge_w.append(piece)
-        h_first = quantise_hidden("raw2", "h_plane0", woven_first)
-        last = gather_states(TILES - 1, whole_cols, "woven0")
+        h_first = quantise_hidden("h_codes0", "h_plane0", woven_first)
+        last = gather_states(TILES - 1, whole_cols, "scaled0")
         picked.append((last[:, :HALF], last[:, HALF:]))
 
         def late_page(name):
@@ -218,9 +215,7 @@ def tile_list_msg_gelu_resL_kernel(
             nc.gpsimd.memset(page[:], 0.0)
             pages.append(page)
 
-        page = laid.tile([P, T], F32, name="page1", offset=STATE_AT + 4 * HALF)
-        nc.gpsimd.memset(page[:], 0.0)
-        pages.append(page)
+        late_page("table")
 
         def scatter(h, n, sums):
             nc.vector.tensor_tensor(
@@ -241,20 +236,17 @@ def tile_list_msg_gelu_resL_kernel(
             )
             y_first.append(bank)
 
-        direct = [
-            laid.tile([P, HALF], F32, name="direct0", offset=STATE_AT),
-            sbuf.tile([P, HALF], F32, name="direct1", align_bytes=64),
-        ]
+        direct = []
         for n in range(DIRECT):
-            nc.vector.tensor_tensor(direct[n][:], y_first[n][:], picked[n][0], ALU.add)
+            total = sbuf.tile([P, HALF], F32, name="direct%d" % n, align_bytes=64)
+            nc.vector.tensor_tensor(total[:], y_first[n][:], picked[n][0], ALU.add)
+            direct.append(total)
         for n in range(DIRECT):
             scatter(0, n, direct[n][:])
-        page = laid.tile([P, T], F32, name="page2", offset=0)
-        nc.gpsimd.memset(page[:], 0.0)
-        pages.append(page)
+        late_page("direct0")
 
         woven_second = hidden(1)
-        h_second = quantise_hidden("direct1", "h_plane1", woven_second)
+        h_second = quantise_hidden("h_codes1", "h_plane1", woven_second)
         late_page("woven1")
 
         def turned_product(hq, n):

@@ -75,6 +75,7 @@ def tile_list_msg_gelu_resL_kernel(
         nc.sync.dma_start(out=table[:], in_=tab_words[0].rearrange("p t b -> p (t b)").bitcast(I32))
         raw.append(load_weights(1, R, ("raw1",)))
         raw.append(load_weights(2, R, ("raw2",)))
+        raw.append(load_weights(3, R, ("raw3",)))
 
         pages = [sbuf.tile([P, T], F32, name="page0")]
         lifted = sbuf.tile([P, 2 * J], U8, name="lifted", align_bytes=64)
@@ -133,7 +134,6 @@ def tile_list_msg_gelu_resL_kernel(
             )
         nc.sync.dma_start(out=lifted[: P - LIFT, :].bitcast(I32), in_=gathered[LIFT:, :].bitcast(I32))
         v_planes = (gathered, lifted)
-        raw.append(load_weights(3, R, ("table_scales",)))
 
         first_cols, second_cols = slice(0, HALF_COLS), slice(HALF_COLS, 2 * HALF_COLS)
         weights = [quantise_weights(0)]
@@ -144,9 +144,9 @@ def tile_list_msg_gelu_resL_kernel(
         weights.append(quantise_weights(2))
         both.append(gather_words(TARGET, second_cols, "raw2"))
         weights.append(quantise_weights(3))
-        v_words.append(part_words(both, "table_scales"))
+        v_words.append(part_words(both, "raw3"))
 
-        wd_codes = sbuf.tile([P, 2 * N], U8, name="wd_codes", align_bytes=64)
+        wd_codes = sbuf.tile([P, 2 * N], U8, name="rounded3", align_bytes=64)
         nc.sync.dma_start(out=wd_codes[:].bitcast(I32), in_=wd_words[0].bitcast(I32))
         states = []
         for n, name in enumerate(("rounded0", "rounded1", "rounded2", "table")):
@@ -202,7 +202,7 @@ def tile_list_msg_gelu_resL_kernel(
             picked.append((whole[:, :HALF], whole[:, HALF:]))
         woven_first = hidden(0)
         edge_w = []
-        for h, name in enumerate(("parted", "table_scales")):
+        for h, name in enumerate(("parted", "raw3")):
             piece = sbuf.tile([P, HALF], F32, name=name, align_bytes=64)
             nc.sync.dma_start(out=piece[:], in_=wgo[:, HALF * h : HALF * (h + 1)])
             edge_w.append(piece)

@@ -45,11 +45,6 @@ def tile_list_msg_gelu_resL_kernel(
         def list_half(which, h):
             return lists[which][:, HALF_COLS * h : HALF_COLS * (h + 1)]
 
-        def zero_on_vector(words, zero):
-            cut = words.shape[1] // 2 - 1
-            nc.vector.memset(words[:, :cut], zero)
-            nc.vector.memset(words[:, cut:], zero)
-
         lists = [sbuf.tile([P, J // 16], U16, name="list%d" % which) for which in (SOURCE, TARGET)]
         table = sbuf.tile([P, T], I32, name="table", align_bytes=64)
         table_scales = sbuf.tile([P, T], U8, name="table_scales", align_bytes=64)
@@ -77,20 +72,21 @@ def tile_list_msg_gelu_resL_kernel(
         raw.append(load_weights(2, R, ("raw2",)))
         raw.append(load_weights(3, R, ("raw3",)))
 
-        pages = [sbuf.tile([P, T], F32, name="page0")]
+        pages = [sbuf.tile([P, T], F32, name="page%d" % n) for n in range(2)]
         lifted = sbuf.tile([P, 2 * J], U8, name="lifted", align_bytes=64)
         ident = sbuf.tile([P, P], F32, name="ident")
         wd_plane = sbuf.tile([P, N], U8, name="wd_plane", align_bytes=64)
         nc.gpsimd.memset(wd_plane[:].bitcast(I32), 0)
         make_identity(nc, ident[:])
+        nc.gpsimd.memset(lifted[:].bitcast(I32), 0)
         sm_cols = sbuf.tile([P, PACK], F32, name="sm_cols")
         nc.gpsimd.dma_start(out=sm_cols[:], in_=sm.rearrange("(p i) -> p i", i=PACK))
         for q in range(4):
             nc.gpsimd.dma_start(
                 out=wd_plane[32 * q : 32 * q + 4, :].bitcast(I32), in_=wd_scales[0, 4 * q : 4 * q + 4, :].bitcast(I32)
             )
-        zero_on_vector(lifted[:].bitcast(I32), 0)
-        nc.vector.memset(pages[0][:], 0.0)
+        for page in pages:
+            nc.vector.memset(page[:], 0.0)
 
         def gather_words(which, cols, name):
             both = sbuf.tile([P, 16 * (cols.stop - cols.start)], U32, name=name, align_bytes=64)
@@ -247,7 +243,6 @@ def tile_list_msg_gelu_resL_kernel(
 
         woven_second = hidden(1)
         h_second = quantise_hidden("h_codes1", "h_plane1", woven_second)
-        late_page("woven1")
 
         def turned_product(hq, n):
             bank = bank_tile(n % 2)
@@ -293,4 +288,8 @@ def tile_list_msg_gelu_resL_kernel(
         for n in range(TILES):
             sums = turn_back(1, n, turned[n], turned_product(h_second, n))
             scatter(1, n, sums[:])
-            nc.sync.dma_start(out=out[P * n : P * (n + 1), :], in_=pages[n][:])
+            if n < TILES - 1:
+                nc.sync.dma_start(out=out[P * n : P * (n + 1), :], in_=pages[n][:])
+            else:
+                for queue, cols in ((nc.sync, slice(0, T // 2)), (nc.scalar, slice(T // 2, T))):
+                    queue.dma_start(out=out[P * n : P * (n + 1), cols], in_=pages[n][:, cols])

@@ -72,19 +72,19 @@ def tile_list_msg_gelu_resL_kernel(
         raw.append(load_weights(2, R, ("raw2",)))
         raw.append(load_weights(3, R, ("raw3",)))
 
-        pages = [sbuf.tile([P, T], F32, name="page%d" % n) for n in range(2)]
+        pages = [sbuf.tile([P, T], F32, name="page%d" % n) for n in range(TILES - 1)]
         lifted = sbuf.tile([P, 2 * J], U8, name="lifted", align_bytes=64)
         ident = sbuf.tile([P, P], F32, name="ident")
         wd_plane = sbuf.tile([P, N], U8, name="wd_plane", align_bytes=64)
         nc.gpsimd.memset(wd_plane[:].bitcast(I32), 0)
         make_identity(nc, ident[:])
-        nc.gpsimd.memset(lifted[:].bitcast(I32), 0)
         sm_cols = sbuf.tile([P, PACK], F32, name="sm_cols")
         nc.gpsimd.dma_start(out=sm_cols[:], in_=sm.rearrange("(p i) -> p i", i=PACK))
         for q in range(4):
             nc.gpsimd.dma_start(
                 out=wd_plane[32 * q : 32 * q + 4, :].bitcast(I32), in_=wd_scales[0, 4 * q : 4 * q + 4, :].bitcast(I32)
             )
+        nc.gpsimd.memset(lifted[:].bitcast(I32), 0)
         for page in pages:
             nc.vector.memset(page[:], 0.0)
 
@@ -239,7 +239,6 @@ def tile_list_msg_gelu_resL_kernel(
             direct.append(total)
         for n in range(DIRECT):
             scatter(0, n, direct[n][:])
-        late_page("direct0")
 
         woven_second = hidden(1)
         h_second = quantise_hidden("h_codes1", "h_plane1", woven_second)

@@ -25,9 +25,10 @@ HALF_COLS = HALF // 16
 TILES = N // P
 BLOCKS = HALF // P
 LIFT = 16
-DIRECT = 2
 SOURCE, TARGET = 0, 1
 PASSES = ((SOURCE, 0), (TARGET, 0), (SOURCE, 1), (TARGET, 1))
+
+QUARTER = HALF // 2
 
 
 def tile_list_msg_gelu_resL_kernel(
@@ -36,60 +37,63 @@ def tile_list_msg_gelu_resL_kernel(
     nc = tc.nc
     with ExitStack() as ctx:
         sbuf = ctx.enter_context(tc.tile_pool(name="sbuf", bufs=1))
-        ring = ctx.enter_context(tc.tile_pool(name="ring", bufs=4))
         psum = ctx.enter_context(tc.psum_pool(name="psum", bufs=1))
 
         def bank_tile(index):
             return psum.tile([P, HALF], F32, name="bank%d" % index)
 
-        def list_half(which, h):
-            return lists[which][:, HALF_COLS * h : HALF_COLS * (h + 1)]
-
         lists = [sbuf.tile([P, J // 16], U16, name="list%d" % which) for which in (SOURCE, TARGET)]
         table = sbuf.tile([P, T], I32, name="table", align_bytes=64)
         table_scales = sbuf.tile([P, T], U8, name="table_scales", align_bytes=64)
-        nc.gpsimd.memset(table_scales[:].bitcast(I32), 0)
+        nc.vector.memset(table_scales[:].bitcast(I32), 0)
         nc.sync.dma_start(lists[SOURCE][:], offs)
         scale_rows = tab_scales.rearrange("d (q s) t -> s q d t", s=4)
         for s in range(4):
             nc.sync.dma_start(out=table_scales[s:P:LIFT, :].bitcast(I32), in_=scale_rows[s].bitcast(I32))
-
         nc.sync.dma_start(lists[TARGET][:], offs2)
+        w_rows = sbuf.tile([P, P], F32, name="w_rows")
+        nc.sync.dma_start(out=w_rows[:], in_=wgo.rearrange("r (b c) -> (r b) c", c=P)[:P, :])
 
-        def load_weights(k, width, names):
+        def load_weights(k):
             which, d = PASSES[k]
             rows = (ws, wt)[which][K_PASS * d : K_PASS * (d + 1), :].rearrange("(p i) c -> p i c", i=PACK)
-            pieces = []
-            for c0, name in zip(range(0, R, width), names):
-                piece = sbuf.tile([P, PACK, width], F32, name=name, align_bytes=64)
-                nc.sync.dma_start(out=piece[:], in_=rows[:, :, c0 : c0 + width])
-                pieces.append(piece)
-            return pieces
+            piece = sbuf.tile([P, PACK, R], F32, name="raw%d" % k, align_bytes=64)
+            nc.sync.dma_start(out=piece[:], in_=rows)
+            return piece
 
-        raw = [load_weights(0, R // 2, ("raw0a", "raw0b"))]
+        raw = [load_weights(0)]
         nc.sync.dma_start(out=table[:], in_=tab_words[0].rearrange("p t b -> p (t b)").bitcast(I32))
-        raw.append(load_weights(1, R, ("raw1",)))
-        raw.append(load_weights(2, R, ("raw2",)))
-        raw.append(load_weights(3, R, ("raw3",)))
-
-        pages = [sbuf.tile([P, T], F32, name="page%d" % n) for n in range(TILES - 1)]
-        lifted = sbuf.tile([P, 2 * J], U8, name="lifted", align_bytes=64)
-        ident = sbuf.tile([P, P], F32, name="ident")
-        wd_plane = sbuf.tile([P, N], U8, name="wd_plane", align_bytes=64)
-        nc.gpsimd.memset(wd_plane[:].bitcast(I32), 0)
-        make_identity(nc, ident[:])
+        raw.extend(load_weights(k) for k in range(1, len(PASSES)))
         sm_cols = sbuf.tile([P, PACK], F32, name="sm_cols")
-        nc.gpsimd.dma_start(out=sm_cols[:], in_=sm.rearrange("(p i) -> p i", i=PACK))
-        for q in range(4):
-            nc.gpsimd.dma_start(
-                out=wd_plane[32 * q : 32 * q + 4, :].bitcast(I32), in_=wd_scales[0, 4 * q : 4 * q + 4, :].bitcast(I32)
-            )
-        nc.gpsimd.memset(lifted[:].bitcast(I32), 0)
-        for page in pages:
-            nc.vector.memset(page[:], 0.0)
+        nc.sync.dma_start(out=sm_cols[:], in_=sm.rearrange("(p i) -> p i", i=PACK))
 
-        def gather_words(which, cols, name):
-            both = sbuf.tile([P, 16 * (cols.stop - cols.start)], U32, name=name, align_bytes=64)
+        lifted = sbuf.tile([P, 2 * J], U8, name="lifted", align_bytes=64)
+        nc.vector.memset(lifted[:].bitcast(I32), 0)
+        ident = sbuf.tile([P, P], F32, name="ident")
+        make_identity(nc, ident[:])
+        bank = bank_tile(4)
+        nc.tensor.transpose(bank[:, :P], w_rows[:], ident[:])
+        w_cols = sbuf.tile([P, J // P], F32, name="w_cols")
+        nc.scalar.copy(out=w_cols[:], in_=bank[:, : J // P])
+        edge_w = sbuf.tile([P, J], F32, name="edge_w", align_bytes=64)
+        for h in range(2):
+            bank = bank_tile(5 + h)
+            for b in range(BLOCKS):
+                block = BLOCKS * h + b
+                nc.tensor.transpose(
+                    bank[:, P * b : P * (b + 1)], w_cols[:, block : block + 1].to_broadcast([P, P]), ident[:]
+                )
+            nc.scalar.copy(out=edge_w[:, HALF * h : HALF * (h + 1)], in_=bank[:])
+        pages = {0: sbuf.tile([P, T], F32, name="page0")}
+        nc.vector.memset(pages[0][:], 0.0)
+
+        def late_page(n, name):
+            pages[n] = sbuf.tile([P, T], F32, name=name, align_bytes=64)
+            nc.gpsimd.memset(pages[n][:], 0.0)
+
+        def gather_words(which, h, name):
+            both = sbuf.tile([P, HALF], U32, name=name, align_bytes=64)
+            cols = slice(HALF_COLS * h, HALF_COLS * (h + 1))
             nc.vector.tensor_copy(out=both[:], in_=table[:].bitcast(U32).indirect(lists[which][:, cols]))
             return both
 
@@ -107,21 +111,14 @@ def tile_list_msg_gelu_resL_kernel(
 
         def quantise_weights(k):
             rounded = sbuf.tile([P, PACK * R], BF16, name="rounded%d" % k, align_bytes=64)
-            by_m = rounded[:].rearrange("p (t m i) -> p m i t", t=PACK, i=PACK)
-            m0 = 0
-            for piece in raw[k]:
-                m1 = m0 + piece.shape[2] // PACK
-                nc.scalar.copy(out=by_m[:, m0:m1], in_=piece[:].rearrange("p i (m t) -> p m i t", t=PACK))
-                m0 = m1
+            nc.scalar.copy(
+                out=rounded[:].rearrange("p (t m i) -> p m i t", t=PACK, i=PACK),
+                in_=raw[k][:].rearrange("p i (m t) -> p m i t", t=PACK),
+            )
             codes = sbuf.tile([P, R], U32, name="w_codes%d" % k, align_bytes=64)
             plane = sbuf.tile([P, R], U8, name="w_plane%d" % k, align_bytes=64)
             nc.vector.quantize_mx(out=codes[:].bitcast(FP8X4), scales=plane[:], in_=rounded[:])
             return codes, plane
-
-        def gather_states(n, cols, name):
-            picked = sbuf.tile([P, 16 * (cols.stop - cols.start)], F32, name=name, align_bytes=64)
-            nc.vector.tensor_copy(out=picked[:], in_=states[n][:].indirect(lists[TARGET][:, cols]))
-            return picked
 
         gathered = sbuf.tile([P, 2 * J], U8, name="gathered_plane", align_bytes=64)
         for which in (SOURCE, TARGET):
@@ -131,27 +128,37 @@ def tile_list_msg_gelu_resL_kernel(
         nc.sync.dma_start(out=lifted[: P - LIFT, :].bitcast(I32), in_=gathered[LIFT:, :].bitcast(I32))
         v_planes = (gathered, lifted)
 
-        first_cols, second_cols = slice(0, HALF_COLS), slice(HALF_COLS, 2 * HALF_COLS)
         weights = [quantise_weights(0)]
-        both = [gather_words(which, first_cols, "both%d" % which) for which in (SOURCE, TARGET)]
-        v_words = [part_words(both, "parted")]
-        weights.append(quantise_weights(1))
-        both = [gather_words(SOURCE, second_cols, "raw1")]
-        weights.append(quantise_weights(2))
-        both.append(gather_words(TARGET, second_cols, "raw2"))
-        weights.append(quantise_weights(3))
-        v_words.append(part_words(both, "raw3"))
 
-        wd_codes = sbuf.tile([P, 2 * N], U8, name="rounded3", align_bytes=64)
-        nc.sync.dma_start(out=wd_codes[:].bitcast(I32), in_=wd_words[0].bitcast(I32))
-        states = []
-        for n, name in enumerate(("rounded0", "rounded1", "rounded2", "table")):
+        def load_states(n, name):
             state = sbuf.tile([P, T], F32, name=name, align_bytes=64)
             nc.sync.dma_start(out=state[:], in_=rT[P * n : P * (n + 1), :])
-            states.append(state)
+            return state
 
-        def hidden(h):
-            banks = [bank_tile(t) for t in range(PACK)]
+        states = {1: load_states(1, "rounded0")}
+        both = [gather_words(which, 0, "both%d" % which) for which in (SOURCE, TARGET)]
+        v_words = [part_words(both, "parted")]
+        states[2] = load_states(2, "both0")
+        weights.append(quantise_weights(1))
+        wd_bytes = sbuf.tile([P, 3 * N], U8, name="rounded1", align_bytes=64)
+        wd_codes, wd_plane = wd_bytes[:, : 2 * N], wd_bytes[:, 2 * N :]
+        for q in range(4):
+            rows = wd_scales[0, 4 * q : 4 * q + 4, :].bitcast(I32)
+            nc.sync.dma_start(
+                out=wd_plane[32 * q : 32 * (q + 1), :].bitcast(I32),
+                in_=rows.unsqueeze(0).to_broadcast([8, 4, N // 4]),
+            )
+        nc.sync.dma_start(out=wd_codes.bitcast(I32), in_=wd_words[0].bitcast(I32))
+        both = [gather_words(SOURCE, 1, "raw1")]
+        weights.append(quantise_weights(2))
+        both.append(gather_words(TARGET, 1, "raw2"))
+        weights.append(quantise_weights(3))
+        v_words.append(part_words(both, "raw3"))
+        states[3] = load_states(3, "table")
+        states[0] = load_states(0, "rounded2")
+
+        def first_stage(h):
+            banks = [bank_tile(4 * h + t) for t in range(PACK)]
             if h == 0:
                 order = [(k, t) for k in range(len(PASSES)) for t in range(PACK)]
             else:
@@ -168,127 +175,146 @@ def tile_list_msg_gelu_resL_kernel(
                     start=(k == 0),
                     stop=(k == len(PASSES) - 1),
                 )
-            acts = []
+            return banks
+
+        def act_tile(name):
+            return sbuf.tile([P, PACK * QUARTER], F32, name=name, align_bytes=64)
+
+        def smooth_quarter(g, banks, name):
+            acts = act_tile(name)
+            acts = [gelu(acts, banks, g, t) for t in range(PACK)]
+            scaled = scaled_tile(g)
             for t in range(PACK):
-                act = ring.tile([P, HALF], F32, name="act")
-                nc.scalar.activation(out=act[:], in_=banks[t][:], func=ACT.Gelu_apprx_tanh)
-                acts.append(act)
-            scaled = sbuf.tile([P, PACK * HALF], BF16, name="scaled%d" % h, align_bytes=64)
-            for t in range(PACK):
-                nc.scalar.activation(
-                    out=scaled[:, HALF * t : HALF * (t + 1)], in_=acts[t][:], func=ACT.Copy, scale=sm_cols[:, t : t + 1]
-                )
-            woven = sbuf.tile([P, PACK * HALF], BF16, name="woven%d" % h, align_bytes=64)
+                smooth(scaled, t, acts[t])
+            return scaled
+
+        def gelu(acts, banks, g, t):
+            act = acts[:, QUARTER * t : QUARTER * (t + 1)]
+            c0 = QUARTER * (g % 2)
+            nc.scalar.activation(out=act, in_=banks[t][:, c0 : c0 + QUARTER], func=ACT.Gelu_apprx_tanh)
+            return act
+
+        def smooth(scaled, t, act):
+            nc.scalar.activation(
+                out=scaled[:, QUARTER * t : QUARTER * (t + 1)], in_=act, func=ACT.Copy, scale=sm_cols[:, t : t + 1]
+            )
+
+        def scaled_tile(g):
+            return sbuf.tile([P, PACK * QUARTER], BF16, name="scaled%d" % g, align_bytes=64)
+
+        def weave_and_quantise(g, scaled, codes_name):
+            woven = sbuf.tile([P, PACK * QUARTER], BF16, name="woven%d" % g, align_bytes=64)
             nc.scalar.copy(
                 out=woven[:].rearrange("p (c e t) -> p c t e", e=4, t=PACK),
                 in_=scaled[:].rearrange("p (t c e) -> p c t e", t=PACK, e=4),
             )
-            return woven
-
-        def quantise_hidden(codes_name, plane_name, woven):
-            codes = sbuf.tile([P, HALF], U32, name=codes_name, align_bytes=64)
-            plane = sbuf.tile([P, HALF], U8, name=plane_name, align_bytes=64)
+            codes = sbuf.tile([P, QUARTER], U32, name=codes_name, align_bytes=64)
+            plane = sbuf.tile([P, QUARTER], U8, name="h_plane%d" % g, align_bytes=64)
             nc.vector.quantize_mx(out=codes[:].bitcast(FP8X4), scales=plane[:], in_=woven[:])
             return codes, plane
 
-        whole_cols = slice(0, 2 * HALF_COLS)
-        picked = []
-        for n in range(TILES - 1):
-            whole = gather_states(n, whole_cols, "picked%d" % n)
-            picked.append((whole[:, :HALF], whole[:, HALF:]))
-        woven_first = hidden(0)
-        edge_w = []
-        for h, name in enumerate(("parted", "raw3")):
-            piece = sbuf.tile([P, HALF], F32, name=name, align_bytes=64)
-            nc.sync.dma_start(out=piece[:], in_=wgo[:, HALF * h : HALF * (h + 1)])
-            edge_w.append(piece)
-        h_first = quantise_hidden("h_codes0", "h_plane0", woven_first)
-        last = gather_states(TILES - 1, whole_cols, "scaled0")
-        picked.append((last[:, :HALF], last[:, HALF:]))
-
-        def late_page(name):
-            page = sbuf.tile([P, T], F32, name=name, align_bytes=64)
-            nc.gpsimd.memset(page[:], 0.0)
-            pages.append(page)
-
-        late_page("table")
-
-        def scatter(h, n, sums):
+        def gather_states(n, j0, j1):
             nc.vector.tensor_tensor(
-                pages[n][:].indirect(list_half(TARGET, h)), sums, edge_w[h][:], ALU.mult
+                weighted(n, j0, j1),
+                states[n][:].indirect(lists[TARGET][:, j0 // 16 : j1 // 16]),
+                edge_w[:, j0:j1],
+                ALU.mult,
             )
 
-        y_first = []
-        for n in range(DIRECT):
-            bank = bank_tile(4 + n)
-            nc.tensor.matmul_mx(
-                out=bank[:],
-                lhsT=wd_codes[:, 2 * P * n : 2 * P * (n + 1)].bitcast(FP4X4),
-                lhsT_scale=wd_plane[:, P * n : P * (n + 1)],
-                rhs=h_first[0][:].bitcast(FP8X4),
-                rhs_scale=h_first[1][:],
-                start=True,
-                stop=True,
-            )
-            y_first.append(bank)
+        messages = {}
 
-        direct = []
-        for n in range(DIRECT):
-            total = sbuf.tile([P, HALF], F32, name="direct%d" % n, align_bytes=64)
-            nc.vector.tensor_tensor(total[:], y_first[n][:], picked[n][0], ALU.add)
-            direct.append(total)
-        for n in range(DIRECT):
-            scatter(0, n, direct[n][:])
-
-        woven_second = hidden(1)
-        h_second = quantise_hidden("h_codes1", "h_plane1", woven_second)
-
-        def turned_product(hq, n):
-            bank = bank_tile(n % 2)
-            for b in range(BLOCKS):
+        def turned_messages(g, hq):
+            for b in range(2):
+                bank = bank_tile(b)
                 nc.tensor.matmul_mx(
-                    out=bank[:, P * b : P * (b + 1)],
+                    out=bank[:],
                     lhsT=hq[0][:, P * b : P * (b + 1)].bitcast(FP8X4),
                     lhsT_scale=hq[1][:, P * b : P * (b + 1)],
-                    rhs=wd_codes[:, 2 * P * n : 2 * P * (n + 1)].bitcast(FP4X4),
-                    rhs_scale=wd_plane[:, P * n : P * (n + 1)],
+                    rhs=wd_codes.bitcast(FP4X4),
+                    rhs_scale=wd_plane,
                     start=True,
                     stop=True,
                 )
-            y_turned = ring.tile([P, HALF], F32, name="y_turned")
-            nc.scalar.copy(out=y_turned[:], in_=bank[:])
-            return y_turned
+                block = 2 * g + b
+                messages[block] = sbuf.tile([P, N], F32, name="message%d" % block)
+                nc.scalar.activation(
+                    out=messages[block][:], in_=bank[:], func=ACT.Copy, scale=w_cols[:, block : block + 1]
+                )
 
-        def turn_states(h, n):
-            bank = bank_tile(4 - 2 * h + n % 2)
-            for b in range(BLOCKS):
-                nc.tensor.transpose(bank[:, P * b : P * (b + 1)], picked[n][h][:, P * b : P * (b + 1)], ident[:])
-            turned = ring.tile([P, HALF], F32, name="turned")
-            nc.scalar.copy(out=turned[:], in_=bank[:])
-            return turned
+        def put(n, blocks):
+            width = P * len(blocks)
+            bank = bank_tile(2 + n % 2)
+            for i, block in enumerate(blocks):
+                nc.tensor.transpose(bank[:, P * i : P * (i + 1)], messages[block][:, P * n : P * (n + 1)], ident[:])
+            upright = sbuf.tile([P, width], F32, name="upright%d_%d" % (n, blocks[0]), align_bytes=64)
+            nc.scalar.copy(out=upright[:], in_=bank[:, :width])
+            j0 = P * blocks[0]
+            nc.vector.tensor_tensor(
+                pages[n][:].indirect(lists[TARGET][:, j0 // 16 : (j0 + width) // 16]),
+                upright[:],
+                weighted(n, j0, j0 + width),
+                ALU.add,
+            )
 
-        def turn_back(h, n, turned, y_turned):
-            bank = bank_tile(4 * h + n)
-            for b in range(BLOCKS):
-                cols = slice(P * b, P * (b + 1))
-                for first, source in ((True, turned[:, cols]), (False, y_turned[:, cols])):
-                    nc.tensor.matmul(
-                        bank[:, cols], lhsT=source, rhs=ident[:], start=first, stop=not first, is_transpose=True
-                    )
-            sums = ring.tile([P, HALF], F32, name="sums")
-            nc.scalar.copy(out=sums[:], in_=bank[:])
-            return sums
-
-        for n in range(DIRECT, TILES):
-            sums = turn_back(0, n, turn_states(0, n), turned_product(h_first, n))
-            scatter(0, n, sums[:])
-
-        turned = [turn_states(1, n) for n in range(TILES)]
-        for n in range(TILES):
-            sums = turn_back(1, n, turned[n], turned_product(h_second, n))
-            scatter(1, n, sums[:])
+        def store(n):
             if n < TILES - 1:
                 nc.sync.dma_start(out=out[P * n : P * (n + 1), :], in_=pages[n][:])
             else:
                 for queue, cols in ((nc.sync, slice(0, T // 2)), (nc.scalar, slice(T // 2, T))):
                     queue.dma_start(out=out[P * n : P * (n + 1), cols], in_=pages[n][:, cols])
+
+        later, first = {}, {}
+
+        def weighted(n, j0, j1):
+            if j0 < QUARTER:
+                return first[n][:, j0:j1]
+            return later[n][:, j0 - QUARTER : j1 - QUARTER]
+
+        rest = J - QUARTER
+        for n in (1, 2):
+            later[n] = sbuf.tile([P, rest], F32, name="weighted%d" % n, align_bytes=64)[:]
+            gather_states(n, QUARTER, J)
+        sums = [first_stage(0)]
+        scaled = smooth_quarter(0, sums[0], "act0")
+        hq = weave_and_quantise(0, scaled, "h_codes0")
+        late_pair = sbuf.tile([P, 2 * rest + QUARTER], F32, name="scaled0", align_bytes=64)
+        later[3], later[0], first[0] = late_pair[:, :rest], late_pair[:, rest : 2 * rest], late_pair[:, 2 * rest :]
+        gather_states(3, QUARTER, J)
+        gather_states(0, QUARTER, J)
+        gather_states(0, 0, QUARTER)
+        firsts = sbuf.tile([P, rest], F32, name="rounded2", align_bytes=64)
+        for n in range(1, TILES):
+            first[n] = firsts[:, QUARTER * (n - 1) : QUARTER * n]
+            gather_states(n, 0, QUARTER)
+        late_page(1, "raw2")
+        late_page(2, "woven0")
+        late_page(3, "rounded0")
+        acts = act_tile("act0")
+        acts = [gelu(acts, sums[0], 1, t) for t in range(PACK)]
+        turned_messages(0, hq)
+        sums.append(first_stage(1))
+        scaled = scaled_tile(1)
+        for t in range(PACK):
+            smooth(scaled, t, acts[t])
+        put(0, (0, 1))
+        hq = weave_and_quantise(1, scaled, "both0")
+        for n in range(1, TILES):
+            put(n, (0, 1))
+        scaled = smooth_quarter(2, sums[1], "act2")
+        turned_messages(1, hq)
+        hq = weave_and_quantise(2, scaled, "upright2_0")
+        for n in range(TILES - 1):
+            put(n, (2, 3))
+        scaled = smooth_quarter(3, sums[1], "woven1")
+        hq_last = weave_and_quantise(3, scaled, "upright1_2")
+        put(TILES - 1, (2, 3))
+        turned_messages(2, hq)
+        for n in range(2):
+            put(n, (4, 5))
+        turned_messages(3, hq_last)
+        for n in range(2):
+            put(n, (6, 7))
+            store(n)
+        for n in range(2, TILES):
+            put(n, (4, 5, 6, 7))
+            store(n)

@@ -47,12 +47,12 @@ def tile_list_msg_gelu_resL_kernel(
         table_scales = sbuf.tile([P, T], U8, name="table_scales", align_bytes=64)
         nc.vector.memset(table_scales[:].bitcast(I32), 0)
         nc.sync.dma_start(lists[SOURCE][:], offs)
+        w_rows = sbuf.tile([P, P], F32, name="w_rows")
+        nc.sync.dma_start(out=w_rows[:], in_=wgo.rearrange("r (b c) -> (r b) c", c=P)[:P, :])
         scale_rows = tab_scales.rearrange("d (q s) t -> s q d t", s=4)
         for s in range(4):
             nc.sync.dma_start(out=table_scales[s:P:LIFT, :].bitcast(I32), in_=scale_rows[s].bitcast(I32))
         nc.sync.dma_start(lists[TARGET][:], offs2)
-        w_rows = sbuf.tile([P, P], F32, name="w_rows")
-        nc.sync.dma_start(out=w_rows[:], in_=wgo.rearrange("r (b c) -> (r b) c", c=P)[:P, :])
 
         def load_weights(k):
             which, d = PASSES[k]
@@ -223,9 +223,9 @@ def tile_list_msg_gelu_resL_kernel(
 
         messages = {}
 
-        def turned_messages(g, hq):
+        def turned_messages(g, hq, banks):
             for b in range(2):
-                bank = bank_tile(b)
+                bank = bank_tile(banks[b])
                 nc.tensor.matmul_mx(
                     out=bank[:],
                     lhsT=hq[0][:, P * b : P * (b + 1)].bitcast(FP8X4),
@@ -241,12 +241,12 @@ def tile_list_msg_gelu_resL_kernel(
                     out=messages[block][:], in_=bank[:], func=ACT.Copy, scale=w_cols[:, block : block + 1]
                 )
 
-        def put(n, blocks):
+        def put(n, blocks, bank_index, name=None):
             width = P * len(blocks)
-            bank = bank_tile(2 + n % 2)
+            bank = bank_tile(bank_index)
             for i, block in enumerate(blocks):
                 nc.tensor.transpose(bank[:, P * i : P * (i + 1)], messages[block][:, P * n : P * (n + 1)], ident[:])
-            upright = sbuf.tile([P, width], F32, name="upright%d_%d" % (n, blocks[0]), align_bytes=64)
+            upright = sbuf.tile([P, width], F32, name=name or "upright%d_%d" % (n, blocks[0]), align_bytes=64)
             nc.scalar.copy(out=upright[:], in_=bank[:, :width])
             j0 = P * blocks[0]
             nc.vector.tensor_tensor(
@@ -291,30 +291,30 @@ def tile_list_msg_gelu_resL_kernel(
         late_page(3, "rounded0")
         acts = act_tile("act0")
         acts = [gelu(acts, sums[0], 1, t) for t in range(PACK)]
-        turned_messages(0, hq)
+        turned_messages(0, hq, (0, 1))
         sums.append(first_stage(1))
         scaled = scaled_tile(1)
         for t in range(PACK):
             smooth(scaled, t, acts[t])
-        put(0, (0, 1))
+        put(0, (0, 1), 2)
         hq = weave_and_quantise(1, scaled, "both0")
         for n in range(1, TILES):
-            put(n, (0, 1))
+            put(n, (0, 1), 2 + n % 2)
         scaled = smooth_quarter(2, sums[1], "act2")
-        turned_messages(1, hq)
-        hq = weave_and_quantise(2, scaled, "upright2_0")
+        turned_messages(1, hq, (0, 1))
+        hq = weave_and_quantise(2, scaled, "upright1_0")
         for n in range(TILES - 1):
-            put(n, (2, 3))
+            put(n, (2, 3), 2 + n % 2)
         scaled = smooth_quarter(3, sums[1], "woven1")
         hq_last = weave_and_quantise(3, scaled, "upright1_2")
-        put(TILES - 1, (2, 3))
-        turned_messages(2, hq)
+        put(TILES - 1, (2, 3), 0, "scaled3")
+        turned_messages(2, hq, (3, 2))
         for n in range(2):
-            put(n, (4, 5))
-        turned_messages(3, hq_last)
+            put(n, (4, 5), 4 + n)
+        turned_messages(3, hq_last, (4, 5))
         for n in range(2):
-            put(n, (6, 7))
+            put(n, (6, 7), 6 + n)
             store(n)
         for n in range(2, TILES):
-            put(n, (4, 5, 6, 7))
+            put(n, (4, 5, 6, 7), n - 1)
             store(n)

@@ -37,6 +37,7 @@ def tile_list_msg_gelu_resL_kernel(
     nc = tc.nc
     with ExitStack() as ctx:
         sbuf = ctx.enter_context(tc.tile_pool(name="sbuf", bufs=1))
+        laid = ctx.enter_context(tc.tile_pool(name="laid", bufs=1))
         psum = ctx.enter_context(tc.psum_pool(name="psum", bufs=1))
 
         def bank_tile(index):
@@ -84,17 +85,18 @@ def tile_list_msg_gelu_resL_kernel(
                     bank[:, P * b : P * (b + 1)], w_cols[:, block : block + 1].to_broadcast([P, P]), ident[:]
                 )
             nc.scalar.copy(out=edge_w[:, HALF * h : HALF * (h + 1)], in_=bank[:])
-        pages = {0: sbuf.tile([P, T], F32, name="page0")}
-        nc.vector.memset(pages[0][:], 0.0)
+        pages = {}
 
         def late_page(n, name):
             pages[n] = sbuf.tile([P, T], F32, name=name, align_bytes=64)
             nc.gpsimd.memset(pages[n][:], 0.0)
 
-        def gather_words(which, h, name):
-            both = sbuf.tile([P, HALF], U32, name=name, align_bytes=64)
+        def gather_words(h, name):
+            pair = sbuf.tile([P, 2 * HALF], U32, name=name, align_bytes=64)
             cols = slice(HALF_COLS * h, HALF_COLS * (h + 1))
-            nc.vector.tensor_copy(out=both[:], in_=table[:].bitcast(U32).indirect(lists[which][:, cols]))
+            both = [pair[:, HALF * which : HALF * (which + 1)] for which in (SOURCE, TARGET)]
+            for which in (SOURCE, TARGET):
+                nc.vector.tensor_copy(out=both[which], in_=table[:].bitcast(U32).indirect(lists[which][:, cols]))
             return both
 
         def part_words(both, name):
@@ -104,13 +106,16 @@ def tile_list_msg_gelu_resL_kernel(
                 own = parted[:, 4 * HALF * which : 4 * HALF * (which + 1)]
                 nc.vector.tensor_copy(
                     out=own.bitcast(U16).rearrange("p (d j) -> p d j", d=2),
-                    in_=both[which][:].bitcast(U16).rearrange("p (j d) -> p d j", d=2),
+                    in_=both[which].bitcast(U16).rearrange("p (j d) -> p d j", d=2),
                 )
                 result.append(own)
             return result
 
         def quantise_weights(k):
-            rounded = sbuf.tile([P, PACK * R], BF16, name="rounded%d" % k, align_bytes=64)
+            if k < len(PASSES) - 1:
+                rounded = sbuf.tile([P, PACK * R], BF16, name="rounded%d" % k, align_bytes=64)
+            else:
+                rounded = laid.tile([P, PACK * R], BF16, name="rounded3", align_bytes=64, offset=3 * T)
             nc.scalar.copy(
                 out=rounded[:].rearrange("p (t m i) -> p m i t", t=PACK, i=PACK),
                 in_=raw[k][:].rearrange("p i (m t) -> p m i t", t=PACK),
@@ -136,7 +141,7 @@ def tile_list_msg_gelu_resL_kernel(
             return state
 
         states = {1: load_states(1, "rounded0")}
-        both = [gather_words(which, 0, "both%d" % which) for which in (SOURCE, TARGET)]
+        both = gather_words(0, "both0")
         v_words = [part_words(both, "parted")]
         states[2] = load_states(2, "both0")
         weights.append(quantise_weights(1))
@@ -149,11 +154,10 @@ def tile_list_msg_gelu_resL_kernel(
                 in_=rows.unsqueeze(0).to_broadcast([8, 4, N // 4]),
             )
         nc.sync.dma_start(out=wd_codes.bitcast(I32), in_=wd_words[0].bitcast(I32))
-        both = [gather_words(SOURCE, 1, "raw1")]
+        both = gather_words(1, "raw1")
         weights.append(quantise_weights(2))
-        both.append(gather_words(TARGET, 1, "raw2"))
+        v_words.append(part_words(both, "raw2"))
         weights.append(quantise_weights(3))
-        v_words.append(part_words(both, "raw3"))
         states[3] = load_states(3, "table")
         states[0] = load_states(0, "rounded2")
 
@@ -162,7 +166,7 @@ def tile_list_msg_gelu_resL_kernel(
             if h == 0:
                 order = [(k, t) for k in range(len(PASSES)) for t in range(PACK)]
             else:
-                order = [(k, t) for t in range(PACK) for k in range(len(PASSES))]
+                order = [(k, t) for t in range(PACK) for k in reversed(range(len(PASSES)))]
             for k, t in order:
                 which, d = PASSES[k]
                 codes, plane = weights[k]
@@ -172,8 +176,8 @@ def tile_list_msg_gelu_resL_kernel(
                     lhsT_scale=plane[:, P * t : P * (t + 1)],
                     rhs=v_words[h][which][:, 2 * HALF * d : 2 * HALF * (d + 1)].bitcast(FP4X4),
                     rhs_scale=v_planes[d][:, J * which + HALF * h : J * which + HALF * (h + 1)],
-                    start=(k == 0),
-                    stop=(k == len(PASSES) - 1),
+                    start=(k == order[0][0]),
+                    stop=(k == order[-1][0]),
                 )
             return banks
 
@@ -202,8 +206,8 @@ def tile_list_msg_gelu_resL_kernel(
         def scaled_tile(g):
             return sbuf.tile([P, PACK * QUARTER], BF16, name="scaled%d" % g, align_bytes=64)
 
-        def weave_and_quantise(g, scaled, codes_name):
-            woven = sbuf.tile([P, PACK * QUARTER], BF16, name="woven%d" % g, align_bytes=64)
+        def weave_and_quantise(g, scaled, codes_name, woven_name=None):
+            woven = sbuf.tile([P, PACK * QUARTER], BF16, name=woven_name or "woven%d" % g, align_bytes=64)
             nc.scalar.copy(
                 out=woven[:].rearrange("p (c e t) -> p c t e", e=4, t=PACK),
                 in_=scaled[:].rearrange("p (t c e) -> p c t e", t=PACK, e=4),
@@ -236,7 +240,7 @@ def tile_list_msg_gelu_resL_kernel(
                     stop=True,
                 )
                 block = 2 * g + b
-                messages[block] = sbuf.tile([P, N], F32, name="message%d" % block)
+                messages[block] = sbuf.tile([P, N], F32, name="message%d" % block, align_bytes=64)
                 nc.scalar.activation(
                     out=messages[block][:], in_=bank[:], func=ACT.Copy, scale=w_cols[:, block : block + 1]
                 )
@@ -274,19 +278,22 @@ def tile_list_msg_gelu_resL_kernel(
         for n in (1, 2):
             later[n] = sbuf.tile([P, rest], F32, name="weighted%d" % n, align_bytes=64)[:]
             gather_states(n, QUARTER, J)
+        whole = sbuf.tile([P, J], F32, name="weighted3", align_bytes=64)
+        first[3], later[3] = whole[:, :QUARTER], whole[:, QUARTER:]
+        nc.vector.tensor_tensor(whole[:], states[3][:].indirect(lists[TARGET][:]), edge_w[:], ALU.mult)
         sums = [first_stage(0)]
         scaled = smooth_quarter(0, sums[0], "act0")
-        hq = weave_and_quantise(0, scaled, "h_codes0")
-        late_pair = sbuf.tile([P, 2 * rest + QUARTER], F32, name="scaled0", align_bytes=64)
-        later[3], later[0], first[0] = late_pair[:, :rest], late_pair[:, rest : 2 * rest], late_pair[:, 2 * rest :]
-        gather_states(3, QUARTER, J)
-        gather_states(0, QUARTER, J)
-        gather_states(0, 0, QUARTER)
-        firsts = sbuf.tile([P, rest], F32, name="rounded2", align_bytes=64)
-        for n in range(1, TILES):
+        hq = weave_and_quantise(0, scaled, "table")
+        whole = sbuf.tile([P, J], F32, name="scaled0", align_bytes=64)
+        first[0], later[0] = whole[:, :QUARTER], whole[:, QUARTER:]
+        nc.vector.tensor_tensor(whole[:], states[0][:].indirect(lists[TARGET][:]), edge_w[:], ALU.mult)
+        firsts = sbuf.tile([P, HALF], F32, name="rounded2", align_bytes=64)
+        for n in (1, 2):
             first[n] = firsts[:, QUARTER * (n - 1) : QUARTER * n]
             gather_states(n, 0, QUARTER)
-        late_page(1, "raw2")
+        for n in range(2):
+            pages[n] = laid.tile([P, T], F32, name="page%d" % n, align_bytes=64, offset=4 * T * n)
+            nc.gpsimd.memset(pages[n][:], 0.0)
         late_page(2, "woven0")
         late_page(3, "rounded0")
         acts = act_tile("act0")
@@ -297,15 +304,15 @@ def tile_list_msg_gelu_resL_kernel(
         for t in range(PACK):
             smooth(scaled, t, acts[t])
         put(0, (0, 1), 2)
-        hq = weave_and_quantise(1, scaled, "both0")
+        hq = weave_and_quantise(1, scaled, "both0", "h_plane0")
         for n in range(1, TILES):
             put(n, (0, 1), 2 + n % 2)
-        scaled = smooth_quarter(2, sums[1], "act2")
+        scaled = smooth_quarter(2, sums[1], "scaled1")
         turned_messages(1, hq, (0, 1))
         hq = weave_and_quantise(2, scaled, "upright1_0")
         for n in range(TILES - 1):
             put(n, (2, 3), 2 + n % 2)
-        scaled = smooth_quarter(3, sums[1], "woven1")
+        scaled = smooth_quarter(3, sums[1], "h_plane0")
         hq_last = weave_and_quantise(3, scaled, "upright1_2")
         put(TILES - 1, (2, 3), 0, "scaled3")
         turned_messages(2, hq, (3, 2))

@@ -204,7 +204,8 @@ def tile_list_msg_gelu_resL_kernel(
             )
 
         def scaled_tile(g):
-            return sbuf.tile([P, PACK * QUARTER], BF16, name="scaled%d" % g, align_bytes=64)
+            name = "h_plane%d" % (g - 1) if g else "scaled0"
+            return sbuf.tile([P, PACK * QUARTER], BF16, name=name, align_bytes=64)
 
         def weave_and_quantise(g, scaled, codes_name, woven_name=None):
             woven = sbuf.tile([P, PACK * QUARTER], BF16, name=woven_name or "woven%d" % g, align_bytes=64)
@@ -245,20 +246,22 @@ def tile_list_msg_gelu_resL_kernel(
                     out=messages[block][:], in_=bank[:], func=ACT.Copy, scale=w_cols[:, block : block + 1]
                 )
 
-        def put(n, blocks, bank_index, name=None):
+        def put(n, blocks, bank_index, upright):
             width = P * len(blocks)
             bank = bank_tile(bank_index)
             for i, block in enumerate(blocks):
                 nc.tensor.transpose(bank[:, P * i : P * (i + 1)], messages[block][:, P * n : P * (n + 1)], ident[:])
-            upright = sbuf.tile([P, width], F32, name=name or "upright%d_%d" % (n, blocks[0]), align_bytes=64)
-            nc.scalar.copy(out=upright[:], in_=bank[:, :width])
+            nc.scalar.copy(out=upright, in_=bank[:, :width])
             j0 = P * blocks[0]
             nc.vector.tensor_tensor(
                 pages[n][:].indirect(lists[TARGET][:, j0 // 16 : (j0 + width) // 16]),
-                upright[:],
+                upright,
                 weighted(n, j0, j0 + width),
                 ALU.add,
             )
+
+        def upright_tile(width, name):
+            return sbuf.tile([P, width], F32, name=name, align_bytes=64)
 
         def store(n):
             if n < TILES - 1:
@@ -296,32 +299,25 @@ def tile_list_msg_gelu_resL_kernel(
             nc.gpsimd.memset(pages[n][:], 0.0)
         late_page(2, "woven0")
         late_page(3, "rounded0")
-        acts = act_tile("act0")
-        acts = [gelu(acts, sums[0], 1, t) for t in range(PACK)]
-        turned_messages(0, hq, (0, 1))
-        sums.append(first_stage(1))
-        scaled = scaled_tile(1)
-        for t in range(PACK):
-            smooth(scaled, t, acts[t])
-        put(0, (0, 1), 2)
-        hq = weave_and_quantise(1, scaled, "both0", "h_plane0")
-        for n in range(1, TILES):
-            put(n, (0, 1), 2 + n % 2)
-        scaled = smooth_quarter(2, sums[1], "scaled1")
-        turned_messages(1, hq, (0, 1))
-        hq = weave_and_quantise(2, scaled, "upright1_0")
-        for n in range(TILES - 1):
-            put(n, (2, 3), 2 + n % 2)
-        scaled = smooth_quarter(3, sums[1], "h_plane0")
-        hq_last = weave_and_quantise(3, scaled, "upright1_2")
-        put(TILES - 1, (2, 3), 0, "scaled3")
-        turned_messages(2, hq, (3, 2))
-        for n in range(2):
-            put(n, (4, 5), 4 + n)
-        turned_messages(3, hq_last, (4, 5))
-        for n in range(2):
-            put(n, (6, 7), 6 + n)
-            store(n)
-        for n in range(2, TILES):
-            put(n, (4, 5, 6, 7), n - 1)
+        sums.append(None)
+        for g in range(4):
+            blocks = (2 * g, 2 * g + 1)
+            if g < 3:
+                acts = act_tile("act0")
+                acts = [gelu(acts, sums[(g + 1) // 2], g + 1, t) for t in range(PACK)]
+            turned_messages(g, hq, (0, 1))
+            if g == 0:
+                sums[1] = first_stage(1)
+            put(0, blocks, 2, upright_tile(QUARTER, "upright%d" % g)[:])
+            if g < 3:
+                scaled = scaled_tile(g + 1)
+                for t in range(PACK):
+                    smooth(scaled, t, acts[t])
+                hq = weave_and_quantise(g + 1, scaled, "h_codes%d" % g if g else "both0")
+            others = (1, 2, 3) if g < 2 else (1, 2)
+            upright = upright_tile(QUARTER * len(others), "h_plane%d" % g)
+            for n in others:
+                put(n, blocks, (3, 0, 1)[n - 1], upright[:, QUARTER * (n - 1) : QUARTER * n])
+        put(3, (4, 5, 6, 7), 1, upright_tile(HALF, "upright_last")[:])
+        for n in range(TILES):
             store(n)

@@ -44,7 +44,7 @@ def tile_list_msg_gelu_resL_kernel(
             return psum.tile([P, HALF], F32, name="bank%d" % index)
 
         lists = [sbuf.tile([P, J // 16], U16, name="list%d" % which) for which in (SOURCE, TARGET)]
-        table = sbuf.tile([P, T], I32, name="table", align_bytes=64)
+        table = laid.tile([P, T], I32, name="table", align_bytes=64, offset=0)
         table_scales = sbuf.tile([P, T], U8, name="table_scales", align_bytes=64)
         nc.vector.memset(table_scales[:].bitcast(I32), 0)
         nc.sync.dma_start(lists[SOURCE][:], offs)
@@ -91,13 +91,11 @@ def tile_list_msg_gelu_resL_kernel(
             pages[n] = sbuf.tile([P, T], F32, name=name, align_bytes=64)
             nc.gpsimd.memset(pages[n][:], 0.0)
 
-        def gather_words(h, name):
-            pair = sbuf.tile([P, 2 * HALF], U32, name=name, align_bytes=64)
+        def gather_words(which, h, name):
+            both = sbuf.tile([P, HALF], U32, name=name, align_bytes=64)
             cols = slice(HALF_COLS * h, HALF_COLS * (h + 1))
-            both = [pair[:, HALF * which : HALF * (which + 1)] for which in (SOURCE, TARGET)]
-            for which in (SOURCE, TARGET):
-                nc.vector.tensor_copy(out=both[which], in_=table[:].bitcast(U32).indirect(lists[which][:, cols]))
-            return both
+            nc.vector.tensor_copy(out=both[:], in_=table[:].bitcast(U32).indirect(lists[which][:, cols]))
+            return both[:]
 
         def part_words(both, name):
             parted = sbuf.tile([P, 8 * HALF], U8, name=name, align_bytes=64)
@@ -112,10 +110,7 @@ def tile_list_msg_gelu_resL_kernel(
             return result
 
         def quantise_weights(k):
-            if k < len(PASSES) - 1:
-                rounded = sbuf.tile([P, PACK * R], BF16, name="rounded%d" % k, align_bytes=64)
-            else:
-                rounded = laid.tile([P, PACK * R], BF16, name="rounded3", align_bytes=64, offset=3 * T)
+            rounded = sbuf.tile([P, PACK * R], BF16, name="rounded%d" % k, align_bytes=64)
             nc.scalar.copy(
                 out=rounded[:].rearrange("p (t m i) -> p m i t", t=PACK, i=PACK),
                 in_=raw[k][:].rearrange("p i (m t) -> p m i t", t=PACK),
@@ -136,14 +131,17 @@ def tile_list_msg_gelu_resL_kernel(
         weights = [quantise_weights(0)]
 
         def load_states(n, name):
-            state = sbuf.tile([P, T], F32, name=name, align_bytes=64)
+            if n:
+                state = sbuf.tile([P, T], F32, name=name, align_bytes=64)
+            else:
+                state = laid.tile([P, T], F32, name=name, align_bytes=64, offset=0)
             nc.sync.dma_start(out=state[:], in_=rT[P * n : P * (n + 1), :])
             return state
 
         states = {1: load_states(1, "rounded0")}
-        both = gather_words(0, "both0")
+        both = [gather_words(which, 0, "both%d" % which) for which in (SOURCE, TARGET)]
         v_words = [part_words(both, "parted")]
-        states[2] = load_states(2, "both0")
+        states[3] = load_states(3, "both0")
         weights.append(quantise_weights(1))
         wd_bytes = sbuf.tile([P, 3 * N], U8, name="rounded1", align_bytes=64)
         wd_codes, wd_plane = wd_bytes[:, : 2 * N], wd_bytes[:, 2 * N :]
@@ -154,12 +152,13 @@ def tile_list_msg_gelu_resL_kernel(
                 in_=rows.unsqueeze(0).to_broadcast([8, 4, N // 4]),
             )
         nc.sync.dma_start(out=wd_codes.bitcast(I32), in_=wd_words[0].bitcast(I32))
-        both = gather_words(1, "raw1")
+        both = [gather_words(SOURCE, 1, "raw1")]
         weights.append(quantise_weights(2))
-        v_words.append(part_words(both, "raw2"))
+        both.append(gather_words(TARGET, 1, "raw2"))
         weights.append(quantise_weights(3))
-        states[3] = load_states(3, "table")
-        states[0] = load_states(0, "rounded2")
+        v_words.append(part_words(both, "raw3"))
+        states[2] = load_states(2, "rounded2")
+        states[0] = load_states(0, "last_states")
 
         def first_stage(h):
             banks = [bank_tile(4 * h + t) for t in range(PACK)]
@@ -207,16 +206,18 @@ def tile_list_msg_gelu_resL_kernel(
             name = "h_plane%d" % (g - 1) if g else "scaled0"
             return sbuf.tile([P, PACK * QUARTER], BF16, name=name, align_bytes=64)
 
-        def weave_and_quantise(g, scaled, codes_name, woven_name=None):
-            woven = sbuf.tile([P, PACK * QUARTER], BF16, name=woven_name or "woven%d" % g, align_bytes=64)
+        def weave_and_quantise(g, scaled, codes):
+            woven = sbuf.tile([P, PACK * QUARTER], BF16, name="woven%d" % g, align_bytes=64)
             nc.scalar.copy(
                 out=woven[:].rearrange("p (c e t) -> p c t e", e=4, t=PACK),
                 in_=scaled[:].rearrange("p (t c e) -> p c t e", t=PACK, e=4),
             )
-            codes = sbuf.tile([P, QUARTER], U32, name=codes_name, align_bytes=64)
             plane = sbuf.tile([P, QUARTER], U8, name="h_plane%d" % g, align_bytes=64)
-            nc.vector.quantize_mx(out=codes[:].bitcast(FP8X4), scales=plane[:], in_=woven[:])
+            nc.vector.quantize_mx(out=codes.bitcast(FP8X4), scales=plane[:], in_=woven[:])
             return codes, plane
+
+        def codes_tile(g):
+            return sbuf.tile([P, QUARTER], U32, name="h_codes%d" % g, align_bytes=64)[:]
 
         def gather_states(n, j0, j1):
             nc.vector.tensor_tensor(
@@ -270,40 +271,33 @@ def tile_list_msg_gelu_resL_kernel(
                 for queue, cols in ((nc.sync, slice(0, T // 2)), (nc.scalar, slice(T // 2, T))):
                     queue.dma_start(out=out[P * n : P * (n + 1), cols], in_=pages[n][:, cols])
 
-        later, first = {}, {}
+        weighted_states = {}
 
         def weighted(n, j0, j1):
-            if j0 < QUARTER:
-                return first[n][:, j0:j1]
-            return later[n][:, j0 - QUARTER : j1 - QUARTER]
+            return weighted_states[n][:, j0:j1]
 
-        rest = J - QUARTER
-        for n in (1, 2):
-            later[n] = sbuf.tile([P, rest], F32, name="weighted%d" % n, align_bytes=64)[:]
-            gather_states(n, QUARTER, J)
-        whole = sbuf.tile([P, J], F32, name="weighted3", align_bytes=64)
-        first[3], later[3] = whole[:, :QUARTER], whole[:, QUARTER:]
-        nc.vector.tensor_tensor(whole[:], states[3][:].indirect(lists[TARGET][:]), edge_w[:], ALU.mult)
+        for n in (1, 3):
+            weighted_states[n] = sbuf.tile([P, J], F32, name="weighted%d" % n, align_bytes=64)[:]
+            gather_states(n, 0, J)
         sums = [first_stage(0)]
         scaled = smooth_quarter(0, sums[0], "act0")
-        hq = weave_and_quantise(0, scaled, "table")
-        whole = sbuf.tile([P, J], F32, name="scaled0", align_bytes=64)
-        first[0], later[0] = whole[:, :QUARTER], whole[:, QUARTER:]
-        nc.vector.tensor_tensor(whole[:], states[0][:].indirect(lists[TARGET][:]), edge_w[:], ALU.mult)
-        firsts = sbuf.tile([P, HALF], F32, name="rounded2", align_bytes=64)
-        for n in (1, 2):
-            first[n] = firsts[:, QUARTER * (n - 1) : QUARTER * n]
-            gather_states(n, 0, QUARTER)
-        for n in range(2):
-            pages[n] = laid.tile([P, T], F32, name="page%d" % n, align_bytes=64, offset=4 * T * n)
-            nc.gpsimd.memset(pages[n][:], 0.0)
+        hq = weave_and_quantise(0, scaled, codes_tile(0))
+        held = sbuf.tile([P, 2 * J], F32, name="scaled0", align_bytes=64)
+        weighted_states[2], weighted_states[0] = held[:, :J], held[:, J:]
+        gather_states(2, 0, J)
+        gather_states(0, 0, HALF)
+        gather_states(0, HALF, J)
+        late_page(0, "raw1")
+        late_page(1, "raw2")
         late_page(2, "woven0")
-        late_page(3, "rounded0")
+        late_page(3, "rounded2")
         sums.append(None)
+        after_codes = laid.tile([P, QUARTER], U32, name="after_codes", align_bytes=64, offset=0)
+        after = laid.tile([P, T - QUARTER], F32, name="after", align_bytes=64, offset=4 * QUARTER)
         for g in range(4):
             blocks = (2 * g, 2 * g + 1)
             if g < 3:
-                acts = act_tile("act0")
+                acts = after[:, J - QUARTER :] if g == 1 else act_tile("act0")
                 acts = [gelu(acts, sums[(g + 1) // 2], g + 1, t) for t in range(PACK)]
             turned_messages(g, hq, (0, 1))
             if g == 0:
@@ -313,9 +307,9 @@ def tile_list_msg_gelu_resL_kernel(
                 scaled = scaled_tile(g + 1)
                 for t in range(PACK):
                     smooth(scaled, t, acts[t])
-                hq = weave_and_quantise(g + 1, scaled, "h_codes%d" % g if g else "both0")
+                hq = weave_and_quantise(g + 1, scaled, codes_tile(g + 1) if g else after_codes[:])
             others = (1, 2, 3) if g < 2 else (1, 2)
-            upright = upright_tile(QUARTER * len(others), "h_plane%d" % g)
+            upright = upright_tile(QUARTER * len(others), "h_plane%d" % g) if g else after[:, : J - QUARTER]
             for n in others:
                 put(n, blocks, (3, 0, 1)[n - 1], upright[:, QUARTER * (n - 1) : QUARTER * n])
         put(3, (4, 5, 6, 7), 1, upright_tile(HALF, "upright_last")[:])

@@ -44,16 +44,17 @@ def tile_list_msg_gelu_resL_kernel(
             return psum.tile([P, HALF], F32, name="bank%d" % index)
 
         lists = [sbuf.tile([P, J // 16], U16, name="list%d" % which) for which in (SOURCE, TARGET)]
-        table = laid.tile([P, T], I32, name="table", align_bytes=64, offset=0)
+        table = sbuf.tile([P, T], I32, name="table", align_bytes=64)
         table_scales = sbuf.tile([P, T], U8, name="table_scales", align_bytes=64)
         nc.vector.memset(table_scales[:].bitcast(I32), 0)
         nc.sync.dma_start(lists[SOURCE][:], offs)
         w_rows = sbuf.tile([P, P], F32, name="w_rows")
         nc.sync.dma_start(out=w_rows[:], in_=wgo.rearrange("r (b c) -> (r b) c", c=P)[:P, :])
+        table_rows = tab_words[0].rearrange("p t b -> p (t b)").bitcast(I32)
+        nc.sync.dma_start(out=table[:, : T // 4], in_=table_rows[:, : T // 4])
         scale_rows = tab_scales.rearrange("d (q s) t -> s q d t", s=4)
         for s in range(4):
             nc.sync.dma_start(out=table_scales[s:P:LIFT, :].bitcast(I32), in_=scale_rows[s].bitcast(I32))
-        nc.sync.dma_start(lists[TARGET][:], offs2)
 
         def load_weights(k):
             which, d = PASSES[k]
@@ -63,7 +64,8 @@ def tile_list_msg_gelu_resL_kernel(
             return piece
 
         raw = [load_weights(0)]
-        nc.sync.dma_start(out=table[:], in_=tab_words[0].rearrange("p t b -> p (t b)").bitcast(I32))
+        nc.sync.dma_start(lists[TARGET][:], offs2)
+        nc.sync.dma_start(out=table[:, T // 4 :], in_=table_rows[:, T // 4 :])
         raw.extend(load_weights(k) for k in range(1, len(PASSES)))
         sm_cols = sbuf.tile([P, PACK], F32, name="sm_cols")
         nc.sync.dma_start(out=sm_cols[:], in_=sm.rearrange("(p i) -> p i", i=PACK))
@@ -91,11 +93,13 @@ def tile_list_msg_gelu_resL_kernel(
             pages[n] = sbuf.tile([P, T], F32, name=name, align_bytes=64)
             nc.gpsimd.memset(pages[n][:], 0.0)
 
-        def gather_words(which, h, name):
-            both = sbuf.tile([P, HALF], U32, name=name, align_bytes=64)
+        def gather_words(h, name):
+            pair = sbuf.tile([P, 2 * HALF], U32, name=name, align_bytes=64)
             cols = slice(HALF_COLS * h, HALF_COLS * (h + 1))
-            nc.vector.tensor_copy(out=both[:], in_=table[:].bitcast(U32).indirect(lists[which][:, cols]))
-            return both[:]
+            both = [pair[:, HALF * which : HALF * (which + 1)] for which in (SOURCE, TARGET)]
+            for which in (SOURCE, TARGET):
+                nc.vector.tensor_copy(out=both[which], in_=table[:].bitcast(U32).indirect(lists[which][:, cols]))
+            return both
 
         def part_words(both, name):
             parted = sbuf.tile([P, 8 * HALF], U8, name=name, align_bytes=64)
@@ -110,7 +114,10 @@ def tile_list_msg_gelu_resL_kernel(
             return result
 
         def quantise_weights(k):
-            rounded = sbuf.tile([P, PACK * R], BF16, name="rounded%d" % k, align_bytes=64)
+            if k < 2:
+                rounded = sbuf.tile([P, PACK * R], BF16, name="rounded%d" % k, align_bytes=64)
+            else:
+                rounded = laid.tile([P, PACK * R], BF16, name="rounded%d" % k, align_bytes=64, offset=7 * T * (k - 2))
             nc.scalar.copy(
                 out=rounded[:].rearrange("p (t m i) -> p m i t", t=PACK, i=PACK),
                 in_=raw[k][:].rearrange("p i (m t) -> p m i t", t=PACK),
@@ -139,7 +146,7 @@ def tile_list_msg_gelu_resL_kernel(
             return state
 
         states = {1: load_states(1, "rounded0")}
-        both = [gather_words(which, 0, "both%d" % which) for which in (SOURCE, TARGET)]
+        both = gather_words(0, "both0")
         v_words = [part_words(both, "parted")]
         states[3] = load_states(3, "both0")
         weights.append(quantise_weights(1))
@@ -152,12 +159,11 @@ def tile_list_msg_gelu_resL_kernel(
                 in_=rows.unsqueeze(0).to_broadcast([8, 4, N // 4]),
             )
         nc.sync.dma_start(out=wd_codes.bitcast(I32), in_=wd_words[0].bitcast(I32))
-        both = [gather_words(SOURCE, 1, "raw1")]
+        both = gather_words(1, "raw1")
         weights.append(quantise_weights(2))
-        both.append(gather_words(TARGET, 1, "raw2"))
+        v_words.append(part_words(both, "raw2"))
         weights.append(quantise_weights(3))
-        v_words.append(part_words(both, "raw3"))
-        states[2] = load_states(2, "rounded2")
+        states[2] = load_states(2, "table")
         states[0] = load_states(0, "last_states")
 
         def first_stage(h):
@@ -287,10 +293,11 @@ def tile_list_msg_gelu_resL_kernel(
         gather_states(2, 0, J)
         gather_states(0, 0, HALF)
         gather_states(0, HALF, J)
-        late_page(0, "raw1")
-        late_page(1, "raw2")
+        for n in range(2):
+            pages[n] = laid.tile([P, T], F32, name="page%d" % n, align_bytes=64, offset=4 * T * (n + 1))
+            nc.gpsimd.memset(pages[n][:], 0.0)
         late_page(2, "woven0")
-        late_page(3, "rounded2")
+        late_page(3, "table")
         sums.append(None)
         after_codes = laid.tile([P, QUARTER], U32, name="after_codes", align_bytes=64, offset=0)
         after = laid.tile([P, T - QUARTER], F32, name="after", align_bytes=64, offset=4 * QUARTER)

@@ -54,7 +54,7 @@ def tile_list_msg_gelu_resL_kernel(
         nc.sync.dma_start(out=table[:, : T // 4], in_=table_rows[:, : T // 4])
         scale_rows = tab_scales.rearrange("d (q s) t -> s q d t", s=4)
         for s in range(4):
-            nc.sync.dma_start(out=table_scales[s:P:LIFT, :].bitcast(I32), in_=scale_rows[s].bitcast(I32))
+            (nc.sync, nc.scalar)[s % 2].dma_start(out=table_scales[s:P:LIFT, :].bitcast(I32), in_=scale_rows[s].bitcast(I32))
 
         def load_weights(k):
             which, d = PASSES[k]
@@ -166,12 +166,12 @@ def tile_list_msg_gelu_resL_kernel(
         states[2] = load_states(2, "table")
         states[0] = load_states(0, "last_states")
 
-        def first_stage(h):
-            banks = [bank_tile(4 * h + t) for t in range(PACK)]
+        def first_stage(h, placed):
+            banks = {t: bank_tile(index) for t, index in placed}
             if h == 0:
-                order = [(k, t) for k in range(len(PASSES)) for t in range(PACK)]
+                order = [(k, t) for k in range(len(PASSES)) for t in banks]
             else:
-                order = [(k, t) for t in range(PACK) for k in reversed(range(len(PASSES)))]
+                order = [(k, t) for t in banks for k in reversed(range(len(PASSES)))]
             for k, t in order:
                 which, d = PASSES[k]
                 codes, plane = weights[k]
@@ -209,7 +209,7 @@ def tile_list_msg_gelu_resL_kernel(
             )
 
         def scaled_tile(g):
-            name = "h_plane%d" % (g - 1) if g else "scaled0"
+            name = ("scaled0", "message0", "h_plane1", "h_plane2")[g]
             return sbuf.tile([P, PACK * QUARTER], BF16, name=name, align_bytes=64)
 
         def weave_and_quantise(g, scaled, codes):
@@ -236,6 +236,7 @@ def tile_list_msg_gelu_resL_kernel(
         messages = {}
 
         def turned_messages(g, hq, banks):
+            products = []
             for b in range(2):
                 bank = bank_tile(banks[b])
                 nc.tensor.matmul_mx(
@@ -247,11 +248,17 @@ def tile_list_msg_gelu_resL_kernel(
                     start=True,
                     stop=True,
                 )
-                block = 2 * g + b
-                messages[block] = sbuf.tile([P, N], F32, name="message%d" % block, align_bytes=64)
-                nc.scalar.activation(
-                    out=messages[block][:], in_=bank[:], func=ACT.Copy, scale=w_cols[:, block : block + 1]
-                )
+                products.append(bank)
+                messages[2 * g + b] = sbuf.tile([P, N], F32, name="message%d" % (2 * g + b), align_bytes=64)
+            for cols in (slice(0, P), slice(P, N)):
+                for b in range(2):
+                    block = 2 * g + b
+                    nc.scalar.activation(
+                        out=messages[block][:, cols],
+                        in_=products[b][:, cols],
+                        func=ACT.Copy,
+                        scale=w_cols[:, block : block + 1],
+                    )
 
         def put(n, blocks, bank_index, upright):
             width = P * len(blocks)
@@ -285,7 +292,7 @@ def tile_list_msg_gelu_resL_kernel(
         for n in (1, 3):
             weighted_states[n] = sbuf.tile([P, J], F32, name="weighted%d" % n, align_bytes=64)[:]
             gather_states(n, 0, J)
-        sums = [first_stage(0)]
+        sums = [first_stage(0, [(t, t) for t in range(PACK)])]
         scaled = smooth_quarter(0, sums[0], "act0")
         hq = weave_and_quantise(0, scaled, codes_tile(0))
         held = sbuf.tile([P, 2 * J], F32, name="scaled0", align_bytes=64)
@@ -308,8 +315,10 @@ def tile_list_msg_gelu_resL_kernel(
                 acts = [gelu(acts, sums[(g + 1) // 2], g + 1, t) for t in range(PACK)]
             turned_messages(g, hq, (0, 1))
             if g == 0:
-                sums[1] = first_stage(1)
-            put(0, blocks, 2, upright_tile(QUARTER, "upright%d" % g)[:])
+                sums[1] = first_stage(1, [(0, 4), (1, 5)])
+            put(0, blocks, 6 if g else 2, upright_tile(QUARTER, "upright%d" % g)[:])
+            if g == 0:
+                sums[1][2] = first_stage(1, [(2, 2)])[2]
             if g < 3:
                 scaled = scaled_tile(g + 1)
                 for t in range(PACK):
@@ -318,7 +327,9 @@ def tile_list_msg_gelu_resL_kernel(
             others = (1, 2, 3) if g < 2 else (1, 2)
             upright = upright_tile(QUARTER * len(others), "h_plane%d" % g) if g else after[:, : J - QUARTER]
             for n in others:
-                put(n, blocks, (3, 0, 1)[n - 1], upright[:, QUARTER * (n - 1) : QUARTER * n])
+                put(n, blocks, (7 if g else 3, 0, 1)[n - 1], upright[:, QUARTER * (n - 1) : QUARTER * n])
+            if g == 0:
+                sums[1][3] = first_stage(1, [(3, 3)])[3]
         put(3, (4, 5, 6, 7), 1, upright_tile(HALF, "upright_last")[:])
         for n in range(TILES):
             store(n)

@@ -54,7 +54,7 @@ def tile_list_msg_gelu_resL_kernel(
         nc.sync.dma_start(out=table[:, : T // 4], in_=table_rows[:, : T // 4])
         scale_rows = tab_scales.rearrange("d (q s) t -> s q d t", s=4)
         for s in range(4):
-            (nc.sync, nc.scalar)[s % 2].dma_start(out=table_scales[s:P:LIFT, :].bitcast(I32), in_=scale_rows[s].bitcast(I32))
+            nc.sync.dma_start(out=table_scales[s:P:LIFT, :].bitcast(I32), in_=scale_rows[s].bitcast(I32))
 
         def load_weights(k):
             which, d = PASSES[k]
@@ -315,10 +315,10 @@ def tile_list_msg_gelu_resL_kernel(
                 acts = [gelu(acts, sums[(g + 1) // 2], g + 1, t) for t in range(PACK)]
             turned_messages(g, hq, (0, 1))
             if g == 0:
-                sums[1] = first_stage(1, [(0, 4), (1, 5)])
-            put(0, blocks, 6 if g else 2, upright_tile(QUARTER, "upright%d" % g)[:])
+                sums[1] = first_stage(1, [(0, 4), (1, 5), (2, 6)])
+            put(0, blocks, 7 if g else 2, upright_tile(QUARTER, "upright%d" % g)[:])
             if g == 0:
-                sums[1][2] = first_stage(1, [(2, 2)])[2]
+                sums[1][3] = first_stage(1, [(3, 2)])[3]
             if g < 3:
                 scaled = scaled_tile(g + 1)
                 for t in range(PACK):
@@ -327,9 +327,7 @@ def tile_list_msg_gelu_resL_kernel(
             others = (1, 2, 3) if g < 2 else (1, 2)
             upright = upright_tile(QUARTER * len(others), "h_plane%d" % g) if g else after[:, : J - QUARTER]
             for n in others:
-                put(n, blocks, (7 if g else 3, 0, 1)[n - 1], upright[:, QUARTER * (n - 1) : QUARTER * n])
-            if g == 0:
-                sums[1][3] = first_stage(1, [(3, 3)])[3]
+                put(n, blocks, (3, 0, 1)[n - 1], upright[:, QUARTER * (n - 1) : QUARTER * n])
         put(3, (4, 5, 6, 7), 1, upright_tile(HALF, "upright_last")[:])
         for n in range(TILES):
             store(n)

@@ -119,8 +119,8 @@ def tile_list_msg_gelu_resL_kernel(
             else:
                 rounded = laid.tile([P, PACK * R], BF16, name="rounded%d" % k, align_bytes=64, offset=7 * T * (k - 2))
             nc.scalar.copy(
-                out=rounded[:].rearrange("p (t m i) -> p m i t", t=PACK, i=PACK),
-                in_=raw[k][:].rearrange("p i (m t) -> p m i t", t=PACK),
+                out=rounded[:].rearrange("p (t m u e) -> p m u t e", t=PACK, u=2, e=2),
+                in_=raw[k][:].rearrange("p (u e) (m t) -> p m u t e", t=PACK, e=2),
             )
             codes = sbuf.tile([P, R], U32, name="w_codes%d" % k, align_bytes=64)
             plane = sbuf.tile([P, R], U8, name="w_plane%d" % k, align_bytes=64)

@@ -24,7 +24,7 @@ HALF = J // 2
 HALF_COLS = HALF // 16
 TILES = N // P
 BLOCKS = HALF // P
-LIFT = 16
+COMPACT = P - 32
 SOURCE, TARGET = 0, 1
 PASSES = ((SOURCE, 0), (TARGET, 0), (SOURCE, 1), (TARGET, 1))
 
@@ -45,16 +45,16 @@ def tile_list_msg_gelu_resL_kernel(
 
         lists = [sbuf.tile([P, J // 16], U16, name="list%d" % which) for which in (SOURCE, TARGET)]
         table = sbuf.tile([P, T], I32, name="table", align_bytes=64)
-        table_scales = sbuf.tile([P, T], U8, name="table_scales", align_bytes=64)
-        nc.vector.memset(table_scales[:].bitcast(I32), 0)
+        table_scales = sbuf.tile([P, T], U8, name="raw3", align_bytes=64)
+        nc.sync.dma_start(
+            out=table_scales[COMPACT:, :].bitcast(I32),
+            in_=tab_scales.rearrange("d q t -> (d q) t").bitcast(I32),
+        )
+        nc.vector.memset(table_scales[:COMPACT, :].bitcast(I32), 0)
         nc.sync.dma_start(lists[SOURCE][:], offs)
+        nc.sync.dma_start(lists[TARGET][:], offs2)
         w_rows = sbuf.tile([P, P], F32, name="w_rows")
         nc.sync.dma_start(out=w_rows[:], in_=wgo.rearrange("r (b c) -> (r b) c", c=P)[:P, :])
-        table_rows = tab_words[0].rearrange("p t b -> p (t b)").bitcast(I32)
-        nc.sync.dma_start(out=table[:, : T // 4], in_=table_rows[:, : T // 4])
-        scale_rows = tab_scales.rearrange("d (q s) t -> s q d t", s=4)
-        for s in range(4):
-            nc.sync.dma_start(out=table_scales[s:P:LIFT, :].bitcast(I32), in_=scale_rows[s].bitcast(I32))
 
         def load_weights(k):
             which, d = PASSES[k]
@@ -64,14 +64,13 @@ def tile_list_msg_gelu_resL_kernel(
             return piece
 
         raw = [load_weights(0)]
-        nc.sync.dma_start(lists[TARGET][:], offs2)
-        nc.sync.dma_start(out=table[:, T // 4 :], in_=table_rows[:, T // 4 :])
-        raw.extend(load_weights(k) for k in range(1, len(PASSES)))
+        nc.sync.dma_start(out=table[:], in_=tab_words[0].rearrange("p t b -> p (t b)").bitcast(I32))
+        raw.extend(load_weights(k) for k in (1, 2))
         sm_cols = sbuf.tile([P, PACK], F32, name="sm_cols")
         nc.sync.dma_start(out=sm_cols[:], in_=sm.rearrange("(p i) -> p i", i=PACK))
 
-        lifted = sbuf.tile([P, 2 * J], U8, name="lifted", align_bytes=64)
-        nc.vector.memset(lifted[:].bitcast(I32), 0)
+        planes = sbuf.tile([P, 4 * J], U8, name="planes", align_bytes=64)
+        nc.vector.memset(planes[:].bitcast(I32), 0)
         ident = sbuf.tile([P, P], F32, name="ident")
         make_identity(nc, ident[:])
         bank = bank_tile(4)
@@ -132,8 +131,19 @@ def tile_list_msg_gelu_resL_kernel(
             nc.vector.tensor_copy(
                 out=gathered[:, J * which : J * (which + 1)], in_=table_scales[:].indirect(lists[which][:])
             )
-        nc.sync.dma_start(out=lifted[: P - LIFT, :].bitcast(I32), in_=gathered[LIFT:, :].bitcast(I32))
-        v_planes = (gathered, lifted)
+
+        def spread_scales(d):
+            for q in range(4):
+                first = COMPACT + 16 * d + 4 * q
+                nc.sync.dma_start(
+                    out=planes[32 * q : 32 * q + 4, 2 * J * d : 2 * J * (d + 1)].bitcast(I32),
+                    in_=gathered[first : first + 4, :].bitcast(I32),
+                )
+
+        spread_scales(0)
+        raw.append(load_weights(3))
+        spread_scales(1)
+        v_planes = (planes[:, : 2 * J], planes[:, 2 * J :])
 
         weights = [quantise_weights(0)]
 

@@ -176,25 +176,41 @@ def tile_list_msg_gelu_resL_kernel(
         states[2] = load_states(2, "table")
         states[0] = load_states(0, "last_states")
 
-        def first_stage(h, placed):
-            banks = {t: bank_tile(index) for t, index in placed}
-            if h == 0:
-                order = [(k, t) for k in range(len(PASSES)) for t in banks]
-            else:
-                order = [(k, t) for t in banks for k in reversed(range(len(PASSES)))]
-            for k, t in order:
-                which, d = PASSES[k]
-                codes, plane = weights[k]
-                nc.tensor.matmul_mx(
-                    out=banks[t][:],
-                    lhsT=codes[:, P * t : P * (t + 1)].bitcast(FP8X4),
-                    lhsT_scale=plane[:, P * t : P * (t + 1)],
-                    rhs=v_words[h][which][:, 2 * HALF * d : 2 * HALF * (d + 1)].bitcast(FP4X4),
-                    rhs_scale=v_planes[d][:, J * which + HALF * h : J * which + HALF * (h + 1)],
-                    start=(k == order[0][0]),
-                    stop=(k == order[-1][0]),
-                )
-            return banks
+        def first_pass(k, t, j0, j1, sums, start, stop):
+            which, d = PASSES[k]
+            codes, plane = weights[k]
+            c0 = 2 * HALF * d + 2 * (j0 % HALF)
+            nc.tensor.matmul_mx(
+                out=sums,
+                lhsT=codes[:, P * t : P * (t + 1)].bitcast(FP8X4),
+                lhsT_scale=plane[:, P * t : P * (t + 1)],
+                rhs=v_words[j0 // HALF][which][:, c0 : c0 + 2 * (j1 - j0)].bitcast(FP4X4),
+                rhs_scale=v_planes[d][:, J * which + j0 : J * which + j1],
+                start=start,
+                stop=stop,
+            )
+
+        def early_sums():
+            banks = [bank_tile(index) for index in range(4)]
+            sums = {}
+            for k in range(len(PASSES)):
+                for g in range(2):
+                    for t in range(PACK):
+                        sums[g, t] = banks[2 * g + t // 2][:, QUARTER * (t % 2) : QUARTER * (t % 2 + 1)]
+                        start = k == 0 and t % 2 == 0
+                        stop = k == len(PASSES) - 1 and t % 2 == 1
+                        first_pass(k, t, QUARTER * g, QUARTER * (g + 1), sums[g, t], start, stop)
+            return sums
+
+        def late_sums(placed):
+            sums = {}
+            for t, index in placed:
+                bank = bank_tile(index)
+                for k in reversed(range(len(PASSES))):
+                    first_pass(k, t, HALF, J, bank[:], k == len(PASSES) - 1, k == 0)
+                for g in (2, 3):
+                    sums[g, t] = bank[:, QUARTER * (g - 2) : QUARTER * (g - 1)]
+            return sums
 
         def act_tile(name):
             return sbuf.tile([P, PACK * QUARTER], F32, name=name, align_bytes=64)
@@ -209,8 +225,7 @@ def tile_list_msg_gelu_resL_kernel(
 
         def gelu(acts, banks, g, t):
             act = acts[:, QUARTER * t : QUARTER * (t + 1)]
-            c0 = QUARTER * (g % 2)
-            nc.scalar.activation(out=act, in_=banks[t][:, c0 : c0 + QUARTER], func=ACT.Gelu_apprx_tanh)
+            nc.scalar.activation(out=act, in_=banks[g, t], func=ACT.Gelu_apprx_tanh)
             return act
 
         def smooth(scaled, t, act):
@@ -302,8 +317,8 @@ def tile_list_msg_gelu_resL_kernel(
         for n in (1, 3):
             weighted_states[n] = sbuf.tile([P, J], F32, name="weighted%d" % n, align_bytes=64)[:]
             gather_states(n, 0, J)
-        sums = [first_stage(0, [(t, t) for t in range(PACK)])]
-        scaled = smooth_quarter(0, sums[0], "act0")
+        sums = early_sums()
+        scaled = smooth_quarter(0, sums, "act0")
         hq = weave_and_quantise(0, scaled, codes_tile(0))
         held = sbuf.tile([P, 2 * J], F32, name="scaled0", align_bytes=64)
         weighted_states[2], weighted_states[0] = held[:, :J], held[:, J:]
@@ -315,20 +330,19 @@ def tile_list_msg_gelu_resL_kernel(
             nc.gpsimd.memset(pages[n][:], 0.0)
         late_page(2, "woven0")
         late_page(3, "table")
-        sums.append(None)
         after_codes = laid.tile([P, QUARTER], U32, name="after_codes", align_bytes=64, offset=0)
         after = laid.tile([P, T - QUARTER], F32, name="after", align_bytes=64, offset=4 * QUARTER)
         for g in range(4):
             blocks = (2 * g, 2 * g + 1)
             if g < 3:
                 acts = after[:, J - QUARTER :] if g == 1 else act_tile("act0")
-                acts = [gelu(acts, sums[(g + 1) // 2], g + 1, t) for t in range(PACK)]
+                acts = [gelu(acts, sums, g + 1, t) for t in range(PACK)]
             turned_messages(g, hq, (0, 1))
             if g == 0:
-                sums[1] = first_stage(1, [(0, 4), (1, 5), (2, 6)])
+                sums.update(late_sums([(0, 4), (1, 5), (2, 6)]))
             put(0, blocks, 7 if g else 2, upright_tile(QUARTER, "upright%d" % g)[:])
             if g == 0:
-                sums[1][3] = first_stage(1, [(3, 2)])[3]
+                sums.update(late_sums([(3, 2)]))
             if g < 3:
                 scaled = scaled_tile(g + 1)
                 for t in range(PACK):

@@ -285,6 +285,30 @@ def tile_list_msg_gelu_resL_kernel(
                         scale=w_cols[:, block : block + 1],
                     )
 
+        def pair_messages(g, hq, i, bank_index):
+            bank = bank_tile(bank_index)
+            cols = slice(QUARTER * i, QUARTER * (i + 1))
+            for b in range(2):
+                nc.tensor.matmul_mx(
+                    out=bank[:, QUARTER * b : QUARTER * (b + 1)],
+                    lhsT=hq[0][:, P * b : P * (b + 1)].bitcast(FP8X4),
+                    lhsT_scale=hq[1][:, P * b : P * (b + 1)],
+                    rhs=wd_codes[:, 2 * cols.start : 2 * cols.stop].bitcast(FP4X4),
+                    rhs_scale=wd_plane[:, cols],
+                    start=True,
+                    stop=True,
+                )
+                if i == 0:
+                    messages[2 * g + b] = sbuf.tile([P, N], F32, name="message%d" % (2 * g + b), align_bytes=64)
+            for b in range(2):
+                block = 2 * g + b
+                nc.scalar.activation(
+                    out=messages[block][:, cols],
+                    in_=bank[:, QUARTER * b : QUARTER * (b + 1)],
+                    func=ACT.Copy,
+                    scale=w_cols[:, block : block + 1],
+                )
+
         def put(n, blocks, bank_index, upright):
             width = P * len(blocks)
             bank = bank_tile(bank_index)
@@ -337,7 +361,10 @@ def tile_list_msg_gelu_resL_kernel(
             if g < 3:
                 acts = after[:, J - QUARTER :] if g == 1 else act_tile("act0")
                 acts = [gelu(acts, sums, g + 1, t) for t in range(PACK)]
-            turned_messages(g, hq, (0, 1))
+            if g < 3:
+                turned_messages(g, hq, (0, 1))
+            else:
+                pair_messages(g, hq, 0, 0)
             if g == 0:
                 sums.update(late_sums([(0, 4), (1, 5), (2, 6)]))
             put(0, blocks, 7 if g else 2, upright_tile(QUARTER, "upright%d" % g)[:])
@@ -348,10 +375,14 @@ def tile_list_msg_gelu_resL_kernel(
                 for t in range(PACK):
                     smooth(scaled, t, acts[t])
                 hq = weave_and_quantise(g + 1, scaled, codes_tile(g + 1) if g else after_codes[:])
-            others = (1, 2, 3) if g < 2 else (1, 2)
-            upright = upright_tile(QUARTER * len(others), "h_plane%d" % g) if g else after[:, : J - QUARTER]
-            for n in others:
-                put(n, blocks, (3, 0, 1)[n - 1], upright[:, QUARTER * (n - 1) : QUARTER * n])
+            if g < 3:
+                others = (1, 2, 3) if g < 2 else (1, 2)
+                upright = upright_tile(QUARTER * len(others), "h_plane%d" % g) if g else after[:, : J - QUARTER]
+                for n in others:
+                    put(n, blocks, (3, 0, 1)[n - 1], upright[:, QUARTER * (n - 1) : QUARTER * n])
+        put(1, (6, 7), 3, upright_tile(QUARTER, "upright_last1")[:])
+        pair_messages(3, hq, 1, 7)
+        put(2, (6, 7), 2, upright_tile(QUARTER, "upright_last2")[:])
         put(3, (4, 5, 6, 7), 1, upright_tile(HALF, "upright_last")[:])
         for n in range(TILES):
             store(n)

@@ -20,15 +20,14 @@ ALU = mybir.AluOpType
 P = 128
 PACK = 4
 K_PASS = P * PACK
+BANK = 512
 HALF = J // 2
-HALF_COLS = HALF // 16
+QUARTER = J // 4
 TILES = N // P
-BLOCKS = HALF // P
 COMPACT = P - 32
 SOURCE, TARGET = 0, 1
 PASSES = ((SOURCE, 0), (TARGET, 0), (SOURCE, 1), (TARGET, 1))
-
-QUARTER = HALF // 2
+PAGE = 4 * T
 
 
 def tile_list_msg_gelu_resL_kernel(
@@ -41,11 +40,14 @@ def tile_list_msg_gelu_resL_kernel(
         psum = ctx.enter_context(tc.psum_pool(name="psum", bufs=1))
 
         def bank_tile(index):
-            return psum.tile([P, HALF], F32, name="bank%d" % index)
+            return psum.tile([P, BANK], F32, name="bank%d" % index)
+
+        def tile(width, dtype, name):
+            return sbuf.tile([P, width], dtype, name=name, align_bytes=64)
 
         lists = [sbuf.tile([P, J // 16], U16, name="list%d" % which) for which in (SOURCE, TARGET)]
-        table = sbuf.tile([P, T], I32, name="table", align_bytes=64)
-        table_scales = sbuf.tile([P, T], U8, name="raw3", align_bytes=64)
+        table = tile(T, I32, "table")
+        table_scales = tile(T, U8, "table_scales")
         nc.sync.dma_start(
             out=table_scales[COMPACT:, :].bitcast(I32),
             in_=tab_scales.rearrange("d q t -> (d q) t").bitcast(I32),
@@ -65,11 +67,9 @@ def tile_list_msg_gelu_resL_kernel(
 
         raw = [load_weights(0)]
         nc.sync.dma_start(out=table[:], in_=tab_words[0].rearrange("p t b -> p (t b)").bitcast(I32))
-        raw.extend(load_weights(k) for k in (1, 2))
-        sm_cols = sbuf.tile([P, PACK], F32, name="sm_cols")
-        nc.sync.dma_start(out=sm_cols[:], in_=sm.rearrange("(p i) -> p i", i=PACK))
+        raw.extend(load_weights(k) for k in (1, 2, 3))
 
-        planes = sbuf.tile([P, 4 * J], U8, name="planes", align_bytes=64)
+        planes = tile(4 * J, U8, "planes")
         nc.vector.memset(planes[:].bitcast(I32), 0)
         ident = sbuf.tile([P, P], F32, name="ident")
         make_identity(nc, ident[:])
@@ -77,56 +77,20 @@ def tile_list_msg_gelu_resL_kernel(
         nc.tensor.transpose(bank[:, :P], w_rows[:], ident[:])
         w_cols = sbuf.tile([P, J // P], F32, name="w_cols")
         nc.scalar.copy(out=w_cols[:], in_=bank[:, : J // P])
-        edge_w = sbuf.tile([P, J], F32, name="edge_w", align_bytes=64)
+        edge_w = tile(J, F32, "edge_w")
         for h in range(2):
             bank = bank_tile(5 + h)
-            for b in range(BLOCKS):
-                block = BLOCKS * h + b
+            for b in range(HALF // P):
+                block = HALF // P * h + b
                 nc.tensor.transpose(
                     bank[:, P * b : P * (b + 1)], w_cols[:, block : block + 1].to_broadcast([P, P]), ident[:]
                 )
             nc.scalar.copy(out=edge_w[:, HALF * h : HALF * (h + 1)], in_=bank[:])
-        pages = {}
+            if h == 0:
+                lead_w = tile(QUARTER, F32, "lead_w")
+                nc.scalar.copy(out=lead_w[:], in_=bank[:, :QUARTER])
 
-        def late_page(n, name):
-            pages[n] = sbuf.tile([P, T], F32, name=name, align_bytes=64)
-            nc.gpsimd.memset(pages[n][:], 0.0)
-
-        def gather_words(h, name):
-            pair = sbuf.tile([P, 2 * HALF], U32, name=name, align_bytes=64)
-            cols = slice(HALF_COLS * h, HALF_COLS * (h + 1))
-            both = [pair[:, HALF * which : HALF * (which + 1)] for which in (SOURCE, TARGET)]
-            for which in (SOURCE, TARGET):
-                nc.vector.tensor_copy(out=both[which], in_=table[:].bitcast(U32).indirect(lists[which][:, cols]))
-            return both
-
-        def part_words(both, name):
-            parted = sbuf.tile([P, 8 * HALF], U8, name=name, align_bytes=64)
-            result = []
-            for which in (SOURCE, TARGET):
-                own = parted[:, 4 * HALF * which : 4 * HALF * (which + 1)]
-                nc.vector.tensor_copy(
-                    out=own.bitcast(U16).rearrange("p (d j) -> p d j", d=2),
-                    in_=both[which].bitcast(U16).rearrange("p (j d) -> p d j", d=2),
-                )
-                result.append(own)
-            return result
-
-        def quantise_weights(k):
-            if k < 2:
-                rounded = sbuf.tile([P, PACK * R], BF16, name="rounded%d" % k, align_bytes=64)
-            else:
-                rounded = laid.tile([P, PACK * R], BF16, name="rounded%d" % k, align_bytes=64, offset=7 * T * (k - 2))
-            nc.scalar.copy(
-                out=rounded[:].rearrange("p (t m u e) -> p m u t e", t=PACK, u=2, e=2),
-                in_=raw[k][:].rearrange("p (u e) (m t) -> p m u t e", t=PACK, e=2),
-            )
-            codes = sbuf.tile([P, R], U32, name="w_codes%d" % k, align_bytes=64)
-            plane = sbuf.tile([P, R], U8, name="w_plane%d" % k, align_bytes=64)
-            nc.vector.quantize_mx(out=codes[:].bitcast(FP8X4), scales=plane[:], in_=rounded[:])
-            return codes, plane
-
-        gathered = sbuf.tile([P, 2 * J], U8, name="gathered_plane", align_bytes=64)
+        gathered = tile(2 * J, U8, "gathered")
         for which in (SOURCE, TARGET):
             nc.vector.tensor_copy(
                 out=gathered[:, J * which : J * (which + 1)], in_=table_scales[:].indirect(lists[which][:])
@@ -140,27 +104,49 @@ def tile_list_msg_gelu_resL_kernel(
                     in_=gathered[first : first + 4, :].bitcast(I32),
                 )
 
-        spread_scales(0)
-        raw.append(load_weights(3))
-        spread_scales(1)
-        v_planes = (planes[:, : 2 * J], planes[:, 2 * J :])
-
-        weights = [quantise_weights(0)]
-
         def load_states(n, name):
-            if n:
-                state = sbuf.tile([P, T], F32, name=name, align_bytes=64)
-            else:
-                state = laid.tile([P, T], F32, name=name, align_bytes=64, offset=0)
+            state = tile(T, F32, name)
             nc.sync.dma_start(out=state[:], in_=rT[P * n : P * (n + 1), :])
             return state
 
-        states = {1: load_states(1, "rounded0")}
-        both = gather_words(0, "both0")
-        v_words = [part_words(both, "parted")]
-        states[3] = load_states(3, "both0")
+        spread_scales(0)
+        states = {1: load_states(1, "table_scales")}
+        spread_scales(1)
+
+        def quantise_weights(k):
+            if k < 3:
+                rounded = tile(PACK * R, BF16, "rounded%d" % k)
+            else:
+                rounded = laid.tile([P, PACK * R], BF16, name="rounded3", align_bytes=64, offset=PAGE - PACK * R)
+            nc.scalar.copy(
+                out=rounded[:].rearrange("p (t m u e) -> p m u t e", t=PACK, u=2, e=2),
+                in_=raw[k][:].rearrange("p (u e) (m t) -> p m u t e", t=PACK, e=2),
+            )
+            codes = tile(R, U32, "w_codes%d" % k)
+            plane = tile(R, U8, "w_plane%d" % k)
+            nc.vector.quantize_mx(out=codes[:].bitcast(FP8X4), scales=plane[:], in_=rounded[:])
+            return codes, plane
+
+        def part_words(both, name):
+            parted = tile(4 * J, U8, name)
+            nc.vector.tensor_copy(
+                out=parted[:].bitcast(U16).rearrange("p (d j) -> p d j", d=2),
+                in_=both[:].bitcast(U16).rearrange("p (j d) -> p d j", d=2),
+            )
+            return parted
+
+        weights = [quantise_weights(0)]
+        sm_cols = tile(PACK, F32, "raw0")
+        nc.sync.dma_start(out=sm_cols[:], in_=sm.rearrange("(p i) -> p i", i=PACK))
+        both = [tile(J, U32, "both%d" % which) for which in (SOURCE, TARGET)]
+        for which in (SOURCE, TARGET):
+            nc.vector.tensor_copy(out=both[which][:], in_=table[:].bitcast(U32).indirect(lists[which][:]))
+        states[3] = load_states(3, "table")
+        v_words = [part_words(both[SOURCE], "parted")]
+        states[2] = load_states(2, "both0")
         weights.append(quantise_weights(1))
-        wd_bytes = sbuf.tile([P, 3 * N], U8, name="rounded1", align_bytes=64)
+        v_words.append(part_words(both[TARGET], "raw1"))
+        wd_bytes = tile(3 * N, U8, "rounded1")
         wd_codes, wd_plane = wd_bytes[:, : 2 * N], wd_bytes[:, 2 * N :]
         for q in range(4):
             rows = wd_scales[0, 4 * q : 4 * q + 4, :].bitcast(I32)
@@ -169,103 +155,85 @@ def tile_list_msg_gelu_resL_kernel(
                 in_=rows.unsqueeze(0).to_broadcast([8, 4, N // 4]),
             )
         nc.sync.dma_start(out=wd_codes.bitcast(I32), in_=wd_words[0].bitcast(I32))
-        both = gather_words(1, "raw1")
-        weights.append(quantise_weights(2))
-        v_words.append(part_words(both, "raw2"))
-        weights.append(quantise_weights(3))
-        states[2] = load_states(2, "table")
-        states[0] = load_states(0, "last_states")
+        weights.extend(quantise_weights(k) for k in (2, 3))
+        states[0] = load_states(0, "rounded2")
 
-        def first_pass(k, t, j0, j1, sums, start, stop):
+        pages = {}
+
+        def clear_page(n):
+            pages[n] = laid.tile([P, T], F32, name="page%d" % n, align_bytes=64, offset=PAGE * n)
+            nc.gpsimd.memset(pages[n][:], 0.0)
+
+        def first_pass(k, g, t, bank, start, stop):
             which, d = PASSES[k]
             codes, plane = weights[k]
-            c0 = 2 * HALF * d + 2 * (j0 % HALF)
+            j0 = QUARTER * g
             nc.tensor.matmul_mx(
-                out=sums,
+                out=bank[:, QUARTER * (t % 2) : QUARTER * (t % 2 + 1)],
                 lhsT=codes[:, P * t : P * (t + 1)].bitcast(FP8X4),
                 lhsT_scale=plane[:, P * t : P * (t + 1)],
-                rhs=v_words[j0 // HALF][which][:, c0 : c0 + 2 * (j1 - j0)].bitcast(FP4X4),
-                rhs_scale=v_planes[d][:, J * which + j0 : J * which + j1],
+                rhs=v_words[which][:, 2 * (J * d + j0) : 2 * (J * d + j0 + QUARTER)].bitcast(FP4X4),
+                rhs_scale=planes[:, 2 * J * d + J * which + j0 : 2 * J * d + J * which + j0 + QUARTER],
                 start=start,
                 stop=stop,
             )
 
-        def early_sums():
-            banks = [bank_tile(index) for index in range(4)]
-            sums = {}
+        last = len(PASSES) - 1
+
+        def early_sums(g, indices):
+            banks = [bank_tile(index) for index in indices]
             for k in range(len(PASSES)):
-                for g in range(2):
-                    for t in range(PACK):
-                        sums[g, t] = banks[2 * g + t // 2][:, QUARTER * (t % 2) : QUARTER * (t % 2 + 1)]
-                        start = k == 0 and t % 2 == 0
-                        stop = k == len(PASSES) - 1 and t % 2 == 1
-                        first_pass(k, t, QUARTER * g, QUARTER * (g + 1), sums[g, t], start, stop)
-            return sums
+                for t in range(PACK):
+                    first_pass(k, g, t, banks[t // 2], k == 0 and t % 2 == 0, k == last and t % 2 == 1)
+            return banks
 
-        def late_sums(placed):
-            sums = {}
-            for t, index in placed:
-                bank = bank_tile(index)
+        def late_sums(g, indices):
+            banks = [bank_tile(index) for index in indices]
+            for pair in range(2):
                 for k in reversed(range(len(PASSES))):
-                    first_pass(k, t, HALF, J, bank[:], k == len(PASSES) - 1, k == 0)
-                for g in (2, 3):
-                    sums[g, t] = bank[:, QUARTER * (g - 2) : QUARTER * (g - 1)]
-            return sums
+                    for t in (2 * pair, 2 * pair + 1):
+                        first_pass(k, g, t, banks[pair], k == last and t % 2 == 0, k == 0 and t % 2 == 1)
+            return banks
 
-        def act_tile(name):
-            return sbuf.tile([P, PACK * QUARTER], F32, name=name, align_bytes=64)
-
-        def smooth_quarter(g, banks, name):
-            acts = act_tile(name)
-            acts = [gelu(acts, banks, g, t) for t in range(PACK)]
-            scaled = scaled_tile(g)
+        def smoothed(g, banks, name):
+            acts = tile(PACK * QUARTER, F32, name)
+            for pair in range(2):
+                nc.scalar.activation(
+                    out=acts[:, BANK * pair : BANK * (pair + 1)], in_=banks[pair][:], func=ACT.Gelu_apprx_tanh
+                )
+            scaled = tile(PACK * QUARTER, BF16, "scaled%d" % g)
             for t in range(PACK):
-                smooth(scaled, t, acts[t])
+                cols = slice(QUARTER * t, QUARTER * (t + 1))
+                nc.scalar.activation(out=scaled[:, cols], in_=acts[:, cols], func=ACT.Copy, scale=sm_cols[:, t : t + 1])
             return scaled
 
-        def gelu(acts, banks, g, t):
-            act = acts[:, QUARTER * t : QUARTER * (t + 1)]
-            nc.scalar.activation(out=act, in_=banks[g, t], func=ACT.Gelu_apprx_tanh)
-            return act
-
-        def smooth(scaled, t, act):
-            nc.scalar.activation(
-                out=scaled[:, QUARTER * t : QUARTER * (t + 1)], in_=act, func=ACT.Copy, scale=sm_cols[:, t : t + 1]
-            )
-
-        def scaled_tile(g):
-            name = ("scaled0", "message0", "h_plane1", "h_plane2")[g]
-            return sbuf.tile([P, PACK * QUARTER], BF16, name=name, align_bytes=64)
-
-        def weave_and_quantise(g, scaled, codes):
-            woven = sbuf.tile([P, PACK * QUARTER], BF16, name="woven%d" % g, align_bytes=64)
+        def weave(scaled, woven):
             nc.scalar.copy(
                 out=woven[:].rearrange("p (c e t) -> p c t e", e=4, t=PACK),
                 in_=scaled[:].rearrange("p (t c e) -> p c t e", t=PACK, e=4),
             )
-            plane = sbuf.tile([P, QUARTER], U8, name="h_plane%d" % g, align_bytes=64)
-            nc.vector.quantize_mx(out=codes.bitcast(FP8X4), scales=plane[:], in_=woven[:])
+            return woven
+
+        def quantise_hidden(g, woven, name):
+            codes = tile(QUARTER, U32, name)
+            plane = tile(QUARTER, U8, "h_plane%d" % g)
+            nc.vector.quantize_mx(out=codes[:].bitcast(FP8X4), scales=plane[:], in_=woven[:])
             return codes, plane
 
-        def codes_tile(g):
-            return sbuf.tile([P, QUARTER], U32, name="h_codes%d" % g, align_bytes=64)[:]
+        weighted = {}
 
-        def gather_states(n, j0, j1):
+        def gather_states(n, j0, j1, into, factors=edge_w):
             nc.vector.tensor_tensor(
-                weighted(n, j0, j1),
-                states[n][:].indirect(lists[TARGET][:, j0 // 16 : j1 // 16]),
-                edge_w[:, j0:j1],
-                ALU.mult,
+                into, states[n][:].indirect(lists[TARGET][:, j0 // 16 : j1 // 16]), factors[:, j0:j1], ALU.mult
             )
+            for g in range(j0 // QUARTER, j1 // QUARTER):
+                weighted[n, g] = (into, j0)
 
-        messages = {}
-
-        def turned_messages(g, hq, banks):
-            products = []
+        def products(hq, indices):
+            banks = [bank_tile(index) for index in indices]
             for b in range(2):
-                bank = bank_tile(banks[b])
                 nc.tensor.matmul_mx(
-                    out=bank[:],
+                    out=banks[b][:],
                     lhsT=hq[0][:, P * b : P * (b + 1)].bitcast(FP8X4),
                     lhsT_scale=hq[1][:, P * b : P * (b + 1)],
                     rhs=wd_codes.bitcast(FP4X4),
@@ -273,116 +241,117 @@ def tile_list_msg_gelu_resL_kernel(
                     start=True,
                     stop=True,
                 )
-                products.append(bank)
-                messages[2 * g + b] = sbuf.tile([P, N], F32, name="message%d" % (2 * g + b), align_bytes=64)
-            for cols in (slice(0, P), slice(P, N)):
-                for b in range(2):
-                    block = 2 * g + b
-                    nc.scalar.activation(
-                        out=messages[block][:, cols],
-                        in_=products[b][:, cols],
-                        func=ACT.Copy,
-                        scale=w_cols[:, block : block + 1],
-                    )
+            return banks
 
-        def pair_messages(g, hq, i, bank_index):
-            bank = bank_tile(bank_index)
-            cols = slice(QUARTER * i, QUARTER * (i + 1))
-            for b in range(2):
-                nc.tensor.matmul_mx(
-                    out=bank[:, QUARTER * b : QUARTER * (b + 1)],
-                    lhsT=hq[0][:, P * b : P * (b + 1)].bitcast(FP8X4),
-                    lhsT_scale=hq[1][:, P * b : P * (b + 1)],
-                    rhs=wd_codes[:, 2 * cols.start : 2 * cols.stop].bitcast(FP4X4),
-                    rhs_scale=wd_plane[:, cols],
-                    start=True,
-                    stop=True,
-                )
-                if i == 0:
-                    messages[2 * g + b] = sbuf.tile([P, N], F32, name="message%d" % (2 * g + b), align_bytes=64)
+        messages = {}
+
+        def weigh(g, banks, n0, n1):
+            width = P * (n1 - n0)
+            if (g, n0) == (0, 0):
+                message = laid.tile([P, 2 * width], F32, name="message0_0", align_bytes=64, offset=3 * PAGE)
+            else:
+                message = tile(2 * width, F32, "message%d_%d" % (g, n0))
             for b in range(2):
                 block = 2 * g + b
                 nc.scalar.activation(
-                    out=messages[block][:, cols],
-                    in_=bank[:, QUARTER * b : QUARTER * (b + 1)],
+                    out=message[:, width * b : width * (b + 1)],
+                    in_=banks[b][:, P * n0 : P * n1],
                     func=ACT.Copy,
                     scale=w_cols[:, block : block + 1],
                 )
+                for n in range(n0, n1):
+                    c0 = width * b + P * (n - n0)
+                    messages[n, block] = message[:, c0 : c0 + P]
 
-        def put(n, blocks, bank_index, upright):
-            width = P * len(blocks)
-            bank = bank_tile(bank_index)
-            for i, block in enumerate(blocks):
-                nc.tensor.transpose(bank[:, P * i : P * (i + 1)], messages[block][:, P * n : P * (n + 1)], ident[:])
-            nc.scalar.copy(out=upright, in_=bank[:, :width])
-            j0 = P * blocks[0]
+        def turn_back(pieces, index):
+            bank = bank_tile(index)
+            for i, (n, g) in enumerate(pieces):
+                for b in range(2):
+                    c0 = QUARTER * i + P * b
+                    nc.tensor.transpose(bank[:, c0 : c0 + P], messages[n, 2 * g + b], ident[:])
+            return bank
+
+        def upright(pieces, bank, name):
+            width = QUARTER * len(pieces)
+            sums = tile(width, F32, name)
+            nc.scalar.copy(out=sums[:], in_=bank[:, :width])
+            return sums
+
+        def scatter(n, g0, g1, values):
+            held, base = weighted[n, g0]
+            j0, j1 = QUARTER * g0, QUARTER * g1
             nc.vector.tensor_tensor(
-                pages[n][:].indirect(lists[TARGET][:, j0 // 16 : (j0 + width) // 16]),
-                upright,
-                weighted(n, j0, j0 + width),
+                pages[n][:].indirect(lists[TARGET][:, j0 // 16 : j1 // 16]),
+                values,
+                held[:, j0 - base : j1 - base],
                 ALU.add,
             )
 
-        def upright_tile(width, name):
-            return sbuf.tile([P, width], F32, name=name, align_bytes=64)
+        def put(pieces, index):
+            n, g = pieces[0]
+            place(pieces, upright(pieces, turn_back(pieces, index), "upright%d_%d" % (n, g)))
 
-        def store(n):
-            if n < TILES - 1:
-                nc.sync.dma_start(out=out[P * n : P * (n + 1), :], in_=pages[n][:])
+        def place(pieces, sums):
+            if len(set(n for n, g in pieces)) == 1:
+                scatter(pieces[0][0], pieces[0][1], pieces[-1][1] + 1, sums[:])
             else:
-                for queue, cols in ((nc.sync, slice(0, T // 2)), (nc.scalar, slice(T // 2, T))):
-                    queue.dma_start(out=out[P * n : P * (n + 1), cols], in_=pages[n][:, cols])
-
-        weighted_states = {}
-
-        def weighted(n, j0, j1):
-            return weighted_states[n][:, j0:j1]
+                for i, (n, g) in enumerate(pieces):
+                    scatter(n, g, g + 1, sums[:, QUARTER * i : QUARTER * (i + 1)])
 
         for n in (1, 3):
-            weighted_states[n] = sbuf.tile([P, J], F32, name="weighted%d" % n, align_bytes=64)[:]
-            gather_states(n, 0, J)
-        sums = early_sums()
-        scaled = smooth_quarter(0, sums, "act0")
-        hq = weave_and_quantise(0, scaled, codes_tile(0))
-        held = sbuf.tile([P, 2 * J], F32, name="scaled0", align_bytes=64)
-        weighted_states[2], weighted_states[0] = held[:, :J], held[:, J:]
-        gather_states(2, 0, J)
-        gather_states(0, 0, HALF)
-        gather_states(0, HALF, J)
-        for n in range(2):
-            pages[n] = laid.tile([P, T], F32, name="page%d" % n, align_bytes=64, offset=4 * T * (n + 1))
-            nc.gpsimd.memset(pages[n][:], 0.0)
-        late_page(2, "woven0")
-        late_page(3, "table")
-        after_codes = laid.tile([P, QUARTER], U32, name="after_codes", align_bytes=64, offset=0)
-        after = laid.tile([P, T - QUARTER], F32, name="after", align_bytes=64, offset=4 * QUARTER)
-        for g in range(4):
-            blocks = (2 * g, 2 * g + 1)
-            if g < 3:
-                acts = after[:, J - QUARTER :] if g == 1 else act_tile("act0")
-                acts = [gelu(acts, sums, g + 1, t) for t in range(PACK)]
-            if g < 3:
-                turned_messages(g, hq, (0, 1))
-            else:
-                pair_messages(g, hq, 0, 0)
-            if g == 0:
-                sums.update(late_sums([(0, 4), (1, 5), (2, 6)]))
-            put(0, blocks, 7 if g else 2, upright_tile(QUARTER, "upright%d" % g)[:])
-            if g == 0:
-                sums.update(late_sums([(3, 2)]))
-            if g < 3:
-                scaled = scaled_tile(g + 1)
-                for t in range(PACK):
-                    smooth(scaled, t, acts[t])
-                hq = weave_and_quantise(g + 1, scaled, codes_tile(g + 1) if g else after_codes[:])
-            if g < 3:
-                others = (1, 2, 3) if g < 2 else (1, 2)
-                upright = upright_tile(QUARTER * len(others), "h_plane%d" % g) if g else after[:, : J - QUARTER]
-                for n in others:
-                    put(n, blocks, (3, 0, 1)[n - 1], upright[:, QUARTER * (n - 1) : QUARTER * n])
-        put(1, (6, 7), 3, upright_tile(QUARTER, "upright_last1")[:])
-        pair_messages(3, hq, 1, 7)
-        put(2, (6, 7), 2, upright_tile(QUARTER, "upright_last2")[:])
-        put(3, (4, 5, 6, 7), 1, upright_tile(HALF, "upright_last")[:])
-        for n in range(TILES):
-            store(n)
+            gather_states(n, 0, J, tile(J, F32, "weighted%d" % n)[:])
+        sums = [early_sums(0, (0, 1)), late_sums(1, (2, 3)), late_sums(2, (4, 5))]
+        scaled = smoothed(0, sums[0], "act0")
+        woven = laid.tile([P, PACK * QUARTER], BF16, name="woven0", align_bytes=64, offset=2 * PAGE)
+        weave(scaled, woven)
+        front = tile(HALF, F32, "weighted2")
+        gather_states(2, 0, QUARTER, front[:, :QUARTER], lead_w)
+        gather_states(2, QUARTER, HALF, front[:, QUARTER:])
+        hq = quantise_hidden(0, woven, "lead_w")
+        held = tile(HALF + J, F32, "scaled0")
+        gather_states(2, HALF, J, held[:, :HALF])
+        gather_states(0, 0, HALF, held[:, HALF:J])
+        gather_states(0, HALF, J, held[:, J:])
+        for n in range(TILES - 1):
+            clear_page(n)
+
+        scaled = smoothed(1, sums[1], "act0")
+        banks = products(hq, (0, 1))
+        weigh(0, banks, 0, 1)
+        weigh(0, banks, 1, TILES)
+        put([(0, 0)], 6)
+        woven = laid.tile([P, PACK * QUARTER], BF16, name="woven1", align_bytes=64, offset=3 * PAGE)
+        hq = quantise_hidden(1, weave(scaled, woven), "rounded2")
+        clear_page(3)
+        put([(1, 0)], 7)
+        put([(2, 0), (3, 0)], 6)
+        sums.append(late_sums(3, (0, 1)))
+
+        scaled = smoothed(2, sums[2], "message0_1")
+        banks = products(hq, (2, 3))
+        weigh(1, banks, 0, 1)
+        hq = quantise_hidden(2, weave(scaled, tile(PACK * QUARTER, BF16, "woven2")), "h_codes2")
+        put([(0, 1)], 7)
+        weigh(1, banks, 1, TILES)
+        put([(1, 1), (2, 1)], 6)
+        waiting = turn_back([(3, 1)], 4)
+
+        scaled = smoothed(3, sums[3], "scaled2")
+        banks = products(hq, (3, 6))
+        weigh(2, banks, 0, 2)
+        hq = quantise_hidden(3, weave(scaled, tile(PACK * QUARTER, BF16, "message1_1")), "h_codes3")
+        place([(3, 1)], upright([(3, 1)], waiting, "scaled3"))
+        put([(0, 2), (1, 2)], 5)
+        weigh(2, banks, 2, TILES)
+
+        banks = products(hq, (2, 0))
+        weigh(3, banks, 0, 2)
+        put([(0, 3), (1, 3)], 7)
+        weigh(3, banks, 2, TILES)
+        put([(2, 2), (2, 3)], 1)
+        put([(3, 2), (3, 3)], 4)
+
+        for n in range(TILES - 1):
+            nc.sync.dma_start(out=out[P * n : P * (n + 1), :], in_=pages[n][:])
+        for queue, cols in ((nc.sync, slice(0, T // 2)), (nc.scalar, slice(T // 2, T))):
+            queue.dma_start(out=out[P * (TILES - 1) :, cols], in_=pages[TILES - 1][:, cols])

@@ -28,6 +28,7 @@ COMPACT = P - 32
 SOURCE, TARGET = 0, 1
 PASSES = ((SOURCE, 0), (TARGET, 0), (SOURCE, 1), (TARGET, 1))
 PAGE = 4 * T
+SHARE = P // 4
 
 
 def tile_list_msg_gelu_resL_kernel(
@@ -113,15 +114,22 @@ def tile_list_msg_gelu_resL_kernel(
         states = {1: load_states(1, "table_scales")}
         spread_scales(1)
 
-        def quantise_weights(k):
+        def rounded_tile(k):
             if k < 3:
                 rounded = tile(PACK * R, BF16, "rounded%d" % k)
             else:
                 rounded = laid.tile([P, PACK * R], BF16, name="rounded3", align_bytes=64, offset=PAGE - PACK * R)
-            nc.scalar.copy(
-                out=rounded[:].rearrange("p (t m u e) -> p m u t e", t=PACK, u=2, e=2),
-                in_=raw[k][:].rearrange("p (u e) (m t) -> p m u t e", t=PACK, e=2),
+            return rounded
+
+        def round_weights(copy, k, rounded, m0, m1):
+            copy(
+                out=rounded[:].rearrange("p (t m u e) -> p m u t e", t=PACK, u=2, e=2)[:, m0:m1],
+                in_=raw[k][:].rearrange("p (u e) (m t) -> p m u t e", t=PACK, e=2)[:, m0:m1],
             )
+
+        def quantise_weights(k, rounded=None, m0=0):
+            rounded = rounded_tile(k) if rounded is None else rounded
+            round_weights(nc.scalar.copy, k, rounded, m0, P)
             codes = tile(R, U32, "w_codes%d" % k)
             plane = tile(R, U8, "w_plane%d" % k)
             nc.vector.quantize_mx(out=codes[:].bitcast(FP8X4), scales=plane[:], in_=rounded[:])
@@ -144,6 +152,8 @@ def tile_list_msg_gelu_resL_kernel(
         states[3] = load_states(3, "table")
         v_words = [part_words(both[SOURCE], "parted")]
         states[2] = load_states(2, "both0")
+        shared = rounded_tile(2)
+        round_weights(nc.vector.tensor_copy, 2, shared, 0, SHARE)
         weights.append(quantise_weights(1))
         v_words.append(part_words(both[TARGET], "raw1"))
         wd_bytes = tile(3 * N, U8, "rounded1")
@@ -155,7 +165,8 @@ def tile_list_msg_gelu_resL_kernel(
                 in_=rows.unsqueeze(0).to_broadcast([8, 4, N // 4]),
             )
         nc.sync.dma_start(out=wd_codes.bitcast(I32), in_=wd_words[0].bitcast(I32))
-        weights.extend(quantise_weights(k) for k in (2, 3))
+        weights.append(quantise_weights(2, shared, SHARE))
+        weights.append(quantise_weights(3))
         states[0] = load_states(0, "rounded2")
 
         pages = {}

@@ -57,7 +57,8 @@ def tile_list_msg_gelu_resL_kernel(
         nc.sync.dma_start(lists[SOURCE][:], offs)
         nc.sync.dma_start(lists[TARGET][:], offs2)
         w_rows = sbuf.tile([P, P], F32, name="w_rows")
-        nc.sync.dma_start(out=w_rows[:], in_=wgo.rearrange("r (b c) -> (r b) c", c=P)[:P, :])
+        nc.gpsimd.memset(w_rows[:], 0.0)
+        nc.sync.dma_start(out=w_rows[: J // P, :], in_=wgo[0].rearrange("(b c) -> b c", c=P))
 
         def load_weights(k):
             which, d = PASSES[k]
@@ -152,8 +153,6 @@ def tile_list_msg_gelu_resL_kernel(
         states[3] = load_states(3, "table")
         v_words = [part_words(both[SOURCE], "parted")]
         states[2] = load_states(2, "both0")
-        shared = rounded_tile(2)
-        round_weights(nc.vector.tensor_copy, 2, shared, 0, SHARE)
         weights.append(quantise_weights(1))
         v_words.append(part_words(both[TARGET], "raw1"))
         wd_bytes = tile(3 * N, U8, "rounded1")
@@ -165,8 +164,10 @@ def tile_list_msg_gelu_resL_kernel(
                 in_=rows.unsqueeze(0).to_broadcast([8, 4, N // 4]),
             )
         nc.sync.dma_start(out=wd_codes.bitcast(I32), in_=wd_words[0].bitcast(I32))
-        weights.append(quantise_weights(2, shared, SHARE))
-        weights.append(quantise_weights(3))
+        shared = rounded_tile(3)
+        round_weights(nc.vector.tensor_copy, 3, shared, 0, SHARE)
+        weights.append(quantise_weights(2))
+        weights.append(quantise_weights(3, shared, SHARE))
         states[0] = load_states(0, "rounded2")
 
         pages = {}

@@ -194,9 +194,10 @@ def tile_list_msg_gelu_resL_kernel(
 
         def early_sums(g, indices):
             banks = [bank_tile(index) for index in indices]
-            for k in range(len(PASSES)):
-                for t in range(PACK):
-                    first_pass(k, g, t, banks[t // 2], k == 0 and t % 2 == 0, k == last and t % 2 == 1)
+            order = [(k, t) for k in (0, 1) for t in range(PACK)]
+            order.extend((k, t) for pair in range(2) for k in (2, 3) for t in (2 * pair, 2 * pair + 1))
+            for k, t in order:
+                first_pass(k, g, t, banks[t // 2], k == 0 and t % 2 == 0, k == last and t % 2 == 1)
             return banks
 
         def late_sums(g, indices):
@@ -330,8 +331,8 @@ def tile_list_msg_gelu_resL_kernel(
         scaled = smoothed(1, sums[1], "act0")
         banks = products(hq, (0, 1))
         weigh(0, banks, 0, 1)
-        weigh(0, banks, 1, TILES)
         put([(0, 0)], 6)
+        weigh(0, banks, 1, TILES)
         woven = laid.tile([P, PACK * QUARTER], BF16, name="woven1", align_bytes=64, offset=3 * PAGE)
         hq = quantise_hidden(1, weave(scaled, woven), "rounded2")
         clear_page(3)

@@ -364,7 +364,5 @@ def tile_list_msg_gelu_resL_kernel(
         put([(2, 2), (2, 3)], 1)
         put([(3, 2), (3, 3)], 4)
 
-        for n in range(TILES - 1):
+        for n in range(TILES):
             nc.sync.dma_start(out=out[P * n : P * (n + 1), :], in_=pages[n][:])
-        for queue, cols in ((nc.sync, slice(0, T // 2)), (nc.scalar, slice(T // 2, T))):
-            queue.dma_start(out=out[P * (TILES - 1) :, cols], in_=pages[TILES - 1][:, cols])

@@ -28,6 +28,7 @@ COMPACT = P - 32
 SOURCE, TARGET = 0, 1
 PASSES = ((SOURCE, 0), (TARGET, 0), (SOURCE, 1), (TARGET, 1))
 PAGE = 4 * T
+ALIGN = 256
 SHARE = P // 4
 
 
@@ -44,7 +45,7 @@ def tile_list_msg_gelu_resL_kernel(
             return psum.tile([P, BANK], F32, name="bank%d" % index)
 
         def tile(width, dtype, name):
-            return sbuf.tile([P, width], dtype, name=name, align_bytes=64)
+            return sbuf.tile([P, width], dtype, name=name, align_bytes=ALIGN)
 
         lists = [sbuf.tile([P, J // 16], U16, name="list%d" % which) for which in (SOURCE, TARGET)]
         table = tile(T, I32, "table")
@@ -63,7 +64,7 @@ def tile_list_msg_gelu_resL_kernel(
         def load_weights(k):
             which, d = PASSES[k]
             rows = (ws, wt)[which][K_PASS * d : K_PASS * (d + 1), :].rearrange("(p i) c -> p i c", i=PACK)
-            piece = sbuf.tile([P, PACK, R], F32, name="raw%d" % k, align_bytes=64)
+            piece = sbuf.tile([P, PACK, R], F32, name="raw%d" % k, align_bytes=ALIGN)
             nc.sync.dma_start(out=piece[:], in_=rows)
             return piece
 
@@ -119,7 +120,7 @@ def tile_list_msg_gelu_resL_kernel(
             if k < 3:
                 rounded = tile(PACK * R, BF16, "rounded%d" % k)
             else:
-                rounded = laid.tile([P, PACK * R], BF16, name="rounded3", align_bytes=64, offset=PAGE - PACK * R)
+                rounded = laid.tile([P, PACK * R], BF16, name="rounded3", align_bytes=ALIGN, offset=PAGE - PACK * R)
             return rounded
 
         def round_weights(copy, k, rounded, m0, m1):
@@ -173,7 +174,7 @@ def tile_list_msg_gelu_resL_kernel(
         pages = {}
 
         def clear_page(n):
-            pages[n] = laid.tile([P, T], F32, name="page%d" % n, align_bytes=64, offset=PAGE * n)
+            pages[n] = laid.tile([P, T], F32, name="page%d" % n, align_bytes=ALIGN, offset=PAGE * n)
             nc.gpsimd.memset(pages[n][:], 0.0)
 
         def first_pass(k, g, t, bank, start, stop):
@@ -261,7 +262,7 @@ def tile_list_msg_gelu_resL_kernel(
         def weigh(g, banks, n0, n1):
             width = P * (n1 - n0)
             if (g, n0) == (0, 0):
-                message = laid.tile([P, 2 * width], F32, name="message0_0", align_bytes=64, offset=3 * PAGE)
+                message = laid.tile([P, 2 * width], F32, name="message0_0", align_bytes=ALIGN, offset=3 * PAGE)
             else:
                 message = tile(2 * width, F32, "message%d_%d" % (g, n0))
             for b in range(2):
@@ -315,7 +316,7 @@ def tile_list_msg_gelu_resL_kernel(
             gather_states(n, 0, J, tile(J, F32, "weighted%d" % n)[:])
         sums = [early_sums(0, (0, 1)), late_sums(1, (2, 3)), late_sums(2, (4, 5))]
         scaled = smoothed(0, sums[0], "act0")
-        woven = laid.tile([P, PACK * QUARTER], BF16, name="woven0", align_bytes=64, offset=2 * PAGE)
+        woven = laid.tile([P, PACK * QUARTER], BF16, name="woven0", align_bytes=ALIGN, offset=2 * PAGE)
         weave(scaled, woven)
         front = tile(HALF, F32, "weighted2")
         gather_states(2, 0, QUARTER, front[:, :QUARTER], lead_w)
@@ -333,7 +334,7 @@ def tile_list_msg_gelu_resL_kernel(
         weigh(0, banks, 0, 1)
         put([(0, 0)], 6)
         weigh(0, banks, 1, TILES)
-        woven = laid.tile([P, PACK * QUARTER], BF16, name="woven1", align_bytes=64, offset=3 * PAGE)
+        woven = laid.tile([P, PACK * QUARTER], BF16, name="woven1", align_bytes=ALIGN, offset=3 * PAGE)
         hq = quantise_hidden(1, weave(scaled, woven), "rounded2")
         clear_page(3)
         put([(1, 0)], 7)

@@ -29,7 +29,7 @@ SOURCE, TARGET = 0, 1
 PASSES = ((SOURCE, 0), (TARGET, 0), (SOURCE, 1), (TARGET, 1))
 PAGE = 4 * T
 ALIGN = 256
-SHARE = P // 4
+SHARE = 3 * P // 8
 
 
 def tile_list_msg_gelu_resL_kernel(

@@ -29,6 +29,7 @@ SOURCE, TARGET = 0, 1
 PASSES = ((SOURCE, 0), (TARGET, 0), (SOURCE, 1), (TARGET, 1))
 PAGE = 4 * T
 ALIGN = 256
+TABLE_AT = (TILES + 1) * PAGE - ALIGN
 SHARE = 3 * P // 8
 
 
@@ -48,7 +49,7 @@ def tile_list_msg_gelu_resL_kernel(
             return sbuf.tile([P, width], dtype, name=name, align_bytes=ALIGN)
 
         lists = [sbuf.tile([P, J // 16], U16, name="list%d" % which) for which in (SOURCE, TARGET)]
-        table = tile(T, I32, "table")
+        table = laid.tile([P, T], I32, name="table", align_bytes=ALIGN, offset=TABLE_AT)
         table_scales = tile(T, U8, "table_scales")
         nc.sync.dma_start(
             out=table_scales[COMPACT:, :].bitcast(I32),
@@ -108,7 +109,10 @@ def tile_list_msg_gelu_resL_kernel(
                 )
 
         def load_states(n, name):
-            state = tile(T, F32, name)
+            if name == "table":
+                state = laid.tile([P, T], F32, name="states3", align_bytes=ALIGN, offset=TILES * PAGE)
+            else:
+                state = tile(T, F32, name)
             nc.sync.dma_start(out=state[:], in_=rT[P * n : P * (n + 1), :])
             return state
 
@@ -131,8 +135,12 @@ def tile_list_msg_gelu_resL_kernel(
 
         def quantise_weights(k, rounded=None, m0=0):
             rounded = rounded_tile(k) if rounded is None else rounded
-            round_weights(nc.scalar.copy, k, rounded, m0, P)
-            codes = tile(R, U32, "w_codes%d" % k)
+            if m0 < P:
+                round_weights(nc.scalar.copy, k, rounded, m0, P)
+            if k == 0:
+                codes = laid.tile([P, R], U32, name="w_codes0", align_bytes=ALIGN, offset=TABLE_AT + PAGE - ALIGN)
+            else:
+                codes = tile(R, U32, "w_codes%d" % k)
             plane = tile(R, U8, "w_plane%d" % k)
             nc.vector.quantize_mx(out=codes[:].bitcast(FP8X4), scales=plane[:], in_=rounded[:])
             return codes, plane
@@ -145,7 +153,8 @@ def tile_list_msg_gelu_resL_kernel(
             )
             return parted
 
-        weights = [quantise_weights(0)]
+        first_rounded = rounded_tile(0)
+        round_weights(nc.scalar.copy, 0, first_rounded, 0, P)
         sm_cols = tile(PACK, F32, "raw0")
         nc.sync.dma_start(out=sm_cols[:], in_=sm.rearrange("(p i) -> p i", i=PACK))
         both = [tile(J, U32, "both%d" % which) for which in (SOURCE, TARGET)]
@@ -154,6 +163,7 @@ def tile_list_msg_gelu_resL_kernel(
         states[3] = load_states(3, "table")
         v_words = [part_words(both[SOURCE], "parted")]
         states[2] = load_states(2, "both0")
+        weights = [quantise_weights(0, first_rounded, P)]
         weights.append(quantise_weights(1))
         v_words.append(part_words(both[TARGET], "raw1"))
         wd_bytes = tile(3 * N, U8, "rounded1")

@@ -23,13 +23,17 @@ K_PASS = P * PACK
 BANK = 512
 HALF = J // 2
 QUARTER = J // 4
+EARLY = J - QUARTER
 TILES = N // P
 COMPACT = P - 32
 SOURCE, TARGET = 0, 1
 PASSES = ((SOURCE, 0), (TARGET, 0), (SOURCE, 1), (TARGET, 1))
 PAGE = 4 * T
 ALIGN = 256
-TABLE_AT = (TILES + 1) * PAGE - ALIGN
+LATE_AT = PAGE
+STATES_AT = TILES * PAGE + J
+TABLE_AT = STATES_AT + PAGE - ALIGN
+CODES_AT = TABLE_AT + PAGE - ALIGN
 SHARE = 3 * P // 8
 
 
@@ -48,8 +52,11 @@ def tile_list_msg_gelu_resL_kernel(
         def tile(width, dtype, name):
             return sbuf.tile([P, width], dtype, name=name, align_bytes=ALIGN)
 
+        def laid_tile(offset, width, dtype, name):
+            return laid.tile([P, width], dtype, name=name, align_bytes=ALIGN, offset=offset)
+
         lists = [sbuf.tile([P, J // 16], U16, name="list%d" % which) for which in (SOURCE, TARGET)]
-        table = laid.tile([P, T], I32, name="table", align_bytes=ALIGN, offset=TABLE_AT)
+        table = laid_tile(TABLE_AT, T, I32, "table")
         table_scales = tile(T, U8, "table_scales")
         nc.sync.dma_start(
             out=table_scales[COMPACT:, :].bitcast(I32),
@@ -73,10 +80,11 @@ def tile_list_msg_gelu_resL_kernel(
         nc.sync.dma_start(out=table[:], in_=tab_words[0].rearrange("p t b -> p (t b)").bitcast(I32))
         raw.extend(load_weights(k) for k in (1, 2, 3))
 
-        planes = tile(4 * J, U8, "planes")
+        planes = tile(4 * EARLY, U8, "planes")
         nc.vector.memset(planes[:].bitcast(I32), 0)
         ident = sbuf.tile([P, P], F32, name="ident")
         make_identity(nc, ident[:])
+
         bank = bank_tile(4)
         nc.tensor.transpose(bank[:, :P], w_rows[:], ident[:])
         w_cols = sbuf.tile([P, J // P], F32, name="w_cols")
@@ -100,50 +108,44 @@ def tile_list_msg_gelu_resL_kernel(
                 out=gathered[:, J * which : J * (which + 1)], in_=table_scales[:].indirect(lists[which][:])
             )
 
-        def spread_scales(d):
+        plane_of = {}
+
+        def spread_scales(d, j0, j1, plane):
             for q in range(4):
                 first = COMPACT + 16 * d + 4 * q
+                rows = gathered[first : first + 4, :].bitcast(I32).rearrange("p (w c) -> p w c", w=2)
                 nc.sync.dma_start(
-                    out=planes[32 * q : 32 * q + 4, 2 * J * d : 2 * J * (d + 1)].bitcast(I32),
-                    in_=gathered[first : first + 4, :].bitcast(I32),
+                    out=plane[32 * q : 32 * q + 4, :].bitcast(I32).rearrange("p (w c) -> p w c", w=2),
+                    in_=rows[:, :, j0 // 4 : j1 // 4],
                 )
+            for which in (SOURCE, TARGET):
+                for g in range(j0 // QUARTER, j1 // QUARTER):
+                    c0 = (j1 - j0) * which + QUARTER * g - j0
+                    plane_of[which, d, g] = plane[:, c0 : c0 + QUARTER]
 
-        def load_states(n, name):
-            if name == "table":
-                state = laid.tile([P, T], F32, name="states3", align_bytes=ALIGN, offset=TILES * PAGE)
-            else:
-                state = tile(T, F32, name)
+        def load_states(n, state):
             nc.sync.dma_start(out=state[:], in_=rT[P * n : P * (n + 1), :])
             return state
 
-        spread_scales(0)
-        states = {1: load_states(1, "table_scales")}
-        spread_scales(1)
-
-        def rounded_tile(k):
-            if k < 3:
-                rounded = tile(PACK * R, BF16, "rounded%d" % k)
-            else:
-                rounded = laid.tile([P, PACK * R], BF16, name="rounded3", align_bytes=ALIGN, offset=PAGE - PACK * R)
-            return rounded
+        spread_scales(0, 0, EARLY, planes[:, : 2 * EARLY])
+        states = {1: load_states(1, tile(T, F32, "table_scales"))}
+        spread_scales(1, 0, EARLY, planes[:, 2 * EARLY :])
 
         def round_weights(copy, k, rounded, m0, m1):
             copy(
                 out=rounded[:].rearrange("p (t m u e) -> p m u t e", t=PACK, u=2, e=2)[:, m0:m1],
                 in_=raw[k][:].rearrange("p (u e) (m t) -> p m u t e", t=PACK, e=2)[:, m0:m1],
             )
+            return rounded
 
-        def quantise_weights(k, rounded=None, m0=0):
-            rounded = rounded_tile(k) if rounded is None else rounded
-            if m0 < P:
-                round_weights(nc.scalar.copy, k, rounded, m0, P)
-            if k == 0:
-                codes = laid.tile([P, R], U32, name="w_codes0", align_bytes=ALIGN, offset=TABLE_AT + PAGE - ALIGN)
-            else:
-                codes = tile(R, U32, "w_codes%d" % k)
+        def quantise_weights(k, rounded, codes):
             plane = tile(R, U8, "w_plane%d" % k)
             nc.vector.quantize_mx(out=codes[:].bitcast(FP8X4), scales=plane[:], in_=rounded[:])
             return codes, plane
+
+        def round_and_quantise(k, rounded, m0):
+            round_weights(nc.scalar.copy, k, rounded, m0, P)
+            return quantise_weights(k, rounded, tile(R, U32, "w_codes%d" % k))
 
         def part_words(both, name):
             parted = tile(4 * J, U8, name)
@@ -153,18 +155,17 @@ def tile_list_msg_gelu_resL_kernel(
             )
             return parted
 
-        first_rounded = rounded_tile(0)
-        round_weights(nc.scalar.copy, 0, first_rounded, 0, P)
+        first_rounded = round_weights(nc.scalar.copy, 0, tile(PACK * R, BF16, "rounded0"), 0, P)
         sm_cols = tile(PACK, F32, "raw0")
         nc.sync.dma_start(out=sm_cols[:], in_=sm.rearrange("(p i) -> p i", i=PACK))
         both = [tile(J, U32, "both%d" % which) for which in (SOURCE, TARGET)]
         for which in (SOURCE, TARGET):
             nc.vector.tensor_copy(out=both[which][:], in_=table[:].bitcast(U32).indirect(lists[which][:]))
-        states[3] = load_states(3, "table")
+        states[3] = load_states(3, laid_tile(STATES_AT, T, F32, "states3"))
         v_words = [part_words(both[SOURCE], "parted")]
-        states[2] = load_states(2, "both0")
-        weights = [quantise_weights(0, first_rounded, P)]
-        weights.append(quantise_weights(1))
+        states[2] = load_states(2, tile(T, F32, "both0"))
+        weights = [quantise_weights(0, first_rounded, laid_tile(CODES_AT, R, U32, "w_codes0"))]
+        weights.append(round_and_quantise(1, tile(PACK * R, BF16, "rounded1"), 0))
         v_words.append(part_words(both[TARGET], "raw1"))
         wd_bytes = tile(3 * N, U8, "rounded1")
         wd_codes, wd_plane = wd_bytes[:, : 2 * N], wd_bytes[:, 2 * N :]
@@ -175,16 +176,24 @@ def tile_list_msg_gelu_resL_kernel(
                 in_=rows.unsqueeze(0).to_broadcast([8, 4, N // 4]),
             )
         nc.sync.dma_start(out=wd_codes.bitcast(I32), in_=wd_words[0].bitcast(I32))
-        shared = rounded_tile(3)
+        shared = laid_tile(PAGE - PACK * R, PACK * R, BF16, "rounded3")
         round_weights(nc.vector.tensor_copy, 3, shared, 0, SHARE)
-        weights.append(quantise_weights(2))
-        weights.append(quantise_weights(3, shared, SHARE))
-        states[0] = load_states(0, "rounded2")
+        weights.append(round_and_quantise(2, tile(PACK * R, BF16, "rounded2"), 0))
+        weights.append(round_and_quantise(3, shared, SHARE))
+        states[0] = load_states(0, tile(T, F32, "rounded2"))
+
+        late = laid_tile(LATE_AT, J, U8, "late")
+        nc.gpsimd.memset(late[:].bitcast(I32), 0)
+        for d in (1, 0):
+            spread_scales(d, EARLY, J, late[:, HALF * d : HALF * (d + 1)])
 
         pages = {}
 
+        def page_at(n):
+            return PAGE * n + (J if n > 0 else 0)
+
         def clear_page(n):
-            pages[n] = laid.tile([P, T], F32, name="page%d" % n, align_bytes=ALIGN, offset=PAGE * n)
+            pages[n] = laid_tile(page_at(n), T, F32, "page%d" % n)
             nc.gpsimd.memset(pages[n][:], 0.0)
 
         def first_pass(k, g, t, bank, start, stop):
@@ -196,7 +205,7 @@ def tile_list_msg_gelu_resL_kernel(
                 lhsT=codes[:, P * t : P * (t + 1)].bitcast(FP8X4),
                 lhsT_scale=plane[:, P * t : P * (t + 1)],
                 rhs=v_words[which][:, 2 * (J * d + j0) : 2 * (J * d + j0 + QUARTER)].bitcast(FP4X4),
-                rhs_scale=planes[:, 2 * J * d + J * which + j0 : 2 * J * d + J * which + j0 + QUARTER],
+                rhs_scale=plane_of[which, d, g],
                 start=start,
                 stop=stop,
             )
@@ -272,7 +281,7 @@ def tile_list_msg_gelu_resL_kernel(
         def weigh(g, banks, n0, n1):
             width = P * (n1 - n0)
             if (g, n0) == (0, 0):
-                message = laid.tile([P, 2 * width], F32, name="message0_0", align_bytes=ALIGN, offset=3 * PAGE)
+                message = laid_tile(page_at(3), 2 * width, F32, "message0_0")
             else:
                 message = tile(2 * width, F32, "message%d_%d" % (g, n0))
             for b in range(2):
@@ -326,7 +335,7 @@ def tile_list_msg_gelu_resL_kernel(
             gather_states(n, 0, J, tile(J, F32, "weighted%d" % n)[:])
         sums = [early_sums(0, (0, 1)), late_sums(1, (2, 3)), late_sums(2, (4, 5))]
         scaled = smoothed(0, sums[0], "act0")
-        woven = laid.tile([P, PACK * QUARTER], BF16, name="woven0", align_bytes=ALIGN, offset=2 * PAGE)
+        woven = laid_tile(page_at(2), PACK * QUARTER, BF16, "woven0")
         weave(scaled, woven)
         front = tile(HALF, F32, "weighted2")
         gather_states(2, 0, QUARTER, front[:, :QUARTER], lead_w)
@@ -344,7 +353,7 @@ def tile_list_msg_gelu_resL_kernel(
         weigh(0, banks, 0, 1)
         put([(0, 0)], 6)
         weigh(0, banks, 1, TILES)
-        woven = laid.tile([P, PACK * QUARTER], BF16, name="woven1", align_bytes=ALIGN, offset=3 * PAGE)
+        woven = laid_tile(page_at(3), PACK * QUARTER, BF16, "woven1")
         hq = quantise_hidden(1, weave(scaled, woven), "rounded2")
         clear_page(3)
         put([(1, 0)], 7)

@@ -34,7 +34,7 @@ LATE_AT = PAGE
 STATES_AT = TILES * PAGE + J
 TABLE_AT = STATES_AT + PAGE - ALIGN
 CODES_AT = TABLE_AT + PAGE - ALIGN
-SHARE = 3 * P // 8
+SHARE = P // 4
 
 
 def tile_list_msg_gelu_resL_kernel(

@@ -105,7 +105,8 @@ def tile_list_msg_gelu_resL_kernel(
         gathered = tile(2 * J, U8, "gathered")
         for which in (SOURCE, TARGET):
             nc.vector.tensor_copy(
-                out=gathered[:, J * which : J * (which + 1)], in_=table_scales[:].indirect(lists[which][:])
+                out=gathered[:].rearrange("p (g w c) -> p g w c", w=2, c=QUARTER)[:, :, which, :],
+                in_=table_scales[:].indirect(lists[which][:]),
             )
 
         plane_of = {}
@@ -113,14 +114,13 @@ def tile_list_msg_gelu_resL_kernel(
         def spread_scales(d, j0, j1, plane):
             for q in range(4):
                 first = COMPACT + 16 * d + 4 * q
-                rows = gathered[first : first + 4, :].bitcast(I32).rearrange("p (w c) -> p w c", w=2)
                 nc.sync.dma_start(
-                    out=plane[32 * q : 32 * q + 4, :].bitcast(I32).rearrange("p (w c) -> p w c", w=2),
-                    in_=rows[:, :, j0 // 4 : j1 // 4],
+                    out=plane[32 * q : 32 * q + 4, :].bitcast(I32),
+                    in_=gathered[first : first + 4, 2 * j0 : 2 * j1].bitcast(I32),
                 )
             for which in (SOURCE, TARGET):
                 for g in range(j0 // QUARTER, j1 // QUARTER):
-                    c0 = (j1 - j0) * which + QUARTER * g - j0
+                    c0 = 2 * (QUARTER * g - j0) + QUARTER * which
                     plane_of[which, d, g] = plane[:, c0 : c0 + QUARTER]
 
         def load_states(n, state):

from contextlib import ExitStack

import concourse.mybir as mybir
from concourse.masks import make_identity

K, R, N, T, J = 1024, 512, 512, 2048, 1024
FLOPS = 2 * (2 * K * R * J + R * N * J)

F32 = mybir.dt.float32
BF16 = mybir.dt.bfloat16
I32 = mybir.dt.int32
U32 = mybir.dt.uint32
U16 = mybir.dt.uint16
U8 = mybir.dt.uint8
FP8X4 = mybir.dt.float8_e4m3fn_x4
FP4X4 = mybir.dt.float4_e2m1fn_x4
ACT = mybir.ActivationFunctionType
ALU = mybir.AluOpType

P = 128
PACK = 4
K_PASS = P * PACK
BANK = 512
HALF = J // 2
QUARTER = J // 4
EARLY = J - QUARTER
TILES = N // P
COMPACT = P - 32
SOURCE, TARGET = 0, 1
PASSES = ((SOURCE, 0), (TARGET, 0), (SOURCE, 1), (TARGET, 1))
PAGE = 4 * T
ALIGN = 256
LATE_AT = PAGE
STATES_AT = TILES * PAGE + J
TABLE_AT = STATES_AT + PAGE - ALIGN
CODES_AT = TABLE_AT + PAGE - ALIGN
SHARE = P // 4


def tile_list_msg_gelu_resL_kernel(
    tc, tab_words, tab_scales, ws, wt, sm, wd_words, wd_scales, rT, wgo, offs, offs2, out
):
    nc = tc.nc
    with ExitStack() as ctx:
        sbuf = ctx.enter_context(tc.tile_pool(name="sbuf", bufs=1))
        laid = ctx.enter_context(tc.tile_pool(name="laid", bufs=1))
        psum = ctx.enter_context(tc.psum_pool(name="psum", bufs=1))

        def bank_tile(index):
            return psum.tile([P, BANK], F32, name="bank%d" % index)

        def tile(width, dtype, name):
            return sbuf.tile([P, width], dtype, name=name, align_bytes=ALIGN)

        def laid_tile(offset, width, dtype, name):
            return laid.tile([P, width], dtype, name=name, align_bytes=ALIGN, offset=offset)

        lists = [sbuf.tile([P, J // 16], U16, name="list%d" % which) for which in (SOURCE, TARGET)]
        table = laid_tile(TABLE_AT, T, I32, "table")
        table_scales = tile(T, U8, "table_scales")
        nc.sync.dma_start(
            out=table_scales[COMPACT:, :].bitcast(I32),
            in_=tab_scales.rearrange("d q t -> (d q) t").bitcast(I32),
        )
        nc.vector.memset(table_scales[:COMPACT, :].bitcast(I32), 0)
        nc.sync.dma_start(lists[SOURCE][:], offs)
        nc.sync.dma_start(lists[TARGET][:], offs2)
        w_rows = sbuf.tile([P, P], F32, name="w_rows")
        nc.gpsimd.memset(w_rows[:], 0.0)
        nc.sync.dma_start(out=w_rows[: J // P, :], in_=wgo[0].rearrange("(b c) -> b c", c=P))

        def load_weights(k):
            which, d = PASSES[k]
            rows = (ws, wt)[which][K_PASS * d : K_PASS * (d + 1), :].rearrange("(p i) c -> p i c", i=PACK)
            piece = sbuf.tile([P, PACK, R], F32, name="raw%d" % k, align_bytes=ALIGN)
            nc.sync.dma_start(out=piece[:], in_=rows)
            return piece

        raw = [load_weights(0)]
        nc.sync.dma_start(out=table[:], in_=tab_words[0].rearrange("p t b -> p (t b)").bitcast(I32))
        raw.extend(load_weights(k) for k in (1, 2, 3))

        planes = tile(4 * EARLY, U8, "planes")
        nc.vector.memset(planes[:].bitcast(I32), 0)
        ident = sbuf.tile([P, P], F32, name="ident")
        make_identity(nc, ident[:])

        bank = bank_tile(4)
        nc.tensor.transpose(bank[:, :P], w_rows[:], ident[:])
        w_cols = sbuf.tile([P, J // P], F32, name="w_cols")
        nc.scalar.copy(out=w_cols[:], in_=bank[:, : J // P])
        edge_w = tile(J, F32, "edge_w")
        for h in range(2):
            bank = bank_tile(5 + h)
            for b in range(HALF // P):
                block = HALF // P * h + b
                nc.tensor.transpose(
                    bank[:, P * b : P * (b + 1)], w_cols[:, block : block + 1].to_broadcast([P, P]), ident[:]
                )
            nc.scalar.copy(out=edge_w[:, HALF * h : HALF * (h + 1)], in_=bank[:])
            if h == 0:
                lead_w = tile(QUARTER, F32, "lead_w")
                nc.scalar.copy(out=lead_w[:], in_=bank[:, :QUARTER])

        gathered = tile(2 * J, U8, "gathered")
        for which in (SOURCE, TARGET):
            nc.vector.tensor_copy(
                out=gathered[:].rearrange("p (g w c) -> p g w c", w=2, c=QUARTER)[:, :, which, :],
                in_=table_scales[:].indirect(lists[which][:]),
            )

        plane_of = {}

        def spread_scales(d, j0, j1, plane):
            for q in range(4):
                first = COMPACT + 16 * d + 4 * q
                nc.sync.dma_start(
                    out=plane[32 * q : 32 * q + 4, :].bitcast(I32),
                    in_=gathered[first : first + 4, 2 * j0 : 2 * j1].bitcast(I32),
                )
            for which in (SOURCE, TARGET):
                for g in range(j0 // QUARTER, j1 // QUARTER):
                    c0 = 2 * (QUARTER * g - j0) + QUARTER * which
                    plane_of[which, d, g] = plane[:, c0 : c0 + QUARTER]

        def load_states(n, state):
            nc.sync.dma_start(out=state[:], in_=rT[P * n : P * (n + 1), :])
            return state

        spread_scales(0, 0, EARLY, planes[:, : 2 * EARLY])
        states = {1: load_states(1, tile(T, F32, "table_scales"))}
        spread_scales(1, 0, EARLY, planes[:, 2 * EARLY :])

        def round_weights(copy, k, rounded, m0, m1):
            copy(
                out=rounded[:].rearrange("p (t m u e) -> p m u t e", t=PACK, u=2, e=2)[:, m0:m1],
                in_=raw[k][:].rearrange("p (u e) (m t) -> p m u t e", t=PACK, e=2)[:, m0:m1],
            )
            return rounded

        def quantise_weights(k, rounded, codes):
            plane = tile(R, U8, "w_plane%d" % k)
            nc.vector.quantize_mx(out=codes[:].bitcast(FP8X4), scales=plane[:], in_=rounded[:])
            return codes, plane

        def round_and_quantise(k, rounded, m0):
            round_weights(nc.scalar.copy, k, rounded, m0, P)
            return quantise_weights(k, rounded, tile(R, U32, "w_codes%d" % k))

        def part_words(both, name):
            parted = tile(4 * J, U8, name)
            nc.vector.tensor_copy(
                out=parted[:].bitcast(U16).rearrange("p (d j) -> p d j", d=2),
                in_=both[:].bitcast(U16).rearrange("p (j d) -> p d j", d=2),
            )
            return parted

        first_rounded = round_weights(nc.scalar.copy, 0, tile(PACK * R, BF16, "rounded0"), 0, P)
        sm_cols = tile(PACK, F32, "raw0")
        nc.sync.dma_start(out=sm_cols[:], in_=sm.rearrange("(p i) -> p i", i=PACK))
        both = [tile(J, U32, "both%d" % which) for which in (SOURCE, TARGET)]
        for which in (SOURCE, TARGET):
            nc.vector.tensor_copy(out=both[which][:], in_=table[:].bitcast(U32).indirect(lists[which][:]))
        states[3] = load_states(3, laid_tile(STATES_AT, T, F32, "states3"))
        v_words = [part_words(both[SOURCE], "parted")]
        states[2] = load_states(2, tile(T, F32, "both0"))
        weights = [quantise_weights(0, first_rounded, laid_tile(CODES_AT, R, U32, "w_codes0"))]
        weights.append(round_and_quantise(1, tile(PACK * R, BF16, "rounded1"), 0))
        v_words.append(part_words(both[TARGET], "raw1"))
        wd_bytes = tile(3 * N, U8, "rounded1")
        wd_codes, wd_plane = wd_bytes[:, : 2 * N], wd_bytes[:, 2 * N :]
        for q in range(4):
            rows = wd_scales[0, 4 * q : 4 * q + 4, :].bitcast(I32)
            nc.sync.dma_start(
                out=wd_plane[32 * q : 32 * (q + 1), :].bitcast(I32),
                in_=rows.unsqueeze(0).to_broadcast([8, 4, N // 4]),
            )
        nc.sync.dma_start(out=wd_codes.bitcast(I32), in_=wd_words[0].bitcast(I32))
        shared = laid_tile(PAGE - PACK * R, PACK * R, BF16, "rounded3")
        round_weights(nc.vector.tensor_copy, 3, shared, 0, SHARE)
        weights.append(round_and_quantise(2, tile(PACK * R, BF16, "rounded2"), 0))
        weights.append(round_and_quantise(3, shared, SHARE))
        states[0] = load_states(0, tile(T, F32, "rounded2"))

        late = laid_tile(LATE_AT, J, U8, "late")
        nc.gpsimd.memset(late[:].bitcast(I32), 0)
        for d in (1, 0):
            spread_scales(d, EARLY, J, late[:, HALF * d : HALF * (d + 1)])

        pages = {}

        def page_at(n):
            return PAGE * n + (J if n > 0 else 0)

        def clear_page(n):
            pages[n] = laid_tile(page_at(n), T, F32, "page%d" % n)
            nc.gpsimd.memset(pages[n][:], 0.0)

        def first_pass(k, g, t, bank, start, stop):
            which, d = PASSES[k]
            codes, plane = weights[k]
            j0 = QUARTER * g
            nc.tensor.matmul_mx(
                out=bank[:, QUARTER * (t % 2) : QUARTER * (t % 2 + 1)],
                lhsT=codes[:, P * t : P * (t + 1)].bitcast(FP8X4),
                lhsT_scale=plane[:, P * t : P * (t + 1)],
                rhs=v_words[which][:, 2 * (J * d + j0) : 2 * (J * d + j0 + QUARTER)].bitcast(FP4X4),
                rhs_scale=plane_of[which, d, g],
                start=start,
                stop=stop,
            )

        last = len(PASSES) - 1

        def early_sums(g, indices):
            banks = [bank_tile(index) for index in indices]
            order = [(k, t) for k in (0, 1) for t in range(PACK)]
            order.extend((k, t) for pair in range(2) for k in (2, 3) for t in (2 * pair, 2 * pair + 1))
            for k, t in order:
                first_pass(k, g, t, banks[t // 2], k == 0 and t % 2 == 0, k == last and t % 2 == 1)
            return banks

        def late_sums(g, indices):
            banks = [bank_tile(index) for index in indices]
            for pair in range(2):
                for k in reversed(range(len(PASSES))):
                    for t in (2 * pair, 2 * pair + 1):
                        first_pass(k, g, t, banks[pair], k == last and t % 2 == 0, k == 0 and t % 2 == 1)
            return banks

        def smoothed(g, banks, name):
            acts = tile(PACK * QUARTER, F32, name)
            for pair in range(2):
                nc.scalar.activation(
                    out=acts[:, BANK * pair : BANK * (pair + 1)], in_=banks[pair][:], func=ACT.Gelu_apprx_tanh
                )
            scaled = tile(PACK * QUARTER, BF16, "scaled%d" % g)
            for t in range(PACK):
                cols = slice(QUARTER * t, QUARTER * (t + 1))
                nc.scalar.activation(out=scaled[:, cols], in_=acts[:, cols], func=ACT.Copy, scale=sm_cols[:, t : t + 1])
            return scaled

        def weave(scaled, woven):
            nc.scalar.copy(
                out=woven[:].rearrange("p (c e t) -> p c t e", e=4, t=PACK),
                in_=scaled[:].rearrange("p (t c e) -> p c t e", t=PACK, e=4),
            )
            return woven

        def quantise_hidden(g, woven, name):
            codes = tile(QUARTER, U32, name)
            plane = tile(QUARTER, U8, "h_plane%d" % g)
            nc.vector.quantize_mx(out=codes[:].bitcast(FP8X4), scales=plane[:], in_=woven[:])
            return codes, plane

        weighted = {}

        def gather_states(n, j0, j1, into, factors=edge_w):
            nc.vector.tensor_tensor(
                into, states[n][:].indirect(lists[TARGET][:, j0 // 16 : j1 // 16]), factors[:, j0:j1], ALU.mult
            )
            for g in range(j0 // QUARTER, j1 // QUARTER):
                weighted[n, g] = (into, j0)

        def products(hq, indices):
            banks = [bank_tile(index) for index in indices]
            for b in range(2):
                nc.tensor.matmul_mx(
                    out=banks[b][:],
                    lhsT=hq[0][:, P * b : P * (b + 1)].bitcast(FP8X4),
                    lhsT_scale=hq[1][:, P * b : P * (b + 1)],
                    rhs=wd_codes.bitcast(FP4X4),
                    rhs_scale=wd_plane,
                    start=True,
                    stop=True,
                )
            return banks

        messages = {}

        def weigh(g, banks, n0, n1):
            width = P * (n1 - n0)
            if (g, n0) == (0, 0):
                message = laid_tile(page_at(3), 2 * width, F32, "message0_0")
            else:
                message = tile(2 * width, F32, "message%d_%d" % (g, n0))
            for b in range(2):
                block = 2 * g + b
                nc.scalar.activation(
                    out=message[:, width * b : width * (b + 1)],
                    in_=banks[b][:, P * n0 : P * n1],
                    func=ACT.Copy,
                    scale=w_cols[:, block : block + 1],
                )
                for n in range(n0, n1):
                    c0 = width * b + P * (n - n0)
                    messages[n, block] = message[:, c0 : c0 + P]

        def turn_back(pieces, index):
            bank = bank_tile(index)
            for i, (n, g) in enumerate(pieces):
                for b in range(2):
                    c0 = QUARTER * i + P * b
                    nc.tensor.transpose(bank[:, c0 : c0 + P], messages[n, 2 * g + b], ident[:])
            return bank

        def upright(pieces, bank, name):
            width = QUARTER * len(pieces)
            sums = tile(width, F32, name)
            nc.scalar.copy(out=sums[:], in_=bank[:, :width])
            return sums

        def scatter(n, g0, g1, values):
            held, base = weighted[n, g0]
            j0, j1 = QUARTER * g0, QUARTER * g1
            nc.vector.tensor_tensor(
                pages[n][:].indirect(lists[TARGET][:, j0 // 16 : j1 // 16]),
                values,
                held[:, j0 - base : j1 - base],
                ALU.add,
            )

        def put(pieces, index):
            n, g = pieces[0]
            place(pieces, upright(pieces, turn_back(pieces, index), "upright%d_%d" % (n, g)))

        def place(pieces, sums):
            if len(set(n for n, g in pieces)) == 1:
                scatter(pieces[0][0], pieces[0][1], pieces[-1][1] + 1, sums[:])
            else:
                for i, (n, g) in enumerate(pieces):
                    scatter(n, g, g + 1, sums[:, QUARTER * i : QUARTER * (i + 1)])

        for n in (1, 3):
            gather_states(n, 0, J, tile(J, F32, "weighted%d" % n)[:])
        sums = [early_sums(0, (0, 1)), late_sums(1, (2, 3)), late_sums(2, (4, 5))]
        scaled = smoothed(0, sums[0], "act0")
        woven = laid_tile(page_at(2), PACK * QUARTER, BF16, "woven0")
        weave(scaled, woven)
        front = tile(HALF, F32, "weighted2")
        gather_states(2, 0, QUARTER, front[:, :QUARTER], lead_w)
        gather_states(2, QUARTER, HALF, front[:, QUARTER:])
        hq = quantise_hidden(0, woven, "lead_w")
        held = tile(HALF + J, F32, "scaled0")
        gather_states(2, HALF, J, held[:, :HALF])
        gather_states(0, 0, HALF, held[:, HALF:J])
        gather_states(0, HALF, J, held[:, J:])
        for n in range(TILES - 1):
            clear_page(n)

        scaled = smoothed(1, sums[1], "act0")
        banks = products(hq, (0, 1))
        weigh(0, banks, 0, 1)
        put([(0, 0)], 6)
        weigh(0, banks, 1, TILES)
        woven = laid_tile(page_at(3), PACK * QUARTER, BF16, "woven1")
        hq = quantise_hidden(1, weave(scaled, woven), "rounded2")
        clear_page(3)
        put([(1, 0)], 7)
        put([(2, 0), (3, 0)], 6)
        sums.append(late_sums(3, (0, 1)))

        scaled = smoothed(2, sums[2], "message0_1")
        banks = products(hq, (2, 3))
        weigh(1, banks, 0, 1)
        hq = quantise_hidden(2, weave(scaled, tile(PACK * QUARTER, BF16, "woven2")), "h_codes2")
        put([(0, 1)], 7)
        weigh(1, banks, 1, TILES)
        put([(1, 1), (2, 1)], 6)
        waiting = turn_back([(3, 1)], 4)

        scaled = smoothed(3, sums[3], "scaled2")
        banks = products(hq, (3, 6))
        weigh(2, banks, 0, 2)
        hq = quantise_hidden(3, weave(scaled, tile(PACK * QUARTER, BF16, "message1_1")), "h_codes3")
        place([(3, 1)], upright([(3, 1)], waiting, "scaled3"))
        put([(0, 2), (1, 2)], 5)
        weigh(2, banks, 2, TILES)

        banks = products(hq, (2, 0))
        weigh(3, banks, 0, 2)
        put([(0, 3), (1, 3)], 7)
        weigh(3, banks, 2, TILES)
        put([(2, 2), (2, 3)], 1)
        put([(3, 2), (3, 3)], 4)

        for n in range(TILES):
            nc.sync.dma_start(out=out[P * n : P * (n + 1), :], in_=pages[n][:])
